import numpy as np, ml_dtypes
CORES = [1,5,17,21,33,37,49,53]
N = 8
BF = ml_dtypes.bfloat16
L, S, NR, NC, RO, ST = 192, 16, 3072, 2048, 3, 3
def kill(rng, R, share):
    return np.where(rng.random((N, 8, 1, NR)) < share, 64, R)
def shares(rng):
    return np.stack([rng.permutation(np.array([0.1, 0.3, 0.3, 0.5, 0.5, 0.7, 0.7, 0.85])) for q in range(N)])[:, :, None, None]
def parts(rng):
    a = rng.choice(np.array([0.3, 1.0]), (N, 8, 1, NR))
    R = np.clip((16 + 32 * a * (rng.random((N, 8, 16, NR)) - 0.5)).astype(np.int64), 0, 31)
    H = rng.integers(90, 180, (N, 8, RO)) - 12 * np.arange(RO)
    return (rng.integers(0, 256, (N, 8, 16)), kill(rng, R, shares(rng)), rng.integers(0, NR, (N, 8, 16, NC)), rng.integers(0, 4096, (N, 8, NR)),
            rng.integers(0, 32, (N, 8, 16, L)), rng.integers(0, 4096, (N, 8, L)), np.maximum(H, 0))
def pack(w, R, C, P, Z, F, H):
    i = lambda a, *s: np.ascontiguousarray(a.reshape(*s)).astype(np.int32)
    return {"rec": np.ascontiguousarray(R.reshape(N, 128, NR)).astype(np.float32).astype(BF), "cel": i(C, N, 128, NC), "po": i(P, N, 8, NR),
            "pat": np.ascontiguousarray(Z.reshape(N, 128, L)).astype(np.float32).astype(BF), "phi": i(F, N, 8, L), "th": i(H, N, 8, RO), "wt": i(w, N, 128, 1)}
def lowest(ok, c):
    first = np.full((8, NC), L); lane = np.arange(L)[None, :]; g = np.arange(8)[:, None]
    np.minimum.at(first, (np.broadcast_to(g, c.shape), c), np.where(ok, lane, L))
    return ok & (first[g, c] == lane)
def look(R, C, Z, c):
    s = np.take_along_axis(C, c[:, None, :], 2)
    v = np.take_along_axis(R, s.reshape(8, 1, 16 * L), 2).reshape(8, 16, 16, L)
    return s, np.sum(np.abs(v - Z[:, :, None, :]), axis=1), v[:, 0] < 64
def at(a, k):
    return np.take_along_axis(a, k[:, None, :], 1)[:, 0]
def visit(R, C, P, Z, F, w, h, t):
    h1 = h[:, None, None]
    u = np.sum(w[:, :, None] * Z, axis=1) & 4095
    c = ((F * u >> 5) + F + 77 * t) & (NC - 1); e = ((c * u >> 5) + c + 1) & (NC - 1)
    s, d, live = look(R, C, Z, c); s2, d2, live2 = look(R, C, Z, e)
    sup = live & (d < h1); riv = live & (d >= h1)
    gain = 4 * np.sum(np.where(sup, h1 - d, 0), axis=1); loss = np.sum(np.where(riv, d - h1, 0), axis=1)
    acc = lowest(gain >= loss, c)
    has = np.any(sup, axis=1); y = np.argmin(np.where(sup, d, 9999), axis=1); ny = at(s, y)
    foe = np.any(riv, axis=1); nv = at(s, np.argmax(np.where(riv, d, -1), axis=1))
    zn = np.where(has[:, None, :], (Z + np.take_along_axis(R, ny[:, None, :], 2)) >> 1, Z)
    fn = np.where(acc & has, (np.take_along_axis(P, ny, 1) + 5 * at(d, y) + F) & 4095, (5 * F + u) & 4095)
    n = S * np.arange(L)[None, :] + (u & (S - 1))
    R2 = R.copy(); C2 = C.copy(); P2 = P.copy()
    g, i = np.nonzero(acc & foe); R2[g, :, nv[g, i]] = 64
    g, i = np.nonzero(acc); R2[g, :, n[g, i]] = zn[g, :, i]; P2[g, n[g, i]] = fn[g, i]
    g, i = np.nonzero(acc & np.any(~live, axis=1)); row = np.argmax(~live, axis=1)
    C2[g, row[g, i], c[g, i]] = n[g, i]
    acc2 = lowest(acc & ~np.any(live2 & (d2 < h1), axis=1), e)
    g, i = np.nonzero(acc2 & np.any(~live2, axis=1)); row = 15 - np.argmax(~live2[:, ::-1], axis=1)
    C2[g, row[g, i], e[g, i]] = n[g, i]
    return R2, C2, P2, zn, fn, acc
def setup_inputs(rng):
    return pack(*parts(rng))
def setup_inputs_spread(rng):
    w, R, C, P, Z, F, H = parts(rng)
    R = np.minimum((32 * rng.random((N, 8, 16, NR)) ** np.exp2(rng.integers(-2, 3, (N, 8, 1, NR)))).astype(np.int64), 31)
    Z = np.minimum((32 * rng.random((N, 8, 16, L)) ** np.exp2(rng.integers(-2, 3, (N, 8, 1, L)))).astype(np.int64), 31)
    C = np.minimum((NR * rng.random((N, 8, 16, NC)) ** 3).astype(np.int64), NR - 1)
    P = np.minimum(np.exp2(12 * rng.random((N, 8, NR))).astype(np.int64), 4095); F = np.minimum(np.exp2(12 * rng.random((N, 8, L))).astype(np.int64), 4095)
    w = np.minimum(np.exp2(8 * rng.random((N, 8, 16))).astype(np.int64), 255)
    H = np.where(rng.random((N, 8, RO)) < 0.6, rng.integers(60, 220, (N, 8, RO)), rng.integers(0, 481, (N, 8, RO)))
    return pack(w, kill(rng, R, shares(rng)), C, P, Z, F, H)
def edge(rng, n):
    k = rng.integers(0, 4, (N, 8, 1, n))
    return 31 * np.where(k <= 1, 0, np.where(k == 2, 1, rng.integers(0, 2, (N, 8, 16, n))))
def setup_inputs_ends(rng):
    w = 255 * rng.integers(0, 2, (N, 8, 16)); R = kill(rng, edge(rng, NR), 0.4); Z = edge(rng, L)
    C = np.where(rng.random((N, 8, 16, NC)) < 0.7, (NR - 1) * rng.integers(0, 2, (N, 8, 16, NC)), rng.integers(0, NR, (N, 8, 16, NC)))
    P = 4095 * rng.integers(0, 2, (N, 8, NR)); F = 4095 * rng.integers(0, 2, (N, 8, L)); H = 480 * rng.integers(0, 2, (N, 8, RO))
    for q in range(N):
        for g in range(6):
            R[q, g, :, 0] = (0, 31, 64)[(q + g) % 3]; R[q, g, :, NR - 1] = (0, 31, 64)[(q + g + 1) % 3]
    w[:, 5] = 0; w[:, 5, 0] = 195; Z[:, 5, 0, 0] = 21; F[:, 5, 0] = 4095
    R[:, 6] = 64; Z[:, 6] = 0; F[:, 6] = 0
    H[:, 7, 0] = 0; H[:, 7, 1] = 480; R[:, 7, :, 0] = 31; R[:, 7, :, NR - 1] = 0
    C[:, 7, :, 0] = 0; C[:, 7, :, NC - 1] = 0; C[:, 7, :, 77] = NR - 1
    for k in (0, 5, L - 2, L - 1):
        Z[:, 7, :, k] = 0; F[:, 7, k] = 0
    for q in range(N):
        a = visit(R[q], C[q], P[q], Z[q], F[q], w[q], H[q, :, 0], 0)[5]; a[6] = False
        m = 1 + ((30 - int(np.count_nonzero(a))) & 31)
        F[q, 6, rng.permutation(L)[:m - 1]] = np.arange(1, m)
    return pack(w, R, C, P, Z, F, H)
def selfsame(rng, u0, p0):
    p = np.arange(4096)[:, None]; u = np.arange(256)[None, :]
    c = ((p * u >> 5) + p) & (NC - 1); e = ((c * u >> 5) + c + 1) & (NC - 1)
    c0 = ((p0 * u0 >> 5) + p0) & (NC - 1); e0 = ((c0 * u0 >> 5) + c0 + 1) & (NC - 1)
    i, j = np.nonzero((c == e) & (c != c0) & (c != e0)); z = int(rng.integers(0, len(i)))
    return int(j[z]), int(i[z])
def setup_inputs_corners(rng):
    w, R, C, P, Z, F, H = parts(rng)
    for q in range(N):
        for g in range(8):
            o = (g + q) & 7
            if o == 0:
                R[q, g] = 64; Z[q, g] = 0; F[q, g] = rng.permutation(NC)[:L]
                w[q, g] = 0; w[q, g, 0] = 163; Z[q, g, 0, 0] = 25; F[q, g, 0] = 4093
                u, p = selfsame(rng, 4075, 4093)
                w[q, g, 1] = 1; w[q, g, 2] = 32; Z[q, g, 1, 1] = u & 31; Z[q, g, 2, 1] = u >> 5; F[q, g, 1] = p
            elif o == 1:
                R[q, g] = rng.integers(0, 32, (16, NR))
            elif o == 2:
                h = NR // 2; R[q, g, :, :h] = rng.integers(0, 32, (16, h)); R[q, g, :, h:] = 64
                C[q, g] = rng.integers(0, h, (16, NC)) + h * (np.arange(NC) & 1)[None, :]
                C[q, g, 15, 2::4] = h + rng.integers(0, h, NC // 4); C[q, g, 0, 3::4] = rng.integers(0, h, NC // 4)
            elif o == 3:
                C[q, g] = rng.integers(0, NR, (1, NC))
            elif o == 4:
                w[q, g] = 0; C[q, g] = S * rng.integers(0, L, (16, NC))
            elif o == 5:
                H[q, g] = 0; R[q, g] = np.where(R[q, g, :1] == 64, 64, 7 + (rng.random((1, NR)) < 0.1)); Z[q, g] = 7 + (rng.random((1, L)) < 0.1)
            elif o == 6:
                H[q, g] = 480; R[q, g] = np.where(R[q, g, :1] == 64, 64, 31 * rng.integers(0, 2, (1, NR))); Z[q, g] = 31 * rng.integers(0, 2, (1, L))
            else:
                w[q, g] = 255; C[q, g] = rng.choice(np.array([0, 1, S - 1, S, NR - S, NR - 2, NR - 1]), (16, NC))
                F[q, g] = 4095 * rng.integers(0, 2, L); P[q, g] = 4095 * rng.integers(0, 2, NR)
    return pack(w, R, C, P, Z, F, H)
def meet(rng):
    p = rng.integers(0, 4096, 1024)[:, None]; u = np.arange(1024)[None, :]
    c = ((p * u >> 5) + p) & (NC - 1); e = ((c * u >> 5) + c + 1) & (NC - 1); k = e[int(rng.integers(0, 1024)), int(rng.integers(512, 1024))]
    i, j = np.nonzero(e == k); o = rng.permutation(len(i)); i, j = i[o], j[o]
    x = np.resize(rng.permutation(np.unique(c[i, j], return_index=True)[1]), L); i, j = i[x], j[x]
    a, b = np.nonzero((e != k) & ~np.isin(c, c[i, j])); z = int(rng.integers(0, len(a)))
    return u[0, j], p[i, 0], int(u[0, b[z]]), int(p[a[z], 0])
def setup_inputs_crowd(rng):
    w, R, C, P, Z, F, H = parts(rng)
    for q in range(N):
        for g in range(8):
            o = (g + q) & 7; f0 = int(rng.integers(0, 4095))
            if q < 2:
                R[q, g] = 64; Z[q, g] = 0; F[q, g] = rng.permutation(NC)[:L]; H[q, g, 1] = int(rng.integers(220, 260))
            elif o <= 2:
                Z[q, g] = Z[q, g, :, :1].copy(); F[q, g] = f0; H[q, g, 0] = 480
                if o == 1: F[q, g, L - 1] = f0 + 1
                if o == 2: F[q, g, 1::2] = f0 + 1
            elif o <= 4:
                u, p, u1, p1 = meet(rng)
                if o == 4: u[L - 1] = u1; p[L - 1] = p1
                w[q, g] = 0; w[q, g, 0] = 1; w[q, g, 1] = 32; R[q, g] = 64; Z[q, g, 0] = u & 31; Z[q, g, 1] = u >> 5; F[q, g] = p
            elif o <= 6:
                w[q, g] = 0; R[q, g] = rng.integers(0, 4, (16, NR)); R[q, g, :, NR - 1] = 31; Z[q, g] = rng.integers(0, 4, (16, L)); F[q, g] = rng.permutation(NC)[:L]; H[q, g, 0] = 200
                C[q, g] = rng.integers(0, NR - 1, (16, NC)); C[q, g, rng.integers(0, 16, NC), np.arange(NC)] = NR - 1
                if o == 6: C[q, g, :, F[q, g, 3]] = rng.integers(0, NR - 1, 16)
            else:
                w[q, g] = 0; F[q, g] = f0; H[q, g, 0] = 150
    F[1, 7, L - 1] = F[1, 7, 0]
    return pack(w, R, C, P, Z, F, H)
def setup_inputs_ties(rng):
    w, R, C, P, Z, F, H = parts(rng)
    R = kill(rng, 8 * rng.integers(0, 2, (N, 8, 16, NR)), shares(rng)); Z = 8 * rng.integers(0, 2, (N, 8, 16, L)); H = 8 * rng.integers(4, 11, (N, 8, RO))
    C[:, :, 15] = np.where(rng.random((N, 8, NC)) < 0.3, C[:, :, 0], C[:, :, 15])
    return pack(w, R, C, P, Z, F, H)
def check_inputs(d):
    bad = []
    for k, lo, hi in (("rec", 0, 64), ("cel", 0, NR - 1), ("po", 0, 4095), ("pat", 0, 31), ("phi", 0, 4095), ("th", 0, 480), ("wt", 0, 255)):
        a = np.asarray(d[k]).astype(np.float64)
        if not (np.min(a) >= lo and np.max(a) <= hi and np.all(a == np.floor(a))): bad.append("range of " + k)
    a = np.asarray(d["rec"]).astype(np.float32).reshape(N, 8, 16, NR)
    if not np.all(np.all(a == 64, axis=2) | np.all(a <= 31, axis=2)): bad.append("a record of rec is neither living nor dead")
    return bad
def reference(rec, cel, po, pat, phi, th, wt):
    R = list(rec.astype(np.float32).astype(np.int32).reshape(N, 8, 16, NR)); C = list(cel.astype(np.int32).reshape(N, 8, 16, NC)); P = list(po.astype(np.int64))
    Z = list(pat.astype(np.float32).astype(np.int32).reshape(N, 8, 16, L)); F = list(phi.astype(np.int64))
    w = wt.astype(np.int32).reshape(N, 8, 16); H = th.astype(np.int64); A = [0] * N
    for t in range(RO):
        for q in range(N):
            R[q], C[q], P[q], Z[q], F[q], acc = visit(R[q], C[q], P[q], Z[q], F[q], w[q], H[q, :, t] + (A[q] & 31), t)
            A[q] = int(np.count_nonzero(acc))
        Z = [Z[(q - ST) % N] for q in range(N)]; F = [F[(q - ST) % N] for q in range(N)]
    return {"yrec": np.stack(R).reshape(N, 128, NR).astype(np.float32).astype(BF), "ycel": np.stack(C).reshape(N, 128, NC).astype(np.float32), "ypo": np.stack(P).astype(np.float32),
            "ypat": np.stack(Z).reshape(N, 128, L).astype(np.float32).astype(BF), "yphi": np.stack(F).astype(np.float32)}

@@ -1,0 +1,691 @@
+from concourse.mybir import AluOpType, AxisListType, ActivationFunctionType
+
+OP = AluOpType
+AF = ActivationFunctionType
+L, NR, NC, VIS, STEP = 192, 3072, 2048, 3, 3
+RW, CW = NR + L, NC + L
+POOLS = {"F": 19000, "I": 2900, "U": 1600, "B": 33000, "H": 10200}
+DTN = {"F": "float32", "I": "int32", "U": "uint16", "B": "bfloat16", "H": "float16"}
+SCRATCH = {
+    "rec_t": ("sbuf", [128, RW], "bfloat16"), "cel_t": ("sbuf", [128, CW], "float32"), "po_t": ("sbuf", [128, RW], "float32"),
+    "cel_i": ("sbuf", [128, NC], "int32"), "pod": ("dram", [8, NR], "float32"),
+    "zrep": ("sbuf", [128, 16 * L], "bfloat16"),
+}
+for _k in POOLS:
+    SCRATCH["pool" + _k] = ("sbuf", [128, POOLS[_k]], DTN[_k])
+for _t in range(1, VIS + 1):
+    SCRATCH["zl%d" % _t] = ("sbuf", [128, L], "bfloat16")
+    SCRATCH["pl%d" % _t] = ("sbuf", [128, 12 if _t < VIS else L], "float32")
+BANKS = ["b0", "b1", "b2", "b3", "b4", "b5", "e0", "e1"]
+for _b in BANKS:
+    SCRATCH[_b] = ("psum", [128, 512], "float32")
+SITE = {"dA": "b0", "kP": "b0", "hP": "b0", "tP": "b1", "zP": "b1", "vf": "b1", "ne": "b1", "de": "b2", "lP": "b2", "u": "b2", "s2": "b2",
+        "near": "b3", "dB": "b3", "acc": "b3", "xv": "b3", "fv": "b3", "nv": "b3", "s1": "b4", "nc": "b4", "xe": "b4", "fe": "b4", "aP": "b4",
+        "far": "b5", "xc": "b5", "fc": "b5", "win": "e0", "m1": "e0", "D1": "e0", "m2": "e1", "D2": "e1"}
+SEMAPHORES = ["sv", "sa", "sp", "sg", "ls"] + ["d%d" % i for i in range(20)] + ["rz%d" % t for t in (1, 2, 3)] + ["rp%d" % t for t in (1, 2, 3)]
+NS = 0.83 * 1.15e-3
+MAGIC = 12582912.0
+BIAS = {"ent11": 205, "early1": -530, "far1": 307, "ent12": 315, "far2": 112, "newz0": 492, "cg11": 736, "phL2": 73, "acc2": 31, "ent10": -55,
+        "cg02": 227, "cg22": 638, "load": 630, "cg12": 434, "near2": -74, "eg12": 8, "ecell2": -5, "acc0": 73, "n0": -120, "ecell0": -376,
+        "E21": 125, "n1": -151, "cg01": 238, "n2": -497, "lists2": 251, "ecell1": 3, "E20": -2, "zrep2": -222, "E31": 317, "early2": -60,
+        "E30": 339, "cell2": 160, "cg10": 75, "eg01": 183, "eg02": 110, "newz2": -221, "eg21": 107, "ent20": 1, "phL0": -531, "slots0": 348,
+        "newz1": 132, "zrep0": 67, "acc1": 106, "eg22": 159, "eg11": 20, "far0": 892, "cg20": -1, "cg21": 220, "phL1": -162, "ent21": -1,
+        "slots2": 5, "near1": 242, "E32": -62, "E10": 112, "cg00": 605, "ent22": -73, "slots1": 218, "eg10": 5, "zrep1": -73, "cell0": 4,
+        "lists0": -9, "lists1": -3, "near0": 2, "cell1": -1}
+CACHE = {}
+
+
+def build(ne):
+    ops, top, ndma, cur, vis = [], {k: 0 for k in POOLS}, [0], ["load"], []
+
+    def new(k, w):
+        o = top[k]
+        top[k] = o + (w + 15) // 16 * 16
+        if top[k] > POOLS[k]:
+            raise ValueError("pool %s is full" % k)
+        return ("pool" + k, o, w)
+
+    def r(t, c0=0, c1=None, st=1, p0=0, p1=128):
+        return ("R", t[0], t[1] + c0, t[1] + (t[2] if c1 is None else c1), st, p0, p1)
+
+    def ref(x):
+        return x if isinstance(x, (int, float)) or x is None or x[0] in ("R", "X") else r(x)
+
+    def ind(win, off):
+        return ("X", ref(win), ref(off))
+
+    ptop, sites = {b: 0 for b in BANKS}, {}
+
+    def place(site, w):
+        if site not in sites:
+            b = SITE[site]
+            sites[site] = (b, ptop[b], w)
+            ptop[b] += w
+            if ptop[b] > 512:
+                raise ValueError("bank %s is full" % b)
+        return sites[site]
+
+    def spans(x):
+        if x is None or isinstance(x, (int, float)):
+            return []
+        if x[0] == "X":
+            return spans(x[1]) + spans(x[2])
+        return [(x[1], x[2], x[3])]
+
+    def ncol(x):
+        return 16 * ncol(x[2]) if x[0] == "X" else (x[3] - x[2] + x[4] - 1) // x[4]
+
+    def ap(T, x):
+        if x is None or isinstance(x, (int, float)):
+            return x
+        if x[0] == "X":
+            return ap(T, x[1]).indirect(ap(T, x[2]))
+        t = T[x[1]]
+        return t[x[5]:x[6], x[2]:x[3]] if x[4] == 1 else t[x[5]:x[6], x[2]:x[3]:x[4]]
+
+    def two(x):
+        return x[0] == "R" and x[1] in ("poolB", "poolH", "poolU", "zrep", "rec_t")
+
+    def add(q, fn, reads, writes, cost, sem=None, val=1):
+        ops.append({"q": q, "fn": fn, "r": reads, "w": writes, "cost": cost, "sem": sem, "val": val, "i": len(ops),
+                    "tag": cur[0] + (str(vis[0]) if vis else "")})
+
+    def vcost(o, ins, rate):
+        n = ncol(o)
+        if o[0] == "X":
+            return 0.06 + n * 3.5 * NS
+        if any(x[0] == "X" for x in ins):
+            return 0.06 + n * 1.55 * NS
+        return 0.02 + max(64, n * rate) * NS
+
+    def vop(fn, outs, ins, cost):
+        add("v", fn, [s for x in ins for s in spans(x)], [s for x in outs for s in spans(x)], cost)
+
+    def vt(o, a, b, op):
+        o, a, b = ref(o), ref(a), ref(b)
+        both = a[0] == "R" and a[1] not in BANKS and b[1] not in BANKS
+        vop(lambda g, T: g.vector.tensor_tensor(out=ap(T, o), in0=ap(T, a), in1=ap(T, b), op=op), [o], [a, b], vcost(o, [a, b], 2 if both else 1))
+
+    def vs(o, a, s1, s2, op0, op1=None):
+        o, a, s1, s2 = ref(o), ref(a), ref(s1), ref(s2)
+        ex = {} if op1 is None else {"op1": op1}
+        vop(lambda g, T: g.vector.tensor_scalar(out=ap(T, o), in0=ap(T, a), scalar1=ap(T, s1), scalar2=ap(T, s2), op0=op0, **ex),
+            [o], [a, s1, s2], vcost(o, [a], 0.5 if two(o) and two(a) else 1))
+
+    def vc(o, a):
+        o, a = ref(o), ref(a)
+        vop(lambda g, T: g.vector.tensor_copy(out=ap(T, o), in_=ap(T, a)), [o], [a], vcost(o, [a], 0.5 if two(o) and two(a) else 1))
+
+    def vscan(o, d0, d1, init, o0, o1):
+        o, d0, d1 = ref(o), ref(d0), ref(d1)
+        vop(lambda g, T: g.vector.tensor_tensor_scan(out=ap(T, o), data0=ap(T, d0), data1=ap(T, d1), initial=init, op0=o0, op1=o1), [o], [d0, d1], vcost(o, [d0], 1))
+
+    def vtr(o, a):
+        o, a = ref(o), ref(a)
+        vop(lambda g, T: g.vector.transpose(out=ap(T, o), in_=ap(T, a)), [o], [a], vcost(o, [a], 1))
+
+    def vred(o, a):
+        o, a = ref(o), ref(a)
+        vop(lambda g, T: g.vector.tensor_reduce(out=ap(T, o), in_=ap(T, a), axis=AxisListType.X, op=OP.add), [o], [a], vcost(a, [a], 1))
+
+    def act(o, a, f, scale=1.0, bias=0.0):
+        o, a, scale, bias = ref(o), ref(a), ref(scale), ref(bias)
+        x = a[0] == "X"
+        add("a", lambda g, T: g.scalar.activation(out=ap(T, o), in_=ap(T, a), func=f, bias=ap(T, bias), scale=ap(T, scale)),
+            [s for y in (a, scale, bias) for s in spans(y)], spans(o), (0.07 if x else 0.03) + max(64, ncol(o) * (1.55 if x else 1)) * NS)
+
+    def mm(ms):
+        ms = [(ref(o), ref(a), ref(b), s, e) for o, a, b, s, e in ms]
+
+        def fn(g, T):
+            k = None
+            for o, a, b, s, e in ms:
+                k = g.tensor.matmul(ap(T, o), ap(T, a), ap(T, b), s, e)
+            return k
+        rd = sorted(set(s for o, a, b, x, e in ms for y in (a, b) for s in spans(y)))
+        add("p", fn, rd, sorted(set(s for m in ms for s in spans(m[0]))), sum(max(64, ncol(m[2])) for m in ms) * NS + 0.03)
+
+    def iota(o, pat, base, cm):
+        o = ref(o)
+        add("g", lambda g, T: g.iota(ap(T, o), pat, base, cm, allow_small_or_imprecise_dtypes=True), [], spans(o), 0.13 + 2 * ncol(o) * NS)
+
+    def sel(o, a, pat, base, cm, fill, cmp_):
+        o, a = ref(o), ref(a)
+        add("g", lambda g, T: g.affine_select(ap(T, o), ap(T, a), pat, cmp_, fill, base, cm), spans(a), spans(o), 0.17 + 2 * ncol(o) * NS)
+
+    def dma(fn, reads, writes, cost, n=1):
+        add("s", fn, reads, writes, cost, "d%d" % ndma[0], 16 * n)
+        ndma[0] += 1
+
+    z, wI, thI, phI, poI = new("B", L), new("I", 1), new("I", 3), new("I", L), new("I", L)
+
+    def load(name, o, cost):
+        o = ref(o)
+        dma(lambda g, T: g.sync.dma_start(out=ap(T, o), in_=T[name][:]), [], spans(o), cost)
+    load("phi", r(phI, p1=8), 2.2)
+    load("pat", z, 2.2)
+    load("wt", wI, 2.2)
+    load("th", r(thI, p1=8), 2.2)
+    for h in (0, 1):
+        cs = ("cel_i", 1024 * h, 1024)
+        dma(lambda g, T, h=h: g.sync.dma_start(out=T.cel_i[:, 1024 * h:1024 * h + 1024], in_=T.cel[:, 1024 * h:1024 * h + 1024]), [], spans(ref(cs)), 4.0 + 2 * h)
+    dma(lambda g, T: g.sync.dma_start(out=T.rec_t[:, 0:NR], in_=T.rec[:]), [], [("rec_t", 0, NR)], 8.5)
+    load("po", poI, 9.0)
+
+    cur[0] = "const"
+
+    def col(a, scale=1.0, bias=0.0, f=AF.Identity, k="F"):
+        o = new(k, ref(a)[3] - ref(a)[2])
+        act(o, a, f, scale, bias)
+        return o
+
+    def same(a, neg, k="F"):
+        return col(col(a, 1.0, neg, AF.Abs), -1.0, 1.0, AF.Relu, k)
+
+    def tile(a, scale, bias=0.0):
+        return col(a, scale, bias, AF.Identity, "B")
+    p2, pF, yg, i15, b12, j6, xF, iF = new("F", 1), new("F", 1), new("F", 128), new("F", L), new("F", 12), new("F", 6), new("F", 144), new("F", L)
+    p4, i12 = new("F", 1), new("F", 96)
+    iota(p2, [[0, 1]], -15, 2)
+    iota(pF, [[0, 1]], 0, 1)
+    iota(yg, [[1, 8], [0, 16]], 0, 0)
+    iota(i15, [[0, 12], [1, 16]], 0, 0)
+    iota(xF, [[1, 144]], -15, 0)
+    iota(b12, [[1, 12]], 0, 0)
+    iota(p4, [[0, 1]], -31, 2)
+    iota(j6, [[32, 6]], -11, 2)
+    iota(i12, [[0, 8], [1, 12]], 0, 0)
+    iota(iF, [[1, L]], 0, 0)
+    gc = col(col(p2, 1.0 / 32, MAGIC), 1.0, -MAGIC)
+    kc = col(gc, -16.0, pF)
+    ng, npg = col(gc, -1.0), col(gc, -16.0)
+    M0, diag = col(i15, 1.0, 0.0, AF.Sign), new("F", L)
+    vs(diag, i15, kc, None, OP.is_equal)
+    U, wc = same(xF, npg, "B"), new("F", 1)
+    vc(wc, wI)
+    UW = tile(U, wc)
+    sel8, ph16, th16, thc = new("H", 128), new("H", L), new("H", 3), new("F", 3)
+    vs(r(sel8, p1=8), r(yg, p1=8), r(pF, p1=8), None, OP.is_equal)
+    vs(r(ph16, p1=8), r(phI, p1=8), -2048.0, None, OP.add)
+    vs(r(th16, p1=8), r(thI, p1=8), 0.0, None, OP.add)
+    xq = place("xc", L)
+    mm([(xq, r(sel8, p1=8), r(ph16, p1=8), True, True)])
+    pm, ps, phi = new("F", L), new("F", L), new("F", 12)
+    vt(pm, xq, diag, OP.mult)
+    vscan(ps, M0, pm, 0.0, OP.mult, OP.add)
+    act(phi, r(ps, 15, L, 16), AF.Identity, 1.0, 2048.0)
+    tp = r(place("u", 12), 0, 3)
+    mm([(tp, r(sel8, p1=8), r(th16, p1=8), True, True)])
+    act(thc, tp, AF.Copy)
+    for x in (0, 1):
+        vc(("cel_t", 1024 * x, 1024), ("cel_i", 1024 * x, 1024))
+    BO = same(yg, ng, "B")
+    lane, bl = col(b12, 16.0, kc), new("U", 12)
+    i16A, dumR, dumC, dumS = col(lane, 16.0), col(lane, 1.0, float(NR)), col(lane, 1.0, float(NC)), col(lane, 1.0, NR - 1536.0)
+    dumRC = new("F", 24)
+    act(r(dumRC, 0, 12), dumR, AF.Copy)
+    act(r(dumRC, 12, 24), dumC, AF.Copy)
+    vc(bl, b12)
+    bo8 = new("B", 8)
+    act(bo8, r(BO, 0, 128, 16), AF.Copy)
+    m3, m1, one = tile(bo8, -3.0), tile(bo8, -1.0), tile(BO, 0.0, 1.0)
+    RS = col(M0, 2.0e9, -1.0e9)
+    DW, mb1, mb2, list2 = new("B", 240), new("F", 96), new("F", 96), new("U", 6)
+    act(r(DW, 0, 192), M0, AF.Identity, 0.0)
+    act(r(DW, 192, 240), r(M0, 0, 48), AF.Identity, 0.0)
+    act(r(DW, 112, 128), r(diag, 0, 16), AF.Copy)
+    vs(mb1, i12, 8.0, -4.0, OP.is_ge, OP.mult)
+    vt(mb2, mb1, i12, OP.add)
+    MSK = same(mb2, ng)
+    t1 = col(j6, 1.0, col(npg, 2.0))
+    y1, y2, js = col(col(t1, 1.0 / 24, MAGIC), 1.0, -MAGIC), col(col(col(t1, 1.0, 8.0), 1.0 / 24, MAGIC), 1.0, -MAGIC), new("F", 6)
+    vt(js, y1, y2, OP.add)
+    vc(list2, js)
+    oc = col(col(col(p4, 1.0 / 64, MAGIC), 1.0, -MAGIC), -2.0, gc)
+    ec = col(oc, -1.0, 1.0)
+    klt = col(col(kc, -1.0, 11.5, AF.Sign), 1.0, 0.0, AF.Relu)
+    k0, k10, k11, k12, k13 = [same(kc, -float(v)) for v in (0, 10, 11, 12, 13)]
+    hf, pw, pw2, d16, d17, sc0, sc2 = new("F", 48), new("F", 16), new("F", 16), new("F", 16), new("F", 16), new("F", 1), new("F", 1)
+    for x, v in ((0, 0.5), (16, 0.0), (32, 2.0)):
+        act(r(hf, x, x + 16), r(M0, 0, 16), AF.Identity, 0.0, v)
+    vscan(pw, r(hf, 0, 16), r(hf, 16, 32), 2.0, OP.mult, OP.add)
+    vscan(pw2, r(hf, 32, 48), r(hf, 16, 32), 0.5, OP.mult, OP.add)
+    vt(d16, pw, r(diag, 0, 16), OP.mult)
+    vt(d17, pw2, r(diag, 0, 16), OP.mult)
+    vred(sc0, d16)
+    vred(sc2, d17)
+    scol = col(sc0, klt)
+    fs, gs = col(k13, -1.0 / 512, klt), col(k12, 1.0 / 512, klt)
+    fse, fso = col(fs, ec), col(fs, oc)
+    kv = col(col(kc, 1.0, 0.0, AF.Sign), klt)
+    fb0 = col(k10, 2.0, col(klt, -0.5))
+    fb, gb = col(fb0, 1.0, k12), col(fb0, 1.0, k13)
+    fbe, fbo = col(fb, ec), col(fb, oc)
+    C2, c2c, bM = new("H", L), col(col(sc2, -0.5, 0.5), klt), col(k11, 1.0, MAGIC)
+    vs(C2, M0, 0.0, c2c, OP.mult, OP.add)
+    b11 = col(col(scol, 0.5, col(klt, -0.5)), 1.0, col(kv, 1025.0))
+    f11 = col(k11, -2050.0, col(k0, 1025.0, col(klt, 1024.5)))
+    fb2, gb2 = col(f11, 1.0, k12), col(f11, 1.0, k13)
+    fbe2, fbo2 = col(fb2, ec), col(fb2, oc)
+    Y, GT, EQ, NE = [[1, 128]], OP.is_gt, OP.is_equal, OP.not_equal
+    I16, LA, L16, nBO, TA, TL, TB, TH = [new("B", 128) for i in range(8)]
+    KV = tile(one, col(kv, -2.0))
+    act(nBO, BO, AF.Identity, -1.0)
+    sel(I16, one, Y, 0, -1, 0.0, EQ)
+    sel(LA, KV, Y, 1, -1, 0.0, EQ)
+    sel(L16, LA, Y, 0, -1, 1.0, NE)
+    sel(TA, nBO, Y, 0, -1, 0.0, GT)
+    sel(TL, TA, Y, 0, -1, 1.0, NE)
+    sel(TB, nBO, [[-1, 128]], 0, 1, 0.0, GT)
+    sel(TH, TB, Y, 0, -1, 1.0, NE)
+    nI, hI16, kI16 = [tile(I16, v) for v in (-1.0, 0.5, -1024.0)]
+    laneC, c64 = tile(iF, col(k12, 1.0, k13)), tile(M0, 0.0, 64.0)
+    pas, acc, cand, winB, vfB = [new("B", 16) for i in range(5)]
+    P = [[tile(I16, ec), new("B", 128)], [new("B", 128), tile(I16, oc)]]
+    sel(P[0][1], tile(one, ec), Y, -16, -1, 0.0, EQ)
+    sel(P[1][0], tile(one, oc), Y, 16, -1, 0.0, EQ)
+    knear = col(kc, -1.0 / 16, 255.0 + 15.0 / 16)
+    act(("rec_t", NR, L), M0, AF.Identity, 0.0, 64.0)
+    act(("po_t", NR, L), M0, AF.Identity, 0.0)
+    poF = new("F", L)
+    vc(poF, poI)
+    dma(lambda g, T: g.sync.dma_start(out=T.pod[:], in_=ap(T, r(poF))), spans(r(poF)), [("pod", 0, 1)], 2.2)
+    fan_id = ndma[0]
+
+    def fan(g, T):
+        k = None
+        for i in range(16):
+            k = g.sync.dma_start(out=T.po_t[i::16, 0:NR], in_=T.pod[:])
+            if i < 15:
+                k.then_inc(T.sem["d%d" % fan_id], 16)
+        return k
+    dma(fan, [("pod", 0, 1)], [("po_t", 0, NR)], 7.0, 16)
+    h = new("F", 1)
+    vc(h, r(thc, 0, 1))
+    celw, celn, recw, recn, pow_ = ("cel_t", 0, CW), ("cel_t", 0, NC), ("rec_t", 0, RW), ("rec_t", 0, NR), ("po_t", 0, RW)
+    Es = [new("B", 2048) for x in range(3)]
+    dfad = [(new("B", 1024), new("B", 1024)) for x in range(6)]
+
+    def expand(src):
+        X = new("H", L)
+        vt(X, ind(src, bl), diag, OP.mult)
+        return X
+
+    def pairs(val, E, site):
+        X, Vh, b = expand(val), new("H", L), site != "v"
+        xP, fp = place("x" + site, L), place("f" + site, L)
+        if b:
+            mm([(xP, BO, X, True, True)])
+            vs(Vh, xP, scol, b11, OP.mult, OP.add)
+        else:
+            Vi = new("F", L)
+            mm([(xP, BO, X, True, False), (xP, I16, C2, False, True)])
+            act(Vi, xP, AF.Identity, scol, bM)
+            vs(Vh, Vi, -MAGIC, None, OP.add)
+        mm([(fp, L16, Vh, True, False), (fp, I16, laneC, False, True)])
+        G, Fe, Fo = new("B", L), new("B", L), new("B", L)
+        act(Fe, fp, AF.Identity, fse, fbe2 if b else fbe)
+        act(G, fp, AF.Identity, gs, gb2 if b else gb)
+        act(Fo, fp, AF.Identity, fso, fbo2 if b else fbo)
+        for a in range(4):
+            bank, ms = ("e1", "e0")[a & 1], []
+            for x, F in ((0, Fe), (1, Fo)):
+                pp = {"p0": 32 * a, "p1": 32 * a + 32}
+                ms.append(((bank, 256 * x, L), r(F, 0, 128, **pp), r(G, **pp), True, True))
+                ms.append(((bank, 256 * x + L, 64), r(F, 64, L, **pp), r(G, 128, L, **pp), True, True))
+            mm(ms)
+            act(r(E, 512 * a, 512 * a + 512), (bank, 0, 512), AF.Relu, 512.0, -1536.0)
+        return E
+
+    def lowest(vec, E, site, out):
+        q, ms = place("n" + site, 16), []
+        for g in range(8):
+            h0, h1 = r(vec, 2 * g, 2 * g + 1), r(vec, 2 * g + 1, 2 * g + 2, p0=64)
+            ms.append((r(q, 2 * g, 2 * g + 1), r(E, 256 * g, 256 * g + 128), h0, True, True))
+            ms.append((r(q, 2 * g + 1, 2 * g + 2), r(E, 256 * g + 64, 256 * g + L), h0, True, False))
+            ms.append((r(q, 2 * g + 1, 2 * g + 2), r(E, 256 * g + 128, 256 * g + 256, p0=64), h1, False, True))
+        mm(ms)
+        vt(out, vec, q, OP.is_gt)
+        return out
+
+    def score(terms, site, extra=None):
+        for q, a, b in ((r(place(site, 16), 0, 16, 2), 0, 128), (r(place(site, 16), 1, 16, 2), 64, L)):
+            ms = [(q, r(x, a, b), y) for x, y in terms]
+            if extra:
+                ms.append((q, extra[0], extra[1]))
+            mm([m + (i == 0, i == len(ms) - 1) for i, m in enumerate(ms)])
+
+    def to_a(vec, site):
+        X = new("B", 96)
+        vt(X, ind(vec, list2), MSK, OP.mult)
+        q = place(site, 12)
+        mm([(q, r(DW, 112 - 16 * g, 240 - 16 * g), r(X, 12 * g, 12 * g + 12), g == 0, g == 7) for g in range(8)])
+        return q
+
+    def best(key, site, parts):
+        kt, ks, q = new("F", L), new("F", L), place(site, 24)
+        ki, k2, kp = new("I", 12), new("I", 24), new("H", 24)
+        for a, b in parts:
+            vtr(r(kt, a, b), r(key, a, b))
+            vscan(r(ks, a, b), r(RS, a, b), r(kt, a, b), -1.0e9, OP.min, OP.max)
+        vs(ki, r(ks, 15, L, 16), 65536.0, None, OP.mult)
+        vs(r(k2, 0, 12), ki, 4095, None, OP.bitwise_and)
+        vs(r(k2, 12, 24), ki, 16, None, OP.arith_shift_right)
+        vs(kp, k2, -1536.0, None, OP.add)
+        mm([(r(q, ih, 24, 2), P[ih][x], r(kp, x, 24, 2), x == 0, x == 1) for ih in (0, 1) for x in (0, 1)])
+        return r(q, 0, 12), r(q, 12, 24)
+
+    def send(src, name, sem):
+        src = ref(src)
+
+        def fn(g, T, me, dst, topo):
+            rid, pid, se = topo.addr(dst)
+            return g.remote_dma(T[name][:], ap(T, src), T.sem[sem], T.sem.ls, pid, rid, topo.mask(me, dst))
+        add("g", fn, spans(src), [(name + "_sent", 0, 1)], 1.0, "ls", ne)
+        add("net", None, [(name + "_sent", 0, 1)], [(name, 0, SCRATCH[name][1][1])], 2.5, sem, ne)
+
+    for t in range(VIS):
+        last = t == VIS - 1
+        vis[:] = [t]
+        cur[0] = "cell"
+        h5, hm, h511, hmat, hdead = new("F", 1), new("F", 1), new("F", 1), new("H", 8), new("H", 8)
+        act(h5, h, AF.Identity, 5.0)
+        act(hm, h, AF.Identity, -1.0, 512.0)
+        act(h511, h, AF.Identity, 1.0, -511.0)
+        vs(hmat, bo8, h511, None, OP.mult)
+        vs(hdead, bo8, hm, None, OP.mult)
+        cur[0] = "zrep"
+        for k in range(16):
+            act(r(("zrep", 0, 16 * L), k, 16 * L, 16), z, AF.Copy)
+        cur[0] = "cell"
+        uP = place("u", 12)
+        mm([(uP, r(UW, 15 - k, 143 - k), r(z, k, L, 16), k == 0, k == 15) for k in range(16)])
+        uI, u, ma, mb, mc, c, c1, e = [new("I", 12) for i in range(8)]
+        c16, e16 = new("U", 12), new("U", 12)
+        vc(uI, uP)
+        vs(u, uI, 4095, None, OP.bitwise_and)
+        vt(ma, phi, u, OP.mult)
+        vs(mb, ma, 5, None, OP.arith_shift_right)
+        p77 = phi
+        if t:
+            p77 = new("F", 12)
+            act(p77, phi, AF.Identity, 1.0, 77.0 * t)
+        vt(mc, mb, p77, OP.add)
+        vs(c, mc, NC - 1, None, OP.bitwise_and)
+        vc(c16, c)
+        sc16, se16 = new("U", L), new("U", L)
+        vc(sc16, ind(celn, c16))
+        cur[0] = "ecell"
+        me, mf, mg = [new("I", 12) for i in range(3)]
+        vt(me, c, u, OP.mult)
+        vs(mf, me, 5, None, OP.arith_shift_right)
+        vs(c1, c, 1.0, None, OP.add)
+        vt(mg, mf, c1, OP.add)
+        vs(e, mg, NC - 1, None, OP.bitwise_and)
+        vc(e16, e)
+        vc(se16, ind(celn, e16))
+        dc = lambda a, b: r(place("dA", 128), a, b) if b <= 128 else r(place("dB", 64), a - 128, b - 128)
+        for s16, dst in ((sc16, dc), (se16, lambda a, b: r(place("de", L), a, b))):
+            for ch in range(3):
+                cur[0] = ("cg" if s16 is sc16 else "eg") + str(ch)
+                df, ad = dfad[ch + (0 if s16 is sc16 else 3)]
+                for x in (0, 1):
+                    w = 1024 * ch + 512 * x
+                    vt(r(df, 512 * x, 512 * x + 512), ind(recn, r(s16, 64 * ch + 32 * x, 64 * ch + 32 * x + 32)), ("zrep", w, 512), OP.subtract)
+                    act(r(ad, 512 * x, 512 * x + 512), r(df, 512 * x, 512 * x + 512), AF.Abs)
+                q = dst(64 * ch, 64 * ch + 64)
+                mm([(q, r(U, 15 - k, 143 - k), r(ad, k, 1024, 16), k == 0, k == 15) for k in range(16)])
+        cur[0] = "early"
+        n15, n, pa, pb, P2 = new("I", 12), new("F", 12), new("F", 12), new("I", 12), new("I", 12)
+        vs(n15, u, 15, None, OP.bitwise_and)
+        vt(n, n15, i16A, OP.add)
+        act(pa, phi, AF.Identity, 5.0)
+        vt(pb, pa, u, OP.add)
+        vs(P2, pb, 4095, None, OP.bitwise_and)
+        skN, sc32, s16c = new("F", L), new("F", L), new("H", L)
+        act(sc32, ind(celn, c16), AF.Copy)
+        act(skN, sc32, AF.Identity, 2.0 ** -16, knear)
+        vs(s16c, sc16, -1536.0, None, OP.add)
+        cur[0] = "E1"
+        E1 = pairs(c, Es[0], "c")
+        cur[0] = "E2"
+        E2 = pairs(e, Es[1], "e")
+        cur[0] = "n"
+        nm = new("F", 12)
+        act(nm, n, AF.Identity, 1.0, -1536.0)
+        Xn = expand(nm)
+        cur[0] = "slots"
+        q1, q2, K1, K2, dead = new("H", L), new("H", L), new("F", L), new("F", L), new("B", L)
+        for a, b in ((0, 128), (128, L)):
+            d = dc(a, b)
+            vt(r(K1, a, b), r(skN, a, b), d, OP.subtract)
+            vs(r(q1, a, b), d, 512.0, -511.0, OP.min, OP.add)
+            vs(r(q2, a, b), r(q1, a, b), h511, h511, OP.min, OP.subtract)
+            vs(r(dead, a, b), r(q1, a, b), 1.0, None, OP.is_ge)
+        cur[0] = "far"
+        kP = place("kP", L)
+        mm([(kP, I16, q1, True, False), (kP, kI16, dead, False, True)])
+        vt(K2, skN, kP, OP.add)
+        cur[0] = "near"
+        nyP, dd = best(K1, "near", ((0, 128), (128, L)))
+        ny16, d5, has = new("U", 12), new("F", 12), new("F", 12)
+        vs(ny16, nyP, 1536.0, None, OP.add)
+        act(d5, dd, AF.Identity, -5.0, 1275.0 - 5 * 1536.0)
+        vs(has, d5, h5, None, OP.is_lt)
+        pog, pos, pd, Pa, P1, Dp, Dh = new("F", L), new("F", L), new("F", 12), new("I", 12), new("I", 12), new("F", 12), new("F", 12)
+        vt(pog, ind(pow_, ny16), diag, OP.mult)
+        vscan(pos, M0, pog, 0.0, OP.mult, OP.add)
+        vt(pd, d5, phi, OP.add)
+        vt(Pa, r(pos, 15, L, 16), pd, OP.add)
+        vs(P1, Pa, 4095, None, OP.bitwise_and)
+        vt(Dp, P1, P2, OP.subtract)
+        vt(Dh, Dp, has, OP.mult)
+        cur[0] = "newz"
+        hP, tP, zP = place("hP", L), place("tP", L), place("zP", L)
+        hs, rz, zw, zm, zn = [new("B", L) for i in range(5)]
+        mm([(hP, BO, q2, True, True)])
+        act(hs, hP, AF.Sign, -1.0)
+        act(rz, ind(recw, ny16), AF.Copy)
+        mm([(tP, I16, rz, True, False), (tP, nI, z, False, True)])
+        vt(zw, hs, tP, OP.mult)
+        mm([(zP, I16, z, True, False), (zP, hI16, zw, False, True)])
+        act(zm, zP, AF.Identity, 1.0, 159.75)
+        act(zn, zm, AF.Identity, 1.0, -160.0)
+        send(zn, "zl%d" % (t + 1), "rz%d" % (t + 1))
+        cur[0] = "far"
+        vP, fd = best(K2, "far", ((0, L),))
+        vm_, riv, vd, vdr = new("F", 12), new("F", 12), new("F", 12), new("F", 12)
+        vs(riv, fd, 256.0 + 1536.0, h, OP.add, OP.is_ge)
+        vt(vd, vP, dumS, OP.subtract)
+        vt(vdr, vd, riv, OP.mult)
+        vt(vm_, vdr, dumS, OP.add)
+        cur[0] = "E3"
+        E3 = pairs(vm_, Es[2], "v")
+        cur[0] = "acc"
+        score([(q1, m1), (q2, m3), (dead, hdead)], "s1", (one, hmat))
+        vs(pas, place("s1", 16), 0.0, None, OP.is_ge)
+        lowest(pas, E1, "c", acc)
+        accA = to_a(acc, "acc")
+        ft, phN = new("F", 12), new("F", 12)
+        vt(ft, Dh, accA, OP.mult)
+        vt(phN, ft, P2, OP.add)
+        if not last:
+            send(phN, "pl%d" % (t + 1), "rp%d" % (t + 1))
+        cur[0] = "phL"
+        ph2, phL, lP = new("F", 12), new("F", L), place("lP", L)
+        act(ph2, phN, AF.Identity, 1.0, -2048.0)
+        X = expand(ph2)
+        mm([(lP, BO, X, True, True)])
+        act(phL, lP, AF.Identity, 1.0, 2048.0)
+        if last:
+            send(phL, "pl%d" % VIS, "rp%d" % VIS)
+        else:
+            aP, aF, aI, aJ = place("aP", 16), new("F", 1), new("I", 1), new("I", 1)
+            mm([(r(aP, 0, 16, 2), one, r(acc, 0, 16, 2), True, True), (r(aP, 1, 16, 2), r(one, p0=64), r(acc, 1, 16, 2, p0=64), True, True)])
+            vred(aF, aP)
+            vc(aI, aF)
+            vs(aJ, aI, 31, None, OP.bitwise_and)
+        cur[0] = "E3"
+        vfA = to_a(lowest(acc, E3, "v", vfB), "vf")
+        tv, ov, v16 = new("F", 12), new("F", 12), new("U", 12)
+        vt(tv, vdr, vfA, OP.mult)
+        vt(ov, tv, dumR, OP.add)
+        vc(v16, ov)
+        cur[0] = "lists"
+        nd_, cd_, tn, on, u24 = new("F", 12), new("F", 12), new("F", 24), new("F", 24), new("U", 24)
+        vt(nd_, n, dumR, OP.subtract)
+        vt(cd_, c, dumC, OP.subtract)
+        vt(r(tn, 0, 12), nd_, accA, OP.mult)
+        vt(r(tn, 12, 24), cd_, accA, OP.mult)
+        vt(on, tn, dumRC, OP.add)
+        vc(u24, on)
+        n16, cw = r(u24, 0, 12), r(u24, 12, 24)
+        vc(ind(recw, v16), c64)
+        vc(ind(recw, n16), zn)
+        vc(ind(pow_, n16), phL)
+        cur[0] = "ent1"
+        M1, ch1, mP, DP = new("F", L), new("F", L), place("m1", L), place("D1", L)
+        mm([(mP, TL, dead, True, True), (DP, BO, Xn, True, False), (DP, nI, s16c, False, True)])
+        act(M1, mP, AF.Relu)
+        vt(ch1, M1, DP, OP.mult)
+        vt(ind(celw, cw), ch1, sc32, OP.add)
+        cur[0] = "ent2"
+        q1e, q2e, deade = new("H", L), new("H", L), new("B", L)
+        vs(q1e, place("de", L), 512.0, -511.0, OP.min, OP.add)
+        vs(q2e, q1e, h511, h511, OP.min, OP.subtract)
+        vs(deade, q1e, 1.0, None, OP.is_ge)
+        score([(q2e, m1)], "s2")
+        vt(cand, acc, place("s2", 16), OP.is_gt)
+        wA = to_a(lowest(cand, E2, "e", winB), "win")
+        ed, et, eo, ew = new("F", 12), new("F", 12), new("F", 12), new("U", 12)
+        vt(ed, e, dumC, OP.subtract)
+        vt(et, ed, wA, OP.mult)
+        vt(eo, et, dumC, OP.add)
+        vc(ew, eo)
+        M2, sE, s16e, ch2, mP, DP = new("F", L), new("F", L), new("H", L), new("F", L), place("m2", L), place("D2", L)
+        act(sE, ind(celn, e16), AF.Copy)
+        vs(s16e, sE, -1536.0, None, OP.add)
+        mm([(mP, TH, deade, True, True), (DP, BO, Xn, True, False), (DP, nI, s16e, False, True)])
+        act(M2, mP, AF.Relu)
+        vt(ch2, M2, DP, OP.mult)
+        vt(ind(celw, ew), ch2, sE, OP.add)
+        if not last:
+            h = new("F", 1)
+            vt(h, aJ, r(thc, t + 1, t + 2), OP.add)
+            z, phi = ("zl%d" % (t + 1), 0, L), ("pl%d" % (t + 1), 0, 12)
+    dma(lambda g, T: g.sync.dma_start(out=T.ypat[:], in_=T["zl%d" % VIS][:]), [("zl%d" % VIS, 0, L)], [("ypat", 0, 1)], 2.2)
+    dma(lambda g, T: g.sync.dma_start(out=T.yphi[:], in_=T["pl%d" % VIS][::16, :]), [("pl%d" % VIS, 0, L)], [("yphi", 0, 1)], 2.2)
+    dma(lambda g, T: g.sync.dma_start(out=T.ypo[:], in_=T.po_t[::16, 0:NR]), [("po_t", 0, NR)], [("ypo", 0, 1)], 3.0)
+    dma(lambda g, T: g.sync.dma_start(out=T.yrec[:], in_=T.rec_t[:, 0:NR]), [("rec_t", 0, NR)], [("yrec", 0, 1)], 5.0)
+    dma(lambda g, T: g.sync.dma_start(out=T.ycel[:], in_=T.cel_t[:, 0:NC]), [("cel_t", 0, NC)], [("ycel", 0, 1)], 6.0)
+    return ops
+
+
+def depend(ops):
+    hist, deps = {}, []
+    for o in ops:
+        d = set()
+        acc = [(s, False) for s in o["r"]] + [(s, True) for s in o["w"]]
+        for (buf, lo, hi), wr in acc:
+            for (k, a, b, w) in hist.get(buf, []):
+                if (w or wr) and a < hi and lo < b:
+                    d.add(k)
+        for (buf, lo, hi), wr in acc:
+            hh = hist.setdefault(buf, [])
+            if wr:
+                hist[buf] = hh = [x for x in hh if not (lo <= x[1] and x[2] <= hi)]
+            hh.append((o["i"], lo, hi, wr))
+        d.discard(o["i"])
+        deps.append(d)
+    return deps
+
+
+def schedule(ops, deps):
+    n = len(ops)
+    succ = [[] for i in range(n)]
+    for i, d in enumerate(deps):
+        for k in d:
+            succ[k].append(i)
+    lat = lambda k, i: 0.05 if ops[k]["q"] == ops[i]["q"] else (0.12 if ops[k]["q"] != "net" else 0.3)
+    pr = [0.0] * n
+    for i in range(n - 1, -1, -1):
+        pr[i] = ops[i]["cost"] + max([lat(i, j) + pr[j] for j in succ[i]] or [0.0])
+    left = [len(d) for d in deps]
+    ready = {i for i in range(n) if not left[i]}
+    banks = [sorted(set(s[0] for s in o["r"] + o["w"] if s[0] in BANKS)) for o in ops]
+    rt, free, order, end, used = [0.0] * n, {}, [], [0.0] * n, {b: {} for b in BANKS}
+    while ready:
+        pick, cand = None, {q: [] for q in ("v", "a", "p", "g", "s", "net")}
+        for i in sorted(ready):
+            cand[ops[i]["q"]].append(i)
+        for q, li in cand.items():
+            if not li:
+                continue
+            f = free.get(q, 0.0) if q != "net" else 0.0
+            at = {}
+            for i in li:
+                at[i] = max([f, rt[i]] + [end[k] + 0.12 for b in banks[i] for o, k in used[b].items() if o != q])
+            s0 = min(at.values())
+            b = max((i for i in li if at[i] <= s0 + 0.04), key=lambda i: (pr[i] + BIAS.get(ops[i]["tag"], 0.0), -i))
+            if pick is None or at[b] < pick[0]:
+                pick = (at[b], b, q)
+        s, i, q = pick
+        ready.discard(i)
+        free[q] = s + (0.1 if q == "s" else ops[i]["cost"])
+        end[i] = s + ops[i]["cost"]
+        order.append(i)
+        for b in banks[i]:
+            deps[i] |= {k for o, k in used[b].items() if o != q}
+            used[b][q] = i
+        for j in succ[i]:
+            rt[j] = max(rt[j], end[i] + lat(i, j))
+            left[j] -= 1
+            if not left[j]:
+                ready.add(j)
+    return order, max(end)
+
+
+QSEM = {"v": "sv", "a": "sa", "p": "sp"}
+
+
+def plan(ne):
+    if "plan" not in CACHE:
+        ops = build(ne)
+        deps = depend(ops)
+        order, span = schedule(ops, deps)
+        CACHE["plan"] = (ops, deps, order, span)
+    return CACHE["plan"]
+
+
+def rank_program(g, core, T, topo):
+    rank = T.rank_of(core)
+    if rank is None:
+        return
+    me, dst = T.cores[rank], T.cores[(rank + STEP) % len(T.cores)]
+    ops, deps, order, span = plan(len(topo.engines(me, dst)))
+    eng = {"v": g.vector, "a": g.scalar, "p": g.tensor, "g": g, "s": g.sync}
+    at, count, seen = {}, {}, {}
+    for i in order:
+        o = ops[i]
+        q = o["q"]
+        sem = o["sem"] or QSEM.get(q, "sg")
+        count[sem] = count.get(sem, 0) + o["val"]
+        at[i] = (sem, count[sem])
+        if q == "net":
+            continue
+        need = {}
+        for k in deps[i]:
+            s, v = at[k]
+            if s == "ls" or (q == "p" and ops[k]["q"] == "p"):
+                continue
+            need[s] = max(need.get(s, 0), v)
+        for s in sorted(need):
+            if seen.get((q, s), 0) < need[s]:
+                eng[q].wait_ge(T.sem[s], need[s])
+                seen[(q, s)] = need[s]
+        if o["sem"] == "ls":
+            o["fn"](g, T, me, dst, topo)
+        else:
+            o["fn"](g, T).then_inc(T.sem[sem], 1 if o["sem"] is None else 16)
+    for s in sorted(count):
+        g.sync.wait_ge(T.sem[s], count[s])

@@ -3,35 +3,31 @@ from concourse.mybir import AluOpType, AxisListType, ActivationFunctionType
 OP = AluOpType
 AF = ActivationFunctionType
 L, NR, NC, VIS, STEP = 192, 3072, 2048, 3, 3
-RW, CW = NR + L, NC + L
-POOLS = {"F": 19000, "I": 2900, "U": 1600, "B": 33000, "H": 10200}
+DU = L
+RW, CW = DU + NR + VIS * L, DU + NC
+SO = 1664.0
+POOLS = {"F": 14000, "I": 2400, "U": 2000, "B": 30000, "H": 7000}
 DTN = {"F": "float32", "I": "int32", "U": "uint16", "B": "bfloat16", "H": "float16"}
 SCRATCH = {
     "rec_t": ("sbuf", [128, RW], "bfloat16"), "cel_t": ("sbuf", [128, CW], "float32"), "po_t": ("sbuf", [128, RW], "float32"),
-    "cel_i": ("sbuf", [128, NC], "int32"), "pod": ("dram", [8, NR], "float32"),
-    "zrep": ("sbuf", [128, 16 * L], "bfloat16"),
+    "cel_i": ("sbuf", [128, NC], "int32"), "zrep": ("sbuf", [128, 16 * L], "bfloat16"), "pair": ("sbuf", [128, 12, 128], "bfloat16"),
+    "zend": ("sbuf", [128, L], "bfloat16"), "pend": ("sbuf", [128, L], "float32"),
+    "pl1": ("sbuf", [128, 12], "int32"), "pl2": ("sbuf", [128, 12], "int32"),
 }
 for _k in POOLS:
     SCRATCH["pool" + _k] = ("sbuf", [128, POOLS[_k]], DTN[_k])
-for _t in range(1, VIS + 1):
-    SCRATCH["zl%d" % _t] = ("sbuf", [128, L], "bfloat16")
-    SCRATCH["pl%d" % _t] = ("sbuf", [128, 12 if _t < VIS else L], "float32")
 BANKS = ["b0", "b1", "b2", "b3", "b4", "b5", "e0", "e1"]
 for _b in BANKS:
     SCRATCH[_b] = ("psum", [128, 512], "float32")
-SITE = {"dA": "b0", "kP": "b0", "hP": "b0", "tP": "b1", "zP": "b1", "vf": "b1", "ne": "b1", "de": "b2", "lP": "b2", "u": "b2", "s2": "b2",
-        "near": "b3", "dB": "b3", "acc": "b3", "xv": "b3", "fv": "b3", "nv": "b3", "s1": "b4", "nc": "b4", "xe": "b4", "fe": "b4", "aP": "b4",
-        "far": "b5", "xc": "b5", "fc": "b5", "win": "e0", "m1": "e0", "D1": "e0", "m2": "e1", "D2": "e1"}
+SITE = {"dA": ("b0", 0), "K": ("b0", 128), "cn": ("b1", 0), "dB": ("b1", 384), "u": ("b1", 448), "aP": ("b1", 464), "pos": ("b1", 480),
+        "de": ("b2", 0), "lP": ("b2", 192), "sc": ("b2", 384), "q": ("b2", 416), "fp": ("b3", 0), "zP": ("b3", 192), "best": ("b3", 384),
+        "ev": ("b4", 0), "t2": ("b5", 0), "t3": ("b5", 192), "m1": ("e0", 0), "D1": ("e0", 192), "m2": ("e1", 0), "D2": ("e1", 192)}
 SEMAPHORES = ["sv", "sa", "sp", "sg", "ls"] + ["d%d" % i for i in range(20)] + ["rz%d" % t for t in (1, 2, 3)] + ["rp%d" % t for t in (1, 2, 3)]
-NS = 0.83 * 1.15e-3
-MAGIC = 12582912.0
-BIAS = {"ent11": 205, "early1": -530, "far1": 307, "ent12": 315, "far2": 112, "newz0": 492, "cg11": 736, "phL2": 73, "acc2": 31, "ent10": -55,
-        "cg02": 227, "cg22": 638, "load": 630, "cg12": 434, "near2": -74, "eg12": 8, "ecell2": -5, "acc0": 73, "n0": -120, "ecell0": -376,
-        "E21": 125, "n1": -151, "cg01": 238, "n2": -497, "lists2": 251, "ecell1": 3, "E20": -2, "zrep2": -222, "E31": 317, "early2": -60,
-        "E30": 339, "cell2": 160, "cg10": 75, "eg01": 183, "eg02": 110, "newz2": -221, "eg21": 107, "ent20": 1, "phL0": -531, "slots0": 348,
-        "newz1": 132, "zrep0": 67, "acc1": 106, "eg22": 159, "eg11": 20, "far0": 892, "cg20": -1, "cg21": 220, "phL1": -162, "ent21": -1,
-        "slots2": 5, "near1": 242, "E32": -62, "E10": 112, "cg00": 605, "ent22": -73, "slots1": 218, "eg10": 5, "zrep1": -73, "cell0": 4,
-        "lists0": -9, "lists1": -3, "near0": 2, "cell1": -1}
+NS, NP = 0.92e-3, 0.5e-3
+M4, M32 = 50331648.0, 402653184.0
+ZG, ZV = 6, 0
+GW = 512
+BIAS = {}
 CACHE = {}
 
 
@@ -46,33 +42,31 @@ def build(ne):
         return ("pool" + k, o, w)
 
     def r(t, c0=0, c1=None, st=1, p0=0, p1=128):
+        if t[0] == "R":
+            return ("R", t[1], t[2] + c0 * t[4], t[3] if c1 is None else t[2] + c1 * t[4], st * t[4], p0, p1)
         return ("R", t[0], t[1] + c0, t[1] + (t[2] if c1 is None else c1), st, p0, p1)
 
     def ref(x):
-        return x if isinstance(x, (int, float)) or x is None or x[0] in ("R", "X") else r(x)
+        return x if isinstance(x, (int, float)) or x is None or x[0] in ("R", "X", "Z") else r(x)
 
     def ind(win, off):
         return ("X", ref(win), ref(off))
 
-    ptop, sites = {b: 0 for b in BANKS}, {}
-
     def place(site, w):
-        if site not in sites:
-            b = SITE[site]
-            sites[site] = (b, ptop[b], w)
-            ptop[b] += w
-            if ptop[b] > 512:
-                raise ValueError("bank %s is full" % b)
-        return sites[site]
+        return (SITE[site][0], SITE[site][1], w)
 
     def spans(x):
         if x is None or isinstance(x, (int, float)):
             return []
         if x[0] == "X":
             return spans(x[1]) + spans(x[2])
-        return [(x[1], x[2], x[3])]
+        if x[0] == "Z":
+            return [("pair", 128 * b + x[3], 128 * b + x[4], 1) for b in range(x[1], x[2])]
+        return [(x[1], x[2], x[3], x[4])]
 
     def ncol(x):
+        if x[0] == "Z":
+            return (x[2] - x[1]) * (x[4] - x[3])
         return 16 * ncol(x[2]) if x[0] == "X" else (x[3] - x[2] + x[4] - 1) // x[4]
 
     def ap(T, x):
@@ -80,6 +74,8 @@ def build(ne):
             return x
         if x[0] == "X":
             return ap(T, x[1]).indirect(ap(T, x[2]))
+        if x[0] == "Z":
+            return T.pair[x[5]:x[6], x[1], :] if x[2] == x[1] + 1 else T.pair[x[5]:x[6], x[1]:x[2], x[3]:x[4]]
         t = T[x[1]]
         return t[x[5]:x[6], x[2]:x[3]] if x[4] == 1 else t[x[5]:x[6], x[2]:x[3]:x[4]]
 
@@ -93,13 +89,14 @@ def build(ne):
     def vcost(o, ins, rate):
         n = ncol(o)
         if o[0] == "X":
-            return 0.06 + n * 3.5 * NS
+            return 0.05 + n * 3.5 * NS
         if any(x[0] == "X" for x in ins):
-            return 0.06 + n * 1.55 * NS
-        return 0.02 + max(64, n * rate) * NS
+            return 0.05 + n * 1.55 * NS
+        return 0.025 + max(64, n * rate) * NS
 
     def vop(fn, outs, ins, cost):
-        add("v", fn, [s for x in ins for s in spans(x)], [s for x in outs for s in spans(x)], cost)
+        add("v", fn, [s for x in ins for s in spans(x)] + [s for x in outs if x[0] == "X" for s in spans(x[2])],
+            [s for x in outs for s in spans(x[1] if x[0] == "X" else x)], cost)
 
     def vt(o, a, b, op):
         o, a, b = ref(o), ref(a), ref(b)
@@ -116,6 +113,10 @@ def build(ne):
         o, a = ref(o), ref(a)
         vop(lambda g, T: g.vector.tensor_copy(out=ap(T, o), in_=ap(T, a)), [o], [a], vcost(o, [a], 0.5 if two(o) and two(a) else 1))
 
+    def vm(o, v):
+        o = ref(o)
+        vop(lambda g, T: g.vector.memset(ap(T, o), v), [o], [], vcost(o, [], 0.5 if two(o) else 1))
+
     def vscan(o, d0, d1, init, o0, o1):
         o, d0, d1 = ref(o), ref(d0), ref(d1)
         vop(lambda g, T: g.vector.tensor_tensor_scan(out=ap(T, o), data0=ap(T, d0), data1=ap(T, d1), initial=init, op0=o0, op1=o1), [o], [d0, d1], vcost(o, [d0], 1))
@@ -124,15 +125,22 @@ def build(ne):
         o, a = ref(o), ref(a)
         vop(lambda g, T: g.vector.transpose(out=ap(T, o), in_=ap(T, a)), [o], [a], vcost(o, [a], 1))
 
-    def vred(o, a):
-        o, a = ref(o), ref(a)
-        vop(lambda g, T: g.vector.tensor_reduce(out=ap(T, o), in_=ap(T, a), axis=AxisListType.X, op=OP.add), [o], [a], vcost(a, [a], 1))
+    def act(o, a, f=AF.Identity, scale=1.0, bias=0.0, acc=None):
+        o, a, scale, bias, acc = ref(o), ref(a), ref(scale), ref(bias), ref(acc)
+        x, ex = a[0] == "X", lambda T: {} if acc is None else {"accum_out": ap(T, acc)}
+        add("a", lambda g, T: g.scalar.activation(out=ap(T, o), in_=ap(T, a), func=f, bias=ap(T, bias), scale=ap(T, scale), **ex(T)),
+            [s for y in (a, scale, bias) for s in spans(y)], spans(o) + spans(acc),
+            (0.065 + ncol(o) * 1.55 * NS if x else 0.03 + max(64, ncol(o)) * NS) + (0.02 if acc else 0.0))
 
-    def act(o, a, f, scale=1.0, bias=0.0):
-        o, a, scale, bias = ref(o), ref(a), ref(scale), ref(bias)
-        x = a[0] == "X"
-        add("a", lambda g, T: g.scalar.activation(out=ap(T, o), in_=ap(T, a), func=f, bias=ap(T, bias), scale=ap(T, scale)),
-            [s for y in (a, scale, bias) for s in spans(y)], spans(o), (0.07 if x else 0.03) + max(64, ncol(o) * (1.55 if x else 1)) * NS)
+    def aff(q, o, a, scale=1.0, bias=0.0):
+        if q == "a":
+            act(o, a, AF.Identity, scale, bias)
+        elif scale == 1.0 and bias == 0.0:
+            vc(o, a)
+        elif scale == 1.0:
+            vs(o, a, bias, None, OP.add)
+        else:
+            vs(o, a, scale, bias, OP.mult, OP.add)
 
     def mm(ms):
         ms = [(ref(o), ref(a), ref(b), s, e) for o, a, b, s, e in ms]
@@ -143,442 +151,390 @@ def build(ne):
                 k = g.tensor.matmul(ap(T, o), ap(T, a), ap(T, b), s, e)
             return k
         rd = sorted(set(s for o, a, b, x, e in ms for y in (a, b) for s in spans(y)))
-        add("p", fn, rd, sorted(set(s for m in ms for s in spans(m[0]))), sum(max(64, ncol(m[2])) for m in ms) * NS + 0.03)
+        add("p", fn, rd, sorted(set(s for m in ms for s in spans(m[0]))), sum(max(min(64, ncol(m[1])), ncol(m[2])) * NP + 0.012 for m in ms) + 0.05)
+
+    def msum(o, terms):
+        mm([(o, a, b, i == 0, i == len(terms) - 1) for i, (a, b) in enumerate(terms)])
 
     def iota(o, pat, base, cm):
         o = ref(o)
-        add("g", lambda g, T: g.iota(ap(T, o), pat, base, cm, allow_small_or_imprecise_dtypes=True), [], spans(o), 0.13 + 2 * ncol(o) * NS)
+        ex = {} if o[1] == "poolI" else {"allow_small_or_imprecise_dtypes": True}
+        add("g", lambda g, T: g.iota(ap(T, o), pat, base, cm, **ex), [], spans(o), 0.13 + 2 * ncol(o) * NS)
 
     def sel(o, a, pat, base, cm, fill, cmp_):
         o, a = ref(o), ref(a)
         add("g", lambda g, T: g.affine_select(ap(T, o), ap(T, a), pat, cmp_, fill, base, cm), spans(a), spans(o), 0.17 + 2 * ncol(o) * NS)
 
-    def dma(fn, reads, writes, cost, n=1):
-        add("s", fn, reads, writes, cost, "d%d" % ndma[0], 16 * n)
+    def gcopy(o, a):
+        sel(o, a, [[0, ncol(ref(o))]], 1, 0, 0.0, OP.is_gt)
+
+    def dma(fn, reads, writes, cost):
+        add("s", fn, reads, writes, cost, "d%d" % ndma[0], 16)
         ndma[0] += 1
 
-    z, wI, thI, phI, poI = new("B", L), new("I", 1), new("I", 3), new("I", L), new("I", L)
+    zin = [("rec_t", DU + NR + L * t, L) for t in range(VIS)] + [("zend", 0, L)]
+    z, wI, thI, phI, poI = zin[0], new("I", 1), new("I", 3), new("I", L), new("I", L)
 
     def load(name, o, cost):
         o = ref(o)
         dma(lambda g, T: g.sync.dma_start(out=ap(T, o), in_=T[name][:]), [], spans(o), cost)
-    load("phi", r(phI, p1=8), 2.2)
-    load("pat", z, 2.2)
-    load("wt", wI, 2.2)
-    load("th", r(thI, p1=8), 2.2)
-    for h in (0, 1):
-        cs = ("cel_i", 1024 * h, 1024)
-        dma(lambda g, T, h=h: g.sync.dma_start(out=T.cel_i[:, 1024 * h:1024 * h + 1024], in_=T.cel[:, 1024 * h:1024 * h + 1024]), [], spans(ref(cs)), 4.0 + 2 * h)
-    dma(lambda g, T: g.sync.dma_start(out=T.rec_t[:, 0:NR], in_=T.rec[:]), [], [("rec_t", 0, NR)], 8.5)
-    load("po", poI, 9.0)
+    load("wt", wI, 1.6)
+    load("pat", z, 1.7)
+    load("phi", r(phI, p1=8), 1.7)
+    load("cel", ("cel_i", 0, NC), 5.0)
+    load("th", r(thI, p1=8), 2.0)
+    load("rec", ("rec_t", DU, NR), 7.5)
+    load("po", poI, 7.5)
 
     cur[0] = "const"
 
-    def col(a, scale=1.0, bias=0.0, f=AF.Identity, k="F"):
-        o = new(k, ref(a)[3] - ref(a)[2])
-        act(o, a, f, scale, bias)
+    def col(a, scale=1.0, bias=0.0, k="F"):
+        o = new(k, ncol(ref(a)))
+        act(o, a, AF.Identity, scale, bias)
         return o
 
-    def same(a, neg, k="F"):
-        return col(col(a, 1.0, neg, AF.Abs), -1.0, 1.0, AF.Relu, k)
-
-    def tile(a, scale, bias=0.0):
-        return col(a, scale, bias, AF.Identity, "B")
-    p2, pF, yg, i15, b12, j6, xF, iF = new("F", 1), new("F", 1), new("F", 128), new("F", L), new("F", 12), new("F", 6), new("F", 144), new("F", L)
-    p4, i12 = new("F", 1), new("F", 96)
-    iota(p2, [[0, 1]], -15, 2)
-    iota(pF, [[0, 1]], 0, 1)
+    def vcol(a, s1, s2, op0, op1=None, k="F"):
+        o = new(k, ncol(ref(a)))
+        vs(o, a, s1, s2, op0, op1)
+        return o
+    EQ, NE, GT = OP.is_equal, OP.not_equal, OP.is_gt
+    pI, pk, xF, yg, i15, i8, lnT = new("I", 3), new("F", 3), new("F", L), new("F", 128), new("F", 2 * L), new("F", 96), new("F", 12)
+    iota(r(pI, 0, 1), [[0, 1]], 0, 1)
+    iota(xF, [[1, L]], 0, 0)
     iota(yg, [[1, 8], [0, 16]], 0, 0)
-    iota(i15, [[0, 12], [1, 16]], 0, 0)
-    iota(xF, [[1, 144]], -15, 0)
-    iota(b12, [[1, 12]], 0, 0)
-    iota(p4, [[0, 1]], -31, 2)
-    iota(j6, [[32, 6]], -11, 2)
-    iota(i12, [[0, 8], [1, 12]], 0, 0)
-    iota(iF, [[1, L]], 0, 0)
-    gc = col(col(p2, 1.0 / 32, MAGIC), 1.0, -MAGIC)
-    kc = col(gc, -16.0, pF)
-    ng, npg = col(gc, -1.0), col(gc, -16.0)
-    M0, diag = col(i15, 1.0, 0.0, AF.Sign), new("F", L)
-    vs(diag, i15, kc, None, OP.is_equal)
-    U, wc = same(xF, npg, "B"), new("F", 1)
-    vc(wc, wI)
-    UW = tile(U, wc)
-    sel8, ph16, th16, thc = new("H", 128), new("H", L), new("H", 3), new("F", 3)
-    vs(r(sel8, p1=8), r(yg, p1=8), r(pF, p1=8), None, OP.is_equal)
-    vs(r(ph16, p1=8), r(phI, p1=8), -2048.0, None, OP.add)
-    vs(r(th16, p1=8), r(thI, p1=8), 0.0, None, OP.add)
-    xq = place("xc", L)
-    mm([(xq, r(sel8, p1=8), r(ph16, p1=8), True, True)])
-    pm, ps, phi = new("F", L), new("F", L), new("F", 12)
-    vt(pm, xq, diag, OP.mult)
-    vscan(ps, M0, pm, 0.0, OP.mult, OP.add)
-    act(phi, r(ps, 15, L, 16), AF.Identity, 1.0, 2048.0)
-    tp = r(place("u", 12), 0, 3)
-    mm([(tp, r(sel8, p1=8), r(th16, p1=8), True, True)])
-    act(thc, tp, AF.Copy)
-    for x in (0, 1):
-        vc(("cel_t", 1024 * x, 1024), ("cel_i", 1024 * x, 1024))
-    BO = same(yg, ng, "B")
-    lane, bl = col(b12, 16.0, kc), new("U", 12)
-    i16A, dumR, dumC, dumS = col(lane, 16.0), col(lane, 1.0, float(NR)), col(lane, 1.0, float(NC)), col(lane, 1.0, NR - 1536.0)
-    dumRC = new("F", 24)
-    act(r(dumRC, 0, 12), dumR, AF.Copy)
-    act(r(dumRC, 12, 24), dumC, AF.Copy)
-    vc(bl, b12)
-    bo8 = new("B", 8)
-    act(bo8, r(BO, 0, 128, 16), AF.Copy)
-    m3, m1, one = tile(bo8, -3.0), tile(bo8, -1.0), tile(BO, 0.0, 1.0)
-    RS = col(M0, 2.0e9, -1.0e9)
-    DW, mb1, mb2, list2 = new("B", 240), new("F", 96), new("F", 96), new("U", 6)
-    act(r(DW, 0, 192), M0, AF.Identity, 0.0)
-    act(r(DW, 192, 240), r(M0, 0, 48), AF.Identity, 0.0)
-    act(r(DW, 112, 128), r(diag, 0, 16), AF.Copy)
-    vs(mb1, i12, 8.0, -4.0, OP.is_ge, OP.mult)
-    vt(mb2, mb1, i12, OP.add)
-    MSK = same(mb2, ng)
-    t1 = col(j6, 1.0, col(npg, 2.0))
-    y1, y2, js = col(col(t1, 1.0 / 24, MAGIC), 1.0, -MAGIC), col(col(col(t1, 1.0, 8.0), 1.0 / 24, MAGIC), 1.0, -MAGIC), new("F", 6)
-    vt(js, y1, y2, OP.add)
-    vc(list2, js)
-    oc = col(col(col(p4, 1.0 / 64, MAGIC), 1.0, -MAGIC), -2.0, gc)
+    vs(r(pI, 1, 2), r(pI, 0, 1), 4, None, OP.arith_shift_right)
+    vs(r(pI, 2, 3), r(pI, 0, 1), 15, None, OP.bitwise_and)
+    vc(pk, pI)
+    pc, gc, kc = r(pk, 0, 1), r(pk, 1, 2), r(pk, 2, 3)
+    one, S8, ph16, th16, wc = new("B", L), new("H", 144), new("H", L), new("H", 3), col(wI)
+    c15 = col(gc, 16.0, 15.0)
+    x128, x144 = r(xF, 0, 128), r(xF, 0, 144)
+    UW = vcol(x144, c15, wc, EQ, OP.mult, "B")
+    vs(r(S8, p1=8), r(xF, 0, 144, p1=8), r(col(pc, 16.0, 15.0), p1=8), None, EQ)
+    act(r(ph16, p1=8), r(phI, p1=8), AF.Identity, 1.0, -2048.0)
+    phi, pq = new("I", 12), place("pos", 12)
+    msum(pq, [(r(S8, 15 - k, 143 - k, p1=8), r(ph16, k, L, 16, p1=8)) for k in range(16)])
+    act(phi, pq, AF.Identity, 1.0, 2048.0)
+    U = vcol(x144, c15, None, EQ, None, "B")
+    vm(one, 1.0)
+    diag, BO = vcol(r(xF, 0, 16), kc, None, EQ), vcol(yg, gc, None, EQ, None, "B")
+    kk = lambda j: r(diag, j, j + 1)
+    Sel, SelI = new("B", 2048), new("B", 2048)
+    for m in range(16):
+        aff("av"[m & 1], r(Sel, 128 * m, 128 * m + 128), BO, kk(m), 0.0)
+    I16 = vcol(x128, pc, None, EQ, None, "B")
+    nI, hI, I64, nI64, sI, cI, kI = [vcol(I16, v, None, OP.mult, None, "B") for v in (-1.0, 0.5, 64.0, -64.0, 2.0 ** -10, -16320.0, -16512.0)]
+    lane = col(r(xF, 0, 12), 16.0, kc)
+    cnH, cnD, ln24 = new("F", 24), new("F", 24), new("F", 24)
+    act(r(cnH, 0, 12), lane, AF.Identity, 0.0)
+    act(r(cnH, 12, 24), lane, AF.Identity, 16.0, -SO)
+    act(r(cnD, 0, 12), lane, AF.Identity, -1.0, float(DU))
+    act(r(cnD, 12, 24), lane, AF.Identity, 15.0, float(DU))
+    act(r(ln24, 0, 12), lane)
+    act(r(ln24, 12, 24), lane)
+    iota(i15, [[0, 24], [1, 16]], 0, 0)
+    iota(i8, [[0, 12], [1, 8]], 0, 0)
+    iota(lnT, [[32, 6], [0, 2]], 0, 0)
+    sel8, selS, thc = new("H", 128), new("H", 256), new("F", 3)
+    vs(r(sel8, p1=8), r(yg, p1=8), r(pc, p1=8), None, EQ)
+    for s in (0, 1):
+        sel(r(selS, 128 * s, 128 * s + 128, p1=8), r(one, 0, 128, p1=8), [[-2, 4], [0, 32]], -s, 1, 0.0, EQ)
+    act(r(th16, p1=8), r(thI, p1=8))
+    tp = place("aP", 9)
+    mm([(r(tp, 0, 3), r(sel8, p1=8), r(th16, p1=8), True, True)] +
+       [(r(tp, 3 + 3 * s, 6 + 3 * s), r(selS, 128 * s, 128 * s + 128, p1=8), r(th16, p1=8), True, True) for s in (0, 1)])
+    act(thc, r(tp, 0, 3))
+    tcol = col(r(tp, 3, 9), 64.0, col(kc, 2.0 ** -10, -16320.0 - 1680.0 / 1024))
+    gI = new("I", 1)
+    vs(gI, r(pI, 1, 2), 1, None, OP.bitwise_and)
+    oc = col(gI)
     ec = col(oc, -1.0, 1.0)
-    klt = col(col(kc, -1.0, 11.5, AF.Sign), 1.0, 0.0, AF.Relu)
-    k0, k10, k11, k12, k13 = [same(kc, -float(v)) for v in (0, 10, 11, 12, 13)]
-    hf, pw, pw2, d16, d17, sc0, sc2 = new("F", 48), new("F", 16), new("F", 16), new("F", 16), new("F", 16), new("F", 1), new("F", 1)
-    for x, v in ((0, 0.5), (16, 0.0), (32, 2.0)):
-        act(r(hf, x, x + 16), r(M0, 0, 16), AF.Identity, 0.0, v)
-    vscan(pw, r(hf, 0, 16), r(hf, 16, 32), 2.0, OP.mult, OP.add)
-    vscan(pw2, r(hf, 32, 48), r(hf, 16, 32), 0.5, OP.mult, OP.add)
-    vt(d16, pw, r(diag, 0, 16), OP.mult)
-    vt(d17, pw2, r(diag, 0, 16), OP.mult)
-    vred(sc0, d16)
-    vred(sc2, d17)
-    scol = col(sc0, klt)
-    fs, gs = col(k13, -1.0 / 512, klt), col(k12, 1.0 / 512, klt)
-    fse, fso = col(fs, ec), col(fs, oc)
-    kv = col(col(kc, 1.0, 0.0, AF.Sign), klt)
-    fb0 = col(k10, 2.0, col(klt, -0.5))
-    fb, gb = col(fb0, 1.0, k12), col(fb0, 1.0, k13)
-    fbe, fbo = col(fb, ec), col(fb, oc)
-    C2, c2c, bM = new("H", L), col(col(sc2, -0.5, 0.5), klt), col(k11, 1.0, MAGIC)
-    vs(C2, M0, 0.0, c2c, OP.mult, OP.add)
-    b11 = col(col(scol, 0.5, col(klt, -0.5)), 1.0, col(kv, 1025.0))
-    f11 = col(k11, -2050.0, col(k0, 1025.0, col(klt, 1024.5)))
-    fb2, gb2 = col(f11, 1.0, k12), col(f11, 1.0, k13)
-    fbe2, fbo2 = col(fb2, ec), col(fb2, oc)
-    Y, GT, EQ, NE = [[1, 128]], OP.is_gt, OP.is_equal, OP.not_equal
-    I16, LA, L16, nBO, TA, TL, TB, TH = [new("B", 128) for i in range(8)]
-    KV = tile(one, col(kv, -2.0))
-    act(nBO, BO, AF.Identity, -1.0)
-    sel(I16, one, Y, 0, -1, 0.0, EQ)
-    sel(LA, KV, Y, 1, -1, 0.0, EQ)
-    sel(L16, LA, Y, 0, -1, 1.0, NE)
-    sel(TA, nBO, Y, 0, -1, 0.0, GT)
-    sel(TL, TA, Y, 0, -1, 1.0, NE)
+    hv, pw = vcol(r(xF, 0, 16), kc, 0.5, OP.is_ge, OP.max), new("F", 16)
+    vscan(pw, hv, hv, 1.0, OP.mult, OP.min)
+    sc0 = r(pw, 15, 16)
+    klt = vcol(kc, 11.5, None, OP.is_lt)
+    kv, scol = vcol(kc, 0.5, klt, GT, OP.mult), col(sc0, klt)
+    b11 = col(col(sc0, 0.5, 1024.5), kv)
+    f11, fsb = col(kk(11), -2050.0, col(kk(0), 1025.0, col(klt, 1024.5))), new("F", 2)
+    act(r(fsb, 0, 1), kk(13), AF.Identity, -1.0 / 512, klt)
+    act(r(fsb, 1, 2), f11, AF.Identity, 1.0, kk(12))
+    fe, fo, gs, gb = col(fsb, ec), col(fsb, oc), col(kk(12), 1.0 / 512, klt), col(f11, 1.0, kk(13))
+    L16, LA, laneC = new("B", 128), vcol(x128, col(pc, 1.0, -1.0), col(kv, -2.0), EQ, OP.mult, "B"), col(xF, col(kk(12), 1.0, kk(13)), 0.0, "B")
+    vt(L16, LA, I16, OP.add)
+    bo8, half = vcol(r(i8, 0, 16), gc, None, EQ, None, "B"), new("F", 24)
+    for x, v in ((0, 0.0), (8, 1.0), (16, -1.0)):
+        act(r(half, x, x + 8), r(xF, 0, 8), AF.Relu, 0.0, col(pc, 1.0e6 * v, -63.5e6 * v))
+    bo3, nOne, nBO = col(bo8, 3.0, 0.0, "B"), col(r(one, 0, 128), -1.0, 0.0, "B"), vcol(BO, -1.0, None, OP.mult, None, "B")
+    cmpc, M8 = vcol(i8, gc, 0.5, EQ, OP.max), vcol(i8, 0.5, None, GT)
+    cK = col(one, col(kc, -4.0, -4.0), 0.0, "B")
+    RS, D2 = new("F", 2 * L), vcol(r(i15, 0, L), 0.5, 2.0, GT, OP.mult)
+    vs(RS, vcol(i15, 0.5, -0.5, GT, OP.add), 2.0e9, None, OP.mult)
+    e10, o10 = col(ec, 1024.0), col(oc, 1024.0)
+    P = [[vcol(x128, pc, e10, EQ, OP.mult, "B"), vcol(x128, col(pc, 1.0, 16.0), e10, EQ, OP.mult, "B")],
+         [vcol(x128, col(pc, 1.0, -16.0), o10, EQ, OP.mult, "B"), vcol(x128, pc, o10, EQ, OP.mult, "B")]]
+    U1 = vcol(x144, c15, kk(0), EQ, OP.mult, "B")
+    p32 = col(oc, 16.0 / 1024, col(kc, 1.0 / 1024))
+    TK, TC = [new("F", 24) for t in range(VIS)], [None, new("F", 12), new("F", 12)]
+    for t in range(VIS):
+        act(r(TK[t], 0, 12), lnT, AF.Identity, 1.0 / 1024, col(p32, 1.0, -16324.0 + (NR + L * t - SO) / 1024))
+        for s in (0, 1):
+            act(r(TC[t], s, 12, 2) if t else r(TK[0], 12 + s, 24, 2), r(xF, 0, 6), AF.Identity, 0.0, r(tcol, 3 * s + t, 3 * s + t + 1))
+    PD0, PD1 = new("F", 72), new("F", 72)
+    vm(PD0, 1.0)
+    vm(r(PD0, 0, 72, 6), 0.0)
+    vm(r(PD0, 2, 72, 6), -1.0)
+    BI, dm1 = new("B", 128), col(diag, 1.0, -1.0)
+    vt(BI, vcol(I16, -2.0, None, OP.mult, None, "B"), BO, OP.add)
+    for m in range(16):
+        vs(r(SelI, 128 * m, 128 * m + 128), BI, r(dm1, m, m + 1), kk(m), OP.max, OP.min)
+    TA, TL, TB, TH = [new("B", 128) for i in range(4)]
+    sel(TA, nBO, [[1, 128]], 0, -1, 0.0, GT)
+    sel(TL, TA, [[1, 128]], 0, -1, 1.0, NE)
     sel(TB, nBO, [[-1, 128]], 0, 1, 0.0, GT)
-    sel(TH, TB, Y, 0, -1, 1.0, NE)
-    nI, hI16, kI16 = [tile(I16, v) for v in (-1.0, 0.5, -1024.0)]
-    laneC, c64 = tile(iF, col(k12, 1.0, k13)), tile(M0, 0.0, 64.0)
-    pas, acc, cand, winB, vfB = [new("B", 16) for i in range(5)]
-    P = [[tile(I16, ec), new("B", 128)], [new("B", 128), tile(I16, oc)]]
-    sel(P[0][1], tile(one, ec), Y, -16, -1, 0.0, EQ)
-    sel(P[1][0], tile(one, oc), Y, 16, -1, 0.0, EQ)
-    knear = col(kc, -1.0 / 16, 255.0 + 15.0 / 16)
-    act(("rec_t", NR, L), M0, AF.Identity, 0.0, 64.0)
-    act(("po_t", NR, L), M0, AF.Identity, 0.0)
-    poF = new("F", L)
-    vc(poF, poI)
-    dma(lambda g, T: g.sync.dma_start(out=T.pod[:], in_=ap(T, r(poF))), spans(r(poF)), [("pod", 0, 1)], 2.2)
-    fan_id = ndma[0]
-
-    def fan(g, T):
-        k = None
-        for i in range(16):
-            k = g.sync.dma_start(out=T.po_t[i::16, 0:NR], in_=T.pod[:])
-            if i < 15:
-                k.then_inc(T.sem["d%d" % fan_id], 16)
-        return k
-    dma(fan, [("pod", 0, 1)], [("po_t", 0, NR)], 7.0, 16)
-    h = new("F", 1)
-    vc(h, r(thc, 0, 1))
-    celw, celn, recw, recn, pow_ = ("cel_t", 0, CW), ("cel_t", 0, NC), ("rec_t", 0, RW), ("rec_t", 0, NR), ("po_t", 0, RW)
-    Es = [new("B", 2048) for x in range(3)]
+    sel(TH, TB, [[1, 128]], 0, -1, 1.0, NE)
+    kb1, kb2, pw15, vdb, edb = col(kc, 0.5, 0.5), col(kc, -0.5, 8.0), col(sc0, 32768.0), col(kc, -1.0, SO + DU), col(kc, -1.0, float(DU))
+    c64 = col(r(one, 0, 16), 64.0, 0.0, "B")
+    cur[0] = "po"
+    iota(("po_t", 0, RW), [[0, RW]], 0, 0)
+    poF = col(poI)
+    dma(lambda g, T: g.sync.dma_start(out=T.po_t[::16, DU:DU + NR], in_=ap(T, r(poF))), spans(r(poF)), [("po_t", DU, DU + NR, 1)], 1.8)
+    cur[0] = "celf"
+    for x in (0, 1):
+        gcopy(("cel_t", DU + 1024 * x, 1024), ("cel_i", 1024 * x, 1024))
+    h = r(thc, 0, 1)
+    celw, celn, recw, recn, pow_ = ("cel_t", 0, CW), ("cel_t", DU, NC), ("rec_t", 0, DU + NR), ("rec_t", DU, NR), ("po_t", 0, DU + NR)
     dfad = [(new("B", 1024), new("B", 1024)) for x in range(6)]
 
-    def expand(src):
-        X = new("H", L)
-        vt(X, ind(src, bl), diag, OP.mult)
-        return X
-
-    def pairs(val, E, site):
-        X, Vh, b = expand(val), new("H", L), site != "v"
-        xP, fp = place("x" + site, L), place("f" + site, L)
-        if b:
-            mm([(xP, BO, X, True, True)])
-            vs(Vh, xP, scol, b11, OP.mult, OP.add)
-        else:
-            Vi = new("F", L)
-            mm([(xP, BO, X, True, False), (xP, I16, C2, False, True)])
-            act(Vi, xP, AF.Identity, scol, bM)
-            vs(Vh, Vi, -MAGIC, None, OP.add)
-        mm([(fp, L16, Vh, True, False), (fp, I16, laneC, False, True)])
-        G, Fe, Fo = new("B", L), new("B", L), new("B", L)
-        act(Fe, fp, AF.Identity, fse, fbe2 if b else fbe)
-        act(G, fp, AF.Identity, gs, gb2 if b else gb)
-        act(Fo, fp, AF.Identity, fso, fbo2 if b else fbo)
-        for a in range(4):
-            bank, ms = ("e1", "e0")[a & 1], []
-            for x, F in ((0, Fe), (1, Fo)):
-                pp = {"p0": 32 * a, "p1": 32 * a + 32}
-                ms.append(((bank, 256 * x, L), r(F, 0, 128, **pp), r(G, **pp), True, True))
-                ms.append(((bank, 256 * x + L, 64), r(F, 64, L, **pp), r(G, 128, L, **pp), True, True))
-            mm(ms)
-            act(r(E, 512 * a, 512 * a + 512), (bank, 0, 512), AF.Relu, 512.0, -1536.0)
-        return E
-
-    def lowest(vec, E, site, out):
-        q, ms = place("n" + site, 16), []
-        for g in range(8):
-            h0, h1 = r(vec, 2 * g, 2 * g + 1), r(vec, 2 * g + 1, 2 * g + 2, p0=64)
-            ms.append((r(q, 2 * g, 2 * g + 1), r(E, 256 * g, 256 * g + 128), h0, True, True))
-            ms.append((r(q, 2 * g + 1, 2 * g + 2), r(E, 256 * g + 64, 256 * g + L), h0, True, False))
-            ms.append((r(q, 2 * g + 1, 2 * g + 2), r(E, 256 * g + 128, 256 * g + 256, p0=64), h1, False, True))
-        mm(ms)
-        vt(out, vec, q, OP.is_gt)
-        return out
-
-    def score(terms, site, extra=None):
-        for q, a, b in ((r(place(site, 16), 0, 16, 2), 0, 128), (r(place(site, 16), 1, 16, 2), 64, L)):
-            ms = [(q, r(x, a, b), y) for x, y in terms]
-            if extra:
-                ms.append((q, extra[0], extra[1]))
-            mm([m + (i == 0, i == len(ms) - 1) for i, m in enumerate(ms)])
-
-    def to_a(vec, site):
-        X = new("B", 96)
-        vt(X, ind(vec, list2), MSK, OP.mult)
-        q = place(site, 12)
-        mm([(q, r(DW, 112 - 16 * g, 240 - 16 * g), r(X, 12 * g, 12 * g + 12), g == 0, g == 7) for g in range(8)])
+    def spread(site, mats, src, w):
+        q = place(site, 16 * w)
+        mm([(r(q, m, 16 * w, 16), r(mats, 128 * m, 128 * m + 128), src, True, True) for m in range(16)])
         return q
 
-    def best(key, site, parts):
-        kt, ks, q = new("F", L), new("F", L), place(site, 24)
-        ki, k2, kp = new("I", 12), new("I", 24), new("H", 24)
-        for a, b in parts:
-            vtr(r(kt, a, b), r(key, a, b))
-            vscan(r(ks, a, b), r(RS, a, b), r(kt, a, b), -1.0e9, OP.min, OP.max)
-        vs(ki, r(ks, 15, L, 16), 65536.0, None, OP.mult)
-        vs(r(k2, 0, 12), ki, 4095, None, OP.bitwise_and)
-        vs(r(k2, 12, 24), ki, 16, None, OP.arith_shift_right)
-        vs(kp, k2, -1536.0, None, OP.add)
-        mm([(r(q, ih, 24, 2), P[ih][x], r(kp, x, 24, 2), x == 0, x == 1) for ih in (0, 1) for x in (0, 1)])
-        return r(q, 0, 12), r(q, 12, 24)
+    def first(site, terms, accb, xd):
+        q, sc, win, x, o = place(site, L), new("F", L), new("F", 12), new("F", 12), new("U", 24)
+        mm([(q, a, b, i == 0, False) for i, (a, b) in enumerate(terms)] +
+           [(r(q, m, L, 16), r(Sel, 128 * m, 128 * m + 128), accb, False, m == 15) for m in range(16)])
+        vscan(sc, D2, q, 0.0, OP.mult, OP.max)
+        vs(win, r(sc, 15, L, 16), pw15, None, EQ)
+        vt(x, win, xd, OP.mult)
+        aff("a", r(o, 0, 24, 2), x, 1.0, kc)
+        return o
 
-    def send(src, name, sem):
-        src = ref(src)
+    def send(src, dst_, sem):
+        src, dst_ = ref(src), ref(dst_)
 
         def fn(g, T, me, dst, topo):
             rid, pid, se = topo.addr(dst)
-            return g.remote_dma(T[name][:], ap(T, src), T.sem[sem], T.sem.ls, pid, rid, topo.mask(me, dst))
-        add("g", fn, spans(src), [(name + "_sent", 0, 1)], 1.0, "ls", ne)
-        add("net", None, [(name + "_sent", 0, 1)], [(name, 0, SCRATCH[name][1][1])], 2.5, sem, ne)
+            return g.remote_dma(ap(T, dst_), ap(T, src), T.sem[sem], T.sem.ls, pid, rid, topo.mask(me, dst))
+        add("g", fn, spans(src), [(sem + "_sent", 0, 1, 1)], 0.6, "ls", ne)
+        add("net", None, [(sem + "_sent", 0, 1, 1)], spans(dst_), 1.8, sem, ne)
 
     for t in range(VIS):
         last = t == VIS - 1
         vis[:] = [t]
-        cur[0] = "cell"
-        h5, hm, h511, hmat, hdead = new("F", 1), new("F", 1), new("F", 1), new("H", 8), new("H", 8)
-        act(h5, h, AF.Identity, 5.0)
-        act(hm, h, AF.Identity, -1.0, 512.0)
-        act(h511, h, AF.Identity, 1.0, -511.0)
-        vs(hmat, bo8, h511, None, OP.mult)
-        vs(hdead, bo8, hm, None, OP.mult)
+        cels = celn if t else ("cel_i", 0, NC)
+        cur[0] = "h"
+        hm2, h5, hdead = col(h, -0.5, 256.0), col(h, 5.0, 2048.0 + 5 * 1281.0), new("H", 16)
+        act(hdead, bo8, AF.Identity, hm2)
         cur[0] = "zrep"
         for k in range(16):
-            act(r(("zrep", 0, 16 * L), k, 16 * L, 16), z, AF.Copy)
-        cur[0] = "cell"
+            o = r(("zrep", 0, 16 * L), k, 16 * L, 16)
+            if t and k < ZG:
+                gcopy(o, z)
+            else:
+                aff("v" if k >= 16 - ZV else "a", o, z)
+        cur[0] = "u"
         uP = place("u", 12)
-        mm([(uP, r(UW, 15 - k, 143 - k), r(z, k, L, 16), k == 0, k == 15) for k in range(16)])
-        uI, u, ma, mb, mc, c, c1, e = [new("I", 12) for i in range(8)]
-        c16, e16 = new("U", 12), new("U", 12)
-        vc(uI, uP)
+        msum(uP, [(r(UW, 15 - k, 143 - k), r(z, k, L, 16)) for k in range(16)])
+        uI, u, ma, kp, xx, mf, e = [new("I", 12) for i in range(7)]
+        cn, c16, e16, me = new("I", 24), new("U", 12), new("U", 12), new("F", 12)
+        c, w = r(cn, 0, 12), r(PD1, 1, 72, 6)
+        aff("a", uI, uP)
         vs(u, uI, 4095, None, OP.bitwise_and)
+        vs(r(cn, 12, 24), uI, 15, None, OP.bitwise_and)
+        aff("a", w, u, 1.0, 32.0)
+        cur[0] = "cell"
+        aff("v", kp, phi, 32.0, 32.0 * 77 * t - 262144.0)
         vt(ma, phi, u, OP.mult)
-        vs(mb, ma, 5, None, OP.arith_shift_right)
-        p77 = phi
-        if t:
-            p77 = new("F", 12)
-            act(p77, phi, AF.Identity, 1.0, 77.0 * t)
-        vt(mc, mb, p77, OP.add)
-        vs(c, mc, NC - 1, None, OP.bitwise_and)
-        vc(c16, c)
+        vt(xx, ma, kp, OP.add)
+        vs(c, xx, 5, NC - 1, OP.arith_shift_right, OP.bitwise_and)
+        aff("v", c16, c)
         sc16, se16 = new("U", L), new("U", L)
-        vc(sc16, ind(celn, c16))
+        vc(sc16, ind(cels, c16))
         cur[0] = "ecell"
-        me, mf, mg = [new("I", 12) for i in range(3)]
-        vt(me, c, u, OP.mult)
-        vs(mf, me, 5, None, OP.arith_shift_right)
-        vs(c1, c, 1.0, None, OP.add)
-        vt(mg, mf, c1, OP.add)
-        vs(e, mg, NC - 1, None, OP.bitwise_and)
-        vc(e16, e)
-        vc(se16, ind(celn, e16))
+        vt(me, c, w, OP.mult)
+        aff("v", mf, me, 1.0 / 32, 33.0 / 64 - 131072.0)
+        vs(e, mf, NC - 1, None, OP.bitwise_and)
+        aff("a", e16, e)
+        act(se16, ind(cels, e16), AF.Copy)
         dc = lambda a, b: r(place("dA", 128), a, b) if b <= 128 else r(place("dB", 64), a - 128, b - 128)
         for s16, dst in ((sc16, dc), (se16, lambda a, b: r(place("de", L), a, b))):
             for ch in range(3):
                 cur[0] = ("cg" if s16 is sc16 else "eg") + str(ch)
                 df, ad = dfad[ch + (0 if s16 is sc16 else 3)]
-                for x in (0, 1):
-                    w = 1024 * ch + 512 * x
-                    vt(r(df, 512 * x, 512 * x + 512), ind(recn, r(s16, 64 * ch + 32 * x, 64 * ch + 32 * x + 32)), ("zrep", w, 512), OP.subtract)
-                    act(r(ad, 512 * x, 512 * x + 512), r(df, 512 * x, 512 * x + 512), AF.Abs)
-                q = dst(64 * ch, 64 * ch + 64)
-                mm([(q, r(U, 15 - k, 143 - k), r(ad, k, 1024, 16), k == 0, k == 15) for k in range(16)])
+                for x in range(0, 1024, GW):
+                    y = 1024 * ch + x
+                    vt(r(df, x, x + GW), ind(recn, r(s16, y // 16, (y + GW) // 16)), ("zrep", y, GW), OP.subtract)
+                    act(r(ad, x, x + GW), r(df, x, x + GW), AF.Abs)
+                msum(dst(64 * ch, 64 * ch + 64), [(r(U, 15 - k, 143 - k), r(ad, k, 1024, 16)) for k in range(16)])
         cur[0] = "early"
-        n15, n, pa, pb, P2 = new("I", 12), new("F", 12), new("F", 12), new("I", 12), new("I", 12)
-        vs(n15, u, 15, None, OP.bitwise_and)
-        vt(n, n15, i16A, OP.add)
-        act(pa, phi, AF.Identity, 5.0)
-        vt(pb, pa, u, OP.add)
-        vs(P2, pb, 4095, None, OP.bitwise_and)
-        skN, sc32, s16c = new("F", L), new("F", L), new("H", L)
-        act(sc32, ind(celn, c16), AF.Copy)
-        act(skN, sc32, AF.Identity, 2.0 ** -16, knear)
-        vs(s16c, sc16, -1536.0, None, OP.add)
+        aff("a", r(PD1, 0, 72, 6), phi, 4.0, -32.0)
+        aff("a", r(PD1, 4, 72, 6), phi, 5.0, -32.0)
+        aff("a", r(PD1, 5, 72, 6), u, 1.0, 32.0)
+        s16c, cnh, cnd, nL32, nLh = new("H", L), new("H", 24), new("F", 24), new("F", L), new("H", L)
+        aff("a", s16c, sc16, 1.0, -SO)
+        vt(cnd, cn, cnD, OP.add)
         cur[0] = "E1"
-        E1 = pairs(c, Es[0], "c")
-        cur[0] = "E2"
-        E2 = pairs(e, Es[1], "e")
+        vt(cnh, cn, cnH, OP.add)
+        xP, fp, Vh = spread("cn", Sel, cnh, 24), place("fp", L), new("H", L)
+        act(Vh, r(xP, 0, L), AF.Identity, scol, b11)
+        msum(fp, [(L16, Vh), (I16, laneC)])
+        G, Fe, Fo = new("B", L), new("B", L), new("B", L)
+        act(G, fp, AF.Identity, gs, gb)
+        act(Fe, fp, AF.Identity, r(fe, 0, 1), r(fe, 1, 2))
+        act(Fo, fp, AF.Identity, r(fo, 0, 1), r(fo, 1, 2))
+        for a in range(4):
+            bank, ms, pp = ("e1", "e0")[a & 1], [], {"p0": 32 * a, "p1": 32 * a + 32}
+            for x, F in ((0, Fe), (1, Fo)):
+                ms.append((r((bank, L * x, L), 64, L), r(F, 0, 128, **pp), r(G, 64, L, **pp), True, True))
+                ms.append((r((bank, L * x, L), 0, 64, p1=64), r(F, 0, 64, **pp), r(G, 0, 64, **pp), True, True))
+                ms.append((r((bank, L * x, L), 0, 64, p0=64), r(F, 128, L, **pp), r(G, 128, L, **pp), True, True))
+            mm(ms)
+            for x in (0, 1):
+                act(("Z", 0, 12, 32 * a + 16 * x, 32 * a + 16 * x + 16, 0, 128), (bank, L * x, L), AF.Relu, 512.0, -1535.0)
         cur[0] = "n"
-        nm = new("F", 12)
-        act(nm, n, AF.Identity, 1.0, -1536.0)
-        Xn = expand(nm)
+        aff("a", nL32, r(xP, L, 2 * L), 1.0, SO)
+        aff("a", nLh, r(xP, L, 2 * L))
         cur[0] = "slots"
-        q1, q2, K1, K2, dead = new("H", L), new("H", L), new("F", L), new("F", L), new("B", L)
+        a5, q2, sg = new("H", L), new("H", L), new("B", L)
         for a, b in ((0, 128), (128, L)):
-            d = dc(a, b)
-            vt(r(K1, a, b), r(skN, a, b), d, OP.subtract)
-            vs(r(q1, a, b), d, 512.0, -511.0, OP.min, OP.add)
-            vs(r(q2, a, b), r(q1, a, b), h511, h511, OP.min, OP.subtract)
-            vs(r(dead, a, b), r(q1, a, b), 1.0, None, OP.is_ge)
-        cur[0] = "far"
-        kP = place("kP", L)
-        mm([(kP, I16, q1, True, False), (kP, kI16, dead, False, True)])
-        vt(K2, skN, kP, OP.add)
-        cur[0] = "near"
-        nyP, dd = best(K1, "near", ((0, 128), (128, L)))
-        ny16, d5, has = new("U", 12), new("F", 12), new("F", 12)
-        vs(ny16, nyP, 1536.0, None, OP.add)
-        act(d5, dd, AF.Identity, -5.0, 1275.0 - 5 * 1536.0)
-        vs(has, d5, h5, None, OP.is_lt)
-        pog, pos, pd, Pa, P1, Dp, Dh = new("F", L), new("F", L), new("F", 12), new("I", 12), new("I", 12), new("F", 12), new("F", 12)
-        vt(pog, ind(pow_, ny16), diag, OP.mult)
-        vscan(pos, M0, pog, 0.0, OP.mult, OP.add)
-        vt(pd, d5, phi, OP.add)
-        vt(Pa, r(pos, 15, L, 16), pd, OP.add)
-        vs(P1, Pa, 4095, None, OP.bitwise_and)
-        vt(Dp, P1, P2, OP.subtract)
-        vt(Dh, Dp, has, OP.mult)
-        cur[0] = "newz"
-        hP, tP, zP = place("hP", L), place("tP", L), place("zP", L)
-        hs, rz, zw, zm, zn = [new("B", L) for i in range(5)]
-        mm([(hP, BO, q2, True, True)])
-        act(hs, hP, AF.Sign, -1.0)
-        act(rz, ind(recw, ny16), AF.Copy)
-        mm([(tP, I16, rz, True, False), (tP, nI, z, False, True)])
-        vt(zw, hs, tP, OP.mult)
-        mm([(zP, I16, z, True, False), (zP, hI16, zw, False, True)])
-        act(zm, zP, AF.Identity, 1.0, 159.75)
-        act(zn, zm, AF.Identity, 1.0, -160.0)
-        send(zn, "zl%d" % (t + 1), "rz%d" % (t + 1))
-        cur[0] = "far"
-        vP, fd = best(K2, "far", ((0, L),))
-        vm_, riv, vd, vdr = new("F", 12), new("F", 12), new("F", 12), new("F", 12)
-        vs(riv, fd, 256.0 + 1536.0, h, OP.add, OP.is_ge)
-        vt(vd, vP, dumS, OP.subtract)
-        vt(vdr, vd, riv, OP.mult)
-        vt(vm_, vdr, dumS, OP.add)
-        cur[0] = "E3"
-        E3 = pairs(vm_, Es[2], "v")
+            act(r(q2, a, b), dc(a, b), AF.Relu, -1.0, h)
+            act(r(a5, a, b), dc(a, b), AF.Relu, -1.0, 512.0)
+            act(r(sg, a, b), dc(a, b), AF.Sign, 1.0, -512.0)
         cur[0] = "acc"
-        score([(q1, m1), (q2, m3), (dead, hdead)], "s1", (one, hmat))
-        vs(pas, place("s1", 16), 0.0, None, OP.is_ge)
-        lowest(pas, E1, "c", acc)
-        accA = to_a(acc, "acc")
-        ft, phN = new("F", 12), new("F", 12)
-        vt(ft, Dh, accA, OP.mult)
-        vt(phN, ft, P2, OP.add)
+        sP, pas, q, yy, accS = place("sc", 24), new("B", 24), place("q", 96), new("F", 96), new("B", 96)
+        for o, a, b, n in ((r(sP, 0, 16), 0, 128, 16), (r(sP, 16, 24), 64, L, 8)):
+            msum(o, [(nOne, r(hdead, 0, n)), (r(q2, a, b), r(bo3, 0, n)), (r(a5, a, b), r(bo8, 0, n)), (r(sg, a, b), r(hdead, 0, n))])
+        vt(pas, sP, half, OP.is_ge)
+        ms = []
+        for b in range(12):
+            o = r(q, 8 * b, 8 * b + 8)
+            ms.append((o, ("Z", b, b + 1, 0, 128, 0, 128), r(pas, 8, 16) if b < 4 else r(pas, 0, 8), True, b < 8))
+            if b >= 8:
+                ms.append((o, ("Z", b - 8, b - 7, 0, 128, 0, 128), r(pas, 16, 24), False, True))
+        mm(ms)
+        vt(yy, q, cmpc, EQ)
+        vscan(accS, M8, yy, 0.0, OP.mult, OP.add)
+        acc = r(accS, 7, 96, 8)
+        cur[0] = "best"
+        K, kt, ks, mx, rr, kh, bq = place("K", 2 * L), new("F", 2 * L), new("F", 2 * L), new("F", 24), new("F", 24), new("H", 36), place("best", 36)
+        msum(r(K, 0, L), [(I16, cK), (cI, one), (I64, q2), (sI, s16c)])
+        msum(r(K, L, 2 * L), [(I16, cK), (kI, sg), (nI64, a5), (sI, s16c)])
+        vtr(kt, K)
+        vscan(ks, RS, kt, -1.0e9, OP.min, OP.max)
+        vt(mx, r(ks, 15, 2 * L, 16), TK[t], OP.max)
+        vs(rr, mx, M4, -M4, OP.add, OP.add)
+        vt(r(kh, 0, 24), mx, rr, OP.subtract)
+        aff("a", r(kh, 24, 36), r(mx, 0, 12), 1.0 / 64, 1536.53125)
+        mm([(r(bq, ih, 36, 2), P[ih][x], r(kh, x, 36, 2), x == 0, x == 1) for ih in (0, 1) for x in (0, 1)])
+        cur[0] = "near"
+        ny16, has, pog, pq = new("U", 12), new("F", 12), new("H", L), place("pos", 12)
+        aff("a", ny16, r(bq, 0, 12), 1.0, SO)
+        act(pog, ind(("po_t", DU, NR + L * (t + 1)), ny16), AF.Identity, 1.0, -2048.0)
+        msum(pq, [(r(U1, 15 - k, 143 - k), r(pog, k, L, 16)) for k in range(16)])
+        aff("a", r(PD1, 2, 72, 6), pq)
+        aff("a", r(PD1, 3, 72, 6), r(bq, 24, 36), -5.0 / 1024, h5)
+        vs(has, r(bq, 24, 36), 1281.5 * 1024, None, GT)
+        cur[0] = "newz"
+        zP, rz, zm, zn = place("zP", L), new("B", L), new("B", L), new("B", L)
+        act(rz, ind(("rec_t", DU, NR + L * (t + 1)), ny16), AF.Copy)
+        msum(zP, [(hI, z), (hI, rz)])
+        aff("a", zm, zP, 1.0, 159.75)
+        aff("a", zn, zm, 1.0, -160.0)
+        send(zn, zin[t + 1], "rz%d" % (t + 1))
+        cur[0] = "phase"
+        px, phN, ph2, phL = new("I", 72), new("I", 12), new("H", 12), new("F", L)
+        vt(r(PD0, 4, 72, 6), has, acc, OP.mult)
+        vscan(px, PD0, PD1, 0.0, OP.mult, OP.add)
+        vs(phN, r(px, 5, 72, 6), 4095, None, OP.bitwise_and)
         if not last:
-            send(phN, "pl%d" % (t + 1), "rp%d" % (t + 1))
+            send(phN, ("pl%d" % (t + 1), 0, 12), "rp%d" % (t + 1))
         cur[0] = "phL"
-        ph2, phL, lP = new("F", 12), new("F", L), place("lP", L)
-        act(ph2, phN, AF.Identity, 1.0, -2048.0)
-        X = expand(ph2)
-        mm([(lP, BO, X, True, True)])
-        act(phL, lP, AF.Identity, 1.0, 2048.0)
+        aff("a", ph2, phN, 1.0, -2048.0)
+        aff("a", phL, spread("lP", Sel, ph2, 12), 1.0, 2048.0)
         if last:
-            send(phL, "pl%d" % VIS, "rp%d" % VIS)
+            send(phL, ("pend", 0, L), "rp%d" % VIS)
         else:
-            aP, aF, aI, aJ = place("aP", 16), new("F", 1), new("I", 1), new("I", 1)
-            mm([(r(aP, 0, 16, 2), one, r(acc, 0, 16, 2), True, True), (r(aP, 1, 16, 2), r(one, p0=64), r(acc, 1, 16, 2, p0=64), True, True)])
-            vred(aF, aP)
-            vc(aI, aF)
-            vs(aJ, aI, 31, None, OP.bitwise_and)
-        cur[0] = "E3"
-        vfA = to_a(lowest(acc, E3, "v", vfB), "vf")
-        tv, ov, v16 = new("F", 12), new("F", 12), new("U", 12)
-        vt(tv, vdr, vfA, OP.mult)
-        vt(ov, tv, dumR, OP.add)
-        vc(v16, ov)
+            cur[0] = "cnt"
+            aP, aS, aF, aY, aN = place("aP", 12), new("F", 12), new("F", 1), new("F", 1), new("F", 1)
+            msum(aP, [(r(one, 0, 128), acc)])
+            act(aS, aP, AF.Identity, 1.0, 0.0, aF)
+            vs(aY, aF, -15.5, M32, OP.add, OP.add)
+            vs(aN, aY, M32, aF, OP.subtract, OP.subtract)
+            hn = col(aN, -1.0, r(thc, t + 1, t + 2))
+            act(r(TK[t + 1], 12, 24), TC[t + 1], AF.Identity, 1.0, col(aN, -64.0))
+        cur[0] = "ev"
+        evh, thr, ed, vd = new("H", 24), new("B", 2 * L), new("F", 12), new("F", 12)
+        aff("a", r(evh, 0, 12), e)
+        aff("a", r(evh, 12, 24), r(bq, 12, 24))
+        aff("a", ed, e, 1.0, edb)
+        aff("a", vd, r(bq, 12, 24), 1.0, vdb)
+        act(thr, spread("ev", SelI, evh, 24), AF.Abs)
         cur[0] = "lists"
-        nd_, cd_, tn, on, u24 = new("F", 12), new("F", 12), new("F", 24), new("F", 24), new("U", 24)
-        vt(nd_, n, dumR, OP.subtract)
-        vt(cd_, c, dumC, OP.subtract)
-        vt(r(tn, 0, 12), nd_, accA, OP.mult)
-        vt(r(tn, 12, 24), cd_, accA, OP.mult)
-        vt(on, tn, dumRC, OP.add)
-        vc(u24, on)
-        n16, cw = r(u24, 0, 12), r(u24, 12, 24)
-        vc(ind(recw, v16), c64)
+        tn, on, u24 = new("F", 24), new("F", 24), new("U", 24)
+        vt(r(tn, 0, 12), r(cnd, 0, 12), acc, OP.mult)
+        vt(r(tn, 12, 24), r(cnd, 12, 24), acc, OP.mult)
+        vt(on, tn, ln24, OP.add)
+        aff("a", u24, on)
+        cw, n16 = r(u24, 0, 12), r(u24, 12, 24)
+        cur[0] = "die"
+        v16 = first("t3", [(nI, r(thr, L, 2 * L))], acc, vd)
+        for b in range(12):
+            vc(ind(recw, r(v16, 2 * b, 2 * b + 1)), c64)
+        cur[0] = "born"
         vc(ind(recw, n16), zn)
+        cur[0] = "bpo"
         vc(ind(pow_, n16), phL)
         cur[0] = "ent1"
-        M1, ch1, mP, DP = new("F", L), new("F", L), place("m1", L), place("D1", L)
-        mm([(mP, TL, dead, True, True), (DP, BO, Xn, True, False), (DP, nI, s16c, False, True)])
-        act(M1, mP, AF.Relu)
-        vt(ch1, M1, DP, OP.mult)
-        vt(ind(celw, cw), ch1, sc32, OP.add)
+        N1, ch1, mP, DP = new("F", L), new("F", L), place("m1", L), place("D1", L)
+        mm([(mP, TL, sg, True, True), (DP, I16, nLh, True, False), (DP, nI, s16c, False, True)])
+        act(N1, mP, AF.Sign, -0.5, kb1)
+        vt(ch1, N1, DP, OP.mult)
+        vt(ind(celw, cw), nL32, ch1, OP.subtract)
+        cur[0] = "slote"
+        q2e, sge = new("H", L), new("B", L)
+        act(q2e, place("de", L), AF.Relu, -1.0, h)
+        act(sge, place("de", L), AF.Sign, 1.0, -512.0)
+        cur[0] = "win"
+        ew = first("t2", [(nI, r(thr, 0, L)), (nBO, q2e)], acc, ed)
         cur[0] = "ent2"
-        q1e, q2e, deade = new("H", L), new("H", L), new("B", L)
-        vs(q1e, place("de", L), 512.0, -511.0, OP.min, OP.add)
-        vs(q2e, q1e, h511, h511, OP.min, OP.subtract)
-        vs(deade, q1e, 1.0, None, OP.is_ge)
-        score([(q2e, m1)], "s2")
-        vt(cand, acc, place("s2", 16), OP.is_gt)
-        wA = to_a(lowest(cand, E2, "e", winB), "win")
-        ed, et, eo, ew = new("F", 12), new("F", 12), new("F", 12), new("U", 12)
-        vt(ed, e, dumC, OP.subtract)
-        vt(et, ed, wA, OP.mult)
-        vt(eo, et, dumC, OP.add)
-        vc(ew, eo)
-        M2, sE, s16e, ch2, mP, DP = new("F", L), new("F", L), new("H", L), new("F", L), place("m2", L), place("D2", L)
-        act(sE, ind(celn, e16), AF.Copy)
-        vs(s16e, sE, -1536.0, None, OP.add)
-        mm([(mP, TH, deade, True, True), (DP, BO, Xn, True, False), (DP, nI, s16e, False, True)])
-        act(M2, mP, AF.Relu)
-        vt(ch2, M2, DP, OP.mult)
-        vt(ind(celw, ew), ch2, sE, OP.add)
+        N2, s16e, ch2, mP, DP = new("F", L), new("H", L), new("F", L), place("m2", L), place("D2", L)
+        msum(mP, [(TH, sge)])
+        act(N2, mP, AF.Sign, -0.5, kb2)
+        act(s16e, ind(celn, e16), AF.Identity, 1.0, -SO)
+        msum(DP, [(I16, nLh), (nI, s16e)])
+        vt(ch2, N2, DP, OP.mult)
+        for b in range(11, -1, -1):
+            vt(ind(celw, r(ew, 2 * b, 2 * b + 1)), r(nL32, 16 * b, 16 * b + 16), r(ch2, 16 * b, 16 * b + 16), OP.subtract)
         if not last:
-            h = new("F", 1)
-            vt(h, aJ, r(thc, t + 1, t + 2), OP.add)
-            z, phi = ("zl%d" % (t + 1), 0, L), ("pl%d" % (t + 1), 0, 12)
-    dma(lambda g, T: g.sync.dma_start(out=T.ypat[:], in_=T["zl%d" % VIS][:]), [("zl%d" % VIS, 0, L)], [("ypat", 0, 1)], 2.2)
-    dma(lambda g, T: g.sync.dma_start(out=T.yphi[:], in_=T["pl%d" % VIS][::16, :]), [("pl%d" % VIS, 0, L)], [("yphi", 0, 1)], 2.2)
-    dma(lambda g, T: g.sync.dma_start(out=T.ypo[:], in_=T.po_t[::16, 0:NR]), [("po_t", 0, NR)], [("ypo", 0, 1)], 3.0)
-    dma(lambda g, T: g.sync.dma_start(out=T.yrec[:], in_=T.rec_t[:, 0:NR]), [("rec_t", 0, NR)], [("yrec", 0, 1)], 5.0)
-    dma(lambda g, T: g.sync.dma_start(out=T.ycel[:], in_=T.cel_t[:, 0:NC]), [("cel_t", 0, NC)], [("ycel", 0, 1)], 6.0)
+            h, z, phi = hn, zin[t + 1], ("pl%d" % (t + 1), 0, 12)
+    cur[0] = "out"
+    dma(lambda g, T: g.sync.dma_start(out=T.ypat[:], in_=T.zend[:]), [("zend", 0, L, 1)], [("ypat", 0, 1, 1)], 1.7)
+    dma(lambda g, T: g.sync.dma_start(out=T.yphi[:], in_=T.pend[::16, :]), [("pend", 0, L, 1)], [("yphi", 0, 1, 1)], 1.7)
+    dma(lambda g, T: g.sync.dma_start(out=T.ypo[:], in_=T.po_t[::16, DU:DU + NR]), [("po_t", DU, DU + NR, 1)], [("ypo", 0, 1, 1)], 2.5)
+    dma(lambda g, T: g.sync.dma_start(out=T.yrec[:], in_=T.rec_t[:, DU:DU + NR]), [("rec_t", DU, DU + NR, 1)], [("yrec", 0, 1, 1)], 4.0)
+    dma(lambda g, T: g.sync.dma_start(out=T.ycel[:], in_=T.cel_t[:, DU:CW]), [("cel_t", DU, CW, 1)], [("ycel", 0, 1, 1)], 5.0)
     return ops
+
+
+def meet(a, b, s, lo, hi, st):
+    if a >= hi or lo >= b:
+        return False
+    if s == 1 and st == 1:
+        return True
+    if s < st:
+        a, b, s, lo, hi, st = lo, hi, st, a, b, s
+    return any(lo <= x < hi and (x - lo) % st == 0 for x in range(a, b, s))
 
 
 def depend(ops):
@@ -586,51 +542,54 @@ def depend(ops):
     for o in ops:
         d = set()
         acc = [(s, False) for s in o["r"]] + [(s, True) for s in o["w"]]
-        for (buf, lo, hi), wr in acc:
-            for (k, a, b, w) in hist.get(buf, []):
-                if (w or wr) and a < hi and lo < b:
+        for (buf, lo, hi, st), wr in acc:
+            for (k, a, b, s, w) in hist.get(buf, []):
+                if (w or wr) and meet(a, b, s, lo, hi, st):
                     d.add(k)
-        for (buf, lo, hi), wr in acc:
+        for (buf, lo, hi, st), wr in acc:
             hh = hist.setdefault(buf, [])
             if wr:
-                hist[buf] = hh = [x for x in hh if not (lo <= x[1] and x[2] <= hi)]
-            hh.append((o["i"], lo, hi, wr))
+                hist[buf] = hh = [x for x in hh if not (lo <= x[1] and x[2] <= hi + st - 1 and (st == 1 or (x[3] % st == 0 and (x[1] - lo) % st == 0)))]
+            hh.append((o["i"], lo, hi, st, wr))
         d.discard(o["i"])
         deps.append(d)
     return deps
 
 
-def schedule(ops, deps):
+def schedule(ops, deps, bias):
     n = len(ops)
     succ = [[] for i in range(n)]
     for i, d in enumerate(deps):
         for k in d:
             succ[k].append(i)
-    lat = lambda k, i: 0.05 if ops[k]["q"] == ops[i]["q"] else (0.12 if ops[k]["q"] != "net" else 0.3)
+    qs = [o["q"] for o in ops]
+    lat = lambda k, i: (0.0 if qs[k] == "p" else 0.08) if qs[k] == qs[i] else (0.18 if qs[k] != "net" else 0.3)
     pr = [0.0] * n
     for i in range(n - 1, -1, -1):
         pr[i] = ops[i]["cost"] + max([lat(i, j) + pr[j] for j in succ[i]] or [0.0])
+    key = [pr[i] + bias.get(ops[i]["tag"], bias.get(ops[i]["tag"].rstrip("012") if ops[i]["tag"][:2] not in ("cg", "eg") else ops[i]["tag"][:3], 0.0)) for i in range(n)]
     left = [len(d) for d in deps]
-    ready = {i for i in range(n) if not left[i]}
+    cand = {q: [] for q in ("v", "a", "p", "g", "s", "net")}
+    for i in range(n):
+        if not left[i]:
+            cand[qs[i]].append(i)
     banks = [sorted(set(s[0] for s in o["r"] + o["w"] if s[0] in BANKS)) for o in ops]
     rt, free, order, end, used = [0.0] * n, {}, [], [0.0] * n, {b: {} for b in BANKS}
-    while ready:
-        pick, cand = None, {q: [] for q in ("v", "a", "p", "g", "s", "net")}
-        for i in sorted(ready):
-            cand[ops[i]["q"]].append(i)
+    while len(order) < n:
+        pick = None
         for q, li in cand.items():
             if not li:
                 continue
             f = free.get(q, 0.0) if q != "net" else 0.0
             at = {}
             for i in li:
-                at[i] = max([f, rt[i]] + [end[k] + 0.12 for b in banks[i] for o, k in used[b].items() if o != q])
+                at[i] = max([f, rt[i]] + [end[k] + 0.18 for b in banks[i] for o, k in used[b].items() if o != q])
             s0 = min(at.values())
-            b = max((i for i in li if at[i] <= s0 + 0.04), key=lambda i: (pr[i] + BIAS.get(ops[i]["tag"], 0.0), -i))
+            b = max((i for i in li if at[i] <= s0 + 0.06), key=lambda i: (key[i], -i))
             if pick is None or at[b] < pick[0]:
                 pick = (at[b], b, q)
         s, i, q = pick
-        ready.discard(i)
+        cand[q].remove(i)
         free[q] = s + (0.1 if q == "s" else ops[i]["cost"])
         end[i] = s + ops[i]["cost"]
         order.append(i)
@@ -641,7 +600,7 @@ def schedule(ops, deps):
             rt[j] = max(rt[j], end[i] + lat(i, j))
             left[j] -= 1
             if not left[j]:
-                ready.add(j)
+                cand[qs[j]].append(j)
     return order, max(end)
 
 
@@ -652,7 +611,7 @@ def plan(ne):
     if "plan" not in CACHE:
         ops = build(ne)
         deps = depend(ops)
-        order, span = schedule(ops, deps)
+        order, span = schedule(ops, deps, BIAS)
         CACHE["plan"] = (ops, deps, order, span)
     return CACHE["plan"]
 

@@ -6,13 +6,13 @@ L, NR, NC, VIS, STEP = 192, 3072, 2048, 3, 3
 DU = L
 RW, CW = DU + NR + VIS * L, DU + NC
 SO = 1664.0
-POOLS = {"F": 14000, "I": 2400, "U": 2000, "B": 30000, "H": 7000}
+POOLS = {"F": 14000, "I": 2400, "U": 2000, "B": 32000, "H": 7000}
 DTN = {"F": "float32", "I": "int32", "U": "uint16", "B": "bfloat16", "H": "float16"}
 SCRATCH = {
     "rec_t": ("sbuf", [128, RW], "bfloat16"), "cel_t": ("sbuf", [128, CW], "float32"), "po_t": ("sbuf", [128, RW], "float32"),
     "cel_i": ("sbuf", [128, NC], "int32"), "zrep": ("sbuf", [128, 16 * L], "bfloat16"), "pair": ("sbuf", [128, 12, 128], "bfloat16"),
     "zend": ("sbuf", [128, L], "bfloat16"), "pend": ("sbuf", [128, L], "float32"),
-    "pl1": ("sbuf", [128, 12], "int32"), "pl2": ("sbuf", [128, 12], "int32"),
+    "hb": ("sbuf", [128, VIS, 32], "float32"), "pl1": ("sbuf", [128, 12], "int32"), "pl2": ("sbuf", [128, 12], "int32"),
 }
 for _k in POOLS:
     SCRATCH["pool" + _k] = ("sbuf", [128, POOLS[_k]], DTN[_k])
@@ -21,13 +21,25 @@ for _b in BANKS:
     SCRATCH[_b] = ("psum", [128, 512], "float32")
 SITE = {"dA": ("b0", 0), "K": ("b0", 128), "cn": ("b1", 0), "dB": ("b1", 384), "u": ("b1", 448), "aP": ("b1", 464), "pos": ("b1", 480),
         "de": ("b2", 0), "lP": ("b2", 192), "sc": ("b2", 384), "q": ("b2", 416), "fp": ("b3", 0), "zP": ("b3", 192), "best": ("b3", 384),
-        "ev": ("b4", 0), "t2": ("b5", 0), "t3": ("b5", 192), "m1": ("e0", 0), "D1": ("e0", 192), "m2": ("e1", 0), "D2": ("e1", 192)}
+        "ev": ("b4", 0), "t": ("b5", 0), "t2": ("b4", 0), "m1": ("e0", 0), "D1": ("e0", 192), "m2": ("e1", 0), "D2": ("e1", 192)}
 SEMAPHORES = ["sv", "sa", "sp", "sg", "ls"] + ["d%d" % i for i in range(20)] + ["rz%d" % t for t in (1, 2, 3)] + ["rp%d" % t for t in (1, 2, 3)]
-NS, NP = 0.92e-3, 0.5e-3
 M4, M32 = 50331648.0, 402653184.0
-ZG, ZV = 6, 0
-GW = 512
-BIAS = {}
+ZG, ZV = 7, 8
+C1, C2, C3, C4 = [0, 1024], [0, 512, 1024], [0, 512, 768, 1024], [0, 768, 1024]
+CUT = [(C1, C1), (C1, C1), (C3, C3), (C2, C1), (C1, C1), (C4, C4)]
+JOINT = (True, True, False)
+ENG = {k: "a" for k in "kp c16 sc16 se16 hx uI w w2 p5 s16c nL32 nLh ny16 zm zn ph2 phL evh0 evh1 e16 pog rz s16e hdead N1 N2".split()}
+ENG.update({k: "v" for k in "acc2 ev16 evd kD pos d5 q2e u24".split()})
+NS, NP, LAT, BW, SAME, CROSS, WIN, HOLD = 0.85e-3, 0.5e-3, 1.5, 290.0, 0.09, 0.22, 0.06, 0.3
+MODELS = [(1.0, 1.0, 1.0, 1.0, SAME, CROSS), (0.5, 1.3, 1.15, 1.3, 0.08, 0.2), (0.6, 0.97, 0.8, 0.75, 0.11, 0.27)]
+ROUNDS = [(50000, 1.0, 5.0, 1), (40000, 0.6, 2.0, 1), (20000, 0.4, 1.0, 3)]
+DUE = {"a": dict(cell=-12, u=-11.5, zrep=-11, h=-9, cg0=-8, cg1=-7, cg2=-6, ecell=-5.5, slots=-5, early=-4.5, best=-4, near=-3, acc=-3, newz=-2, E1=0, n=1.5,
+                 ent1=2, ev=3, lists=3.5, slote=4, win=4, vic=4, ent2=4.5, eg0=5, eg1=6, eg2=7, cnt=10, phL=12),
+       "v": dict(u=-12.5, cell=-12, E1=-11, ecell=-10.5, zrep=-10, h=-10, best=-1, phase=-0.9, near=-0.8, newz=-0.6, acc=-0.5, cg0=0, cg1=1, cg2=2, early=2.6,
+                 n=2.7, ev=2.8, lists=3, slote=3.3, vic=3.4, win=3.5, ent1=4, eg0=5, eg1=6, eg2=7, cnt=8, phL=8.5, ent2=9.4, die=9.5, born=9.6, bpo=22.5),
+       "p": dict(u=-13, cg0=-5, cg1=-4.5, cg2=-4, best=-3, near=-2.5, acc=-2, newz=-1.5, E1=-1, ev=1, vic=1.5, win=2, eg0=3, eg1=4, eg2=5, ent2=5.5, ent1=6,
+                 cnt=8, phL=9),
+       "g": dict(zrep=-10, phase=0, newz=1, phL=2), "s": dict(out=0), "net": {}}
 CACHE = {}
 
 
@@ -52,6 +64,9 @@ def build(ne):
     def ind(win, off):
         return ("X", ref(win), ref(off))
 
+    def cube(name, a, b, c0, c1):
+        return ("Z", a, b, c0, c1, name)
+
     def place(site, w):
         return (SITE[site][0], SITE[site][1], w)
 
@@ -61,7 +76,8 @@ def build(ne):
         if x[0] == "X":
             return spans(x[1]) + spans(x[2])
         if x[0] == "Z":
-            return [("pair", 128 * b + x[3], 128 * b + x[4], 1) for b in range(x[1], x[2])]
+            w = SCRATCH[x[5]][1][2]
+            return [(x[5], w * b + x[3], w * b + x[4], 1) for b in range(x[1], x[2])]
         return [(x[1], x[2], x[3], x[4])]
 
     def ncol(x):
@@ -75,62 +91,54 @@ def build(ne):
         if x[0] == "X":
             return ap(T, x[1]).indirect(ap(T, x[2]))
         if x[0] == "Z":
-            return T.pair[x[5]:x[6], x[1], :] if x[2] == x[1] + 1 else T.pair[x[5]:x[6], x[1]:x[2], x[3]:x[4]]
+            return T[x[5]][:, x[1], x[3]:x[4]] if x[2] == x[1] + 1 else T[x[5]][:, x[1]:x[2], x[3]:x[4]]
         t = T[x[1]]
         return t[x[5]:x[6], x[2]:x[3]] if x[4] == 1 else t[x[5]:x[6], x[2]:x[3]:x[4]]
 
     def two(x):
         return x[0] == "R" and x[1] in ("poolB", "poolH", "poolU", "zrep", "rec_t")
 
-    def add(q, fn, reads, writes, cost, sem=None, val=1):
-        ops.append({"q": q, "fn": fn, "r": reads, "w": writes, "cost": cost, "sem": sem, "val": val, "i": len(ops),
+    def add(q, fn, reads, writes, cost, sem=None, val=1, kind=1):
+        ops.append({"q": q, "fn": fn, "r": reads, "w": writes, "cost": cost, "sem": sem, "val": val, "i": len(ops), "kind": kind,
                     "tag": cur[0] + (str(vis[0]) if vis else "")})
 
-    def vcost(o, ins, rate):
-        n = ncol(o)
-        if o[0] == "X":
-            return 0.05 + n * 3.5 * NS
-        if any(x[0] == "X" for x in ins):
-            return 0.05 + n * 1.55 * NS
-        return 0.025 + max(64, n * rate) * NS
-
-    def vop(fn, outs, ins, cost):
-        add("v", fn, [s for x in ins for s in spans(x)] + [s for x in outs if x[0] == "X" for s in spans(x[2])],
-            [s for x in outs for s in spans(x[1] if x[0] == "X" else x)], cost)
+    def vop(fn, o, ins, rate):
+        n, kind = ncol(o), 3 if o[0] == "X" else 2 if any(x[0] == "X" for x in ins if isinstance(x, tuple)) else 1
+        add("v", fn, [s for x in ins for s in spans(x)] + (spans(o[2]) if kind == 3 else []), spans(o[1] if kind == 3 else o),
+            0.05 + n * (3.5 if kind == 3 else 1.55) * NS if kind > 1 else 0.045 + max(64, n * rate) * NS, kind=kind)
 
     def vt(o, a, b, op):
         o, a, b = ref(o), ref(a), ref(b)
-        both = a[0] == "R" and a[1] not in BANKS and b[1] not in BANKS
-        vop(lambda g, T: g.vector.tensor_tensor(out=ap(T, o), in0=ap(T, a), in1=ap(T, b), op=op), [o], [a, b], vcost(o, [a, b], 2 if both else 1))
+        vop(lambda g, T: g.vector.tensor_tensor(out=ap(T, o), in0=ap(T, a), in1=ap(T, b), op=op), o, [a, b], 1 if a[1] in BANKS or b[1] in BANKS else 2)
 
     def vs(o, a, s1, s2, op0, op1=None):
         o, a, s1, s2 = ref(o), ref(a), ref(s1), ref(s2)
         ex = {} if op1 is None else {"op1": op1}
         vop(lambda g, T: g.vector.tensor_scalar(out=ap(T, o), in0=ap(T, a), scalar1=ap(T, s1), scalar2=ap(T, s2), op0=op0, **ex),
-            [o], [a, s1, s2], vcost(o, [a], 0.5 if two(o) and two(a) else 1))
+            o, [a, s1, s2], 0.5 if two(o) and two(a) else 1)
 
     def vc(o, a):
         o, a = ref(o), ref(a)
-        vop(lambda g, T: g.vector.tensor_copy(out=ap(T, o), in_=ap(T, a)), [o], [a], vcost(o, [a], 0.5 if two(o) and two(a) else 1))
+        vop(lambda g, T: g.vector.tensor_copy(out=ap(T, o), in_=ap(T, a)), o, [a], 0.5 if two(o) and two(a) else 1)
 
     def vm(o, v):
         o = ref(o)
-        vop(lambda g, T: g.vector.memset(ap(T, o), v), [o], [], vcost(o, [], 0.5 if two(o) else 1))
+        vop(lambda g, T: g.vector.memset(ap(T, o), v), o, [], 0.5 if two(o) else 1)
 
     def vscan(o, d0, d1, init, o0, o1):
         o, d0, d1 = ref(o), ref(d0), ref(d1)
-        vop(lambda g, T: g.vector.tensor_tensor_scan(out=ap(T, o), data0=ap(T, d0), data1=ap(T, d1), initial=init, op0=o0, op1=o1), [o], [d0, d1], vcost(o, [d0], 1))
+        vop(lambda g, T: g.vector.tensor_tensor_scan(out=ap(T, o), data0=ap(T, d0), data1=ap(T, d1), initial=init, op0=o0, op1=o1), o, [d0, d1], 1)
 
     def vtr(o, a):
         o, a = ref(o), ref(a)
-        vop(lambda g, T: g.vector.transpose(out=ap(T, o), in_=ap(T, a)), [o], [a], vcost(o, [a], 1))
+        vop(lambda g, T: g.vector.transpose(out=ap(T, o), in_=ap(T, a)), o, [a], 1)
 
     def act(o, a, f=AF.Identity, scale=1.0, bias=0.0, acc=None):
         o, a, scale, bias, acc = ref(o), ref(a), ref(scale), ref(bias), ref(acc)
         x, ex = a[0] == "X", lambda T: {} if acc is None else {"accum_out": ap(T, acc)}
         add("a", lambda g, T: g.scalar.activation(out=ap(T, o), in_=ap(T, a), func=f, bias=ap(T, bias), scale=ap(T, scale), **ex(T)),
             [s for y in (a, scale, bias) for s in spans(y)], spans(o) + spans(acc),
-            (0.065 + ncol(o) * 1.55 * NS if x else 0.03 + max(64, ncol(o)) * NS) + (0.02 if acc else 0.0))
+            (0.065 + ncol(o) * 1.55 * NS if x else 0.055 + max(64, ncol(o)) * NS) + (0.02 if acc else 0.0), kind=2 if x else 1)
 
     def aff(q, o, a, scale=1.0, bias=0.0):
         if q == "a":
@@ -151,7 +159,7 @@ def build(ne):
                 k = g.tensor.matmul(ap(T, o), ap(T, a), ap(T, b), s, e)
             return k
         rd = sorted(set(s for o, a, b, x, e in ms for y in (a, b) for s in spans(y)))
-        add("p", fn, rd, sorted(set(s for m in ms for s in spans(m[0]))), sum(max(min(64, ncol(m[1])), ncol(m[2])) * NP + 0.012 for m in ms) + 0.05)
+        add("p", fn, rd, sorted(set(s for m in ms for s in spans(m[0]))), sum(max(min(64, ncol(m[1])), ncol(m[2])) * NP + 0.007 for m in ms) + 0.055)
 
     def msum(o, terms):
         mm([(o, a, b, i == 0, i == len(terms) - 1) for i, (a, b) in enumerate(terms)])
@@ -168,23 +176,23 @@ def build(ne):
     def gcopy(o, a):
         sel(o, a, [[0, ncol(ref(o))]], 1, 0, 0.0, OP.is_gt)
 
-    def dma(fn, reads, writes, cost):
-        add("s", fn, reads, writes, cost, "d%d" % ndma[0], 16)
+    def dma(fn, reads, writes, kb, n=1):
+        add("s", fn, reads, writes, LAT + 0.1 * n + kb / BW, "d%d" % ndma[0], 16 * n, 0)
         ndma[0] += 1
 
     zin = [("rec_t", DU + NR + L * t, L) for t in range(VIS)] + [("zend", 0, L)]
     z, wI, thI, phI, poI = zin[0], new("I", 1), new("I", 3), new("I", L), new("I", L)
 
-    def load(name, o, cost):
+    def load(name, o, kb):
         o = ref(o)
-        dma(lambda g, T: g.sync.dma_start(out=ap(T, o), in_=T[name][:]), [], spans(o), cost)
-    load("wt", wI, 1.6)
-    load("pat", z, 1.7)
-    load("phi", r(phI, p1=8), 1.7)
-    load("cel", ("cel_i", 0, NC), 5.0)
-    load("th", r(thI, p1=8), 2.0)
-    load("rec", ("rec_t", DU, NR), 7.5)
-    load("po", poI, 7.5)
+        dma(lambda g, T: g.sync.dma_start(out=ap(T, o), in_=T[name][:]), [("loads", 0, 1, 1)], spans(o) + [("order", ndma[0], ndma[0] + 1, 1)], kb)
+    load("wt", wI, 10)
+    load("pat", z, 48)
+    load("phi", r(phI, p1=8), 10)
+    load("po", poI, 96)
+    load("cel", ("cel_i", 0, NC), 1024)
+    load("rec", ("rec_t", DU, NR), 768)
+    load("th", r(thI, p1=8), 5)
 
     cur[0] = "const"
 
@@ -198,7 +206,7 @@ def build(ne):
         vs(o, a, s1, s2, op0, op1)
         return o
     EQ, NE, GT = OP.is_equal, OP.not_equal, OP.is_gt
-    pI, pk, xF, yg, i15, i8, lnT = new("I", 3), new("F", 3), new("F", L), new("F", 128), new("F", 2 * L), new("F", 96), new("F", 12)
+    pI, pk, xF, yg, i15, i8, lnT = new("I", 3), new("F", 3), new("B", L), new("B", 128), new("B", 2 * L), new("B", 96), new("F", 36)
     iota(r(pI, 0, 1), [[0, 1]], 0, 1)
     iota(xF, [[1, L]], 0, 0)
     iota(yg, [[1, 8], [0, 16]], 0, 0)
@@ -221,30 +229,33 @@ def build(ne):
     kk = lambda j: r(diag, j, j + 1)
     Sel, SelI = new("B", 2048), new("B", 2048)
     for m in range(16):
-        aff("av"[m & 1], r(Sel, 128 * m, 128 * m + 128), BO, kk(m), 0.0)
-    I16 = vcol(x128, pc, None, EQ, None, "B")
-    nI, hI, I64, nI64, sI, cI, kI = [vcol(I16, v, None, OP.mult, None, "B") for v in (-1.0, 0.5, 64.0, -64.0, 2.0 ** -10, -16320.0, -16512.0)]
-    lane = col(r(xF, 0, 12), 16.0, kc)
-    cnH, cnD, ln24 = new("F", 24), new("F", 24), new("F", 24)
-    act(r(cnH, 0, 12), lane, AF.Identity, 0.0)
-    act(r(cnH, 12, 24), lane, AF.Identity, 16.0, -SO)
-    act(r(cnD, 0, 12), lane, AF.Identity, -1.0, float(DU))
-    act(r(cnD, 12, 24), lane, AF.Identity, 15.0, float(DU))
-    act(r(ln24, 0, 12), lane)
-    act(r(ln24, 12, 24), lane)
+        aff("v", r(Sel, 128 * m, 128 * m + 128), BO, kk(m), 0.0)
+    I16, nI, sI, cI, kI = [vcol(x128, pc, v, EQ, OP.mult, "B") for v in (1.0, -1.0, 2.0 ** -10, -16320.0, -16512.0)]
+    b24, cnH, cnD = new("F", 24), new("F", 24), new("F", 24)
+    iota(b24, [[0, 2], [16, 12]], 0, 0)
+    ln24 = col(b24, 1.0, kc)
+    vm(r(cnH, 0, 12), 0.0)
+    act(r(cnH, 12, 24), r(ln24, 0, 12), AF.Identity, 16.0, -SO)
+    act(r(cnD, 0, 12), r(ln24, 0, 12), AF.Identity, -1.0, float(DU))
+    act(r(cnD, 12, 24), r(ln24, 0, 12), AF.Identity, 15.0, float(DU))
     iota(i15, [[0, 24], [1, 16]], 0, 0)
     iota(i8, [[0, 12], [1, 8]], 0, 0)
-    iota(lnT, [[32, 6], [0, 2]], 0, 0)
-    sel8, selS, thc = new("H", 128), new("H", 256), new("F", 3)
+    iota(lnT, [[L, VIS], [32, 6], [0, 2]], 0, 0)
+    sel8, selS = new("H", 128), new("H", 256)
     vs(r(sel8, p1=8), r(yg, p1=8), r(pc, p1=8), None, EQ)
     for s in (0, 1):
         sel(r(selS, 128 * s, 128 * s + 128, p1=8), r(one, 0, 128, p1=8), [[-2, 4], [0, 32]], -s, 1, 0.0, EQ)
     act(r(th16, p1=8), r(thI, p1=8))
-    tp = place("aP", 9)
-    mm([(r(tp, 0, 3), r(sel8, p1=8), r(th16, p1=8), True, True)] +
-       [(r(tp, 3 + 3 * s, 6 + 3 * s), r(selS, 128 * s, 128 * s + 128, p1=8), r(th16, p1=8), True, True) for s in (0, 1)])
-    act(thc, r(tp, 0, 3))
-    tcol = col(r(tp, 3, 9), 64.0, col(kc, 2.0 ** -10, -16320.0 - 1680.0 / 1024))
+    tp, coef = place("t", 39), new("F", 27)
+    mm([(r(tp, 36, 39), r(sel8, p1=8), r(th16, p1=8), True, True)] +
+       [(r(tp, x, x + 1), r(selS, 128 * (x & 1), 128 * (x & 1) + 128, p1=8), r(th16, x // 12, x // 12 + 1, p1=8), True, True) for x in range(36)])
+    act(cube("hb", 0, VIS, 12, 24), r(tp, 0, 36), AF.Identity, 64.0, col(kc, 2.0 ** -10, -16320.0 - 1680.0 / 1024))
+    vm(r(coef, 0, 12), 0.0)
+    vm(r(coef, 12, 25), -64.0)
+    for x, a, b in ((24, 64.0, 0.0), (25, -0.5, 256.0), (26, 5.0, 2048.0 + 5 * 1281.0)):
+        act(cube("hb", 0, VIS, x, x + 1), r(tp, 36, 39), AF.Identity, a, b)
+        if x > 24:
+            vm(r(coef, x, x + 1), -a)
     gI = new("I", 1)
     vs(gI, r(pI, 1, 2), 1, None, OP.bitwise_and)
     oc = col(gI)
@@ -259,49 +270,62 @@ def build(ne):
     act(r(fsb, 0, 1), kk(13), AF.Identity, -1.0 / 512, klt)
     act(r(fsb, 1, 2), f11, AF.Identity, 1.0, kk(12))
     fe, fo, gs, gb = col(fsb, ec), col(fsb, oc), col(kk(12), 1.0 / 512, klt), col(f11, 1.0, kk(13))
-    L16, LA, laneC = new("B", 128), vcol(x128, col(pc, 1.0, -1.0), col(kv, -2.0), EQ, OP.mult, "B"), col(xF, col(kk(12), 1.0, kk(13)), 0.0, "B")
+    L16, LA, laneC = new("B", 128), vcol(x128, col(pc, 1.0, -1.0), col(kv, -2.0), EQ, OP.mult, "B"), vcol(xF, col(kk(12), 1.0, kk(13)), None, OP.mult, None, "B")
     vt(L16, LA, I16, OP.add)
-    bo8, half = vcol(r(i8, 0, 16), gc, None, EQ, None, "B"), new("F", 24)
-    for x, v in ((0, 0.0), (8, 1.0), (16, -1.0)):
-        act(r(half, x, x + 8), r(xF, 0, 8), AF.Relu, 0.0, col(pc, 1.0e6 * v, -63.5e6 * v))
-    bo3, nOne, nBO = col(bo8, 3.0, 0.0, "B"), col(r(one, 0, 128), -1.0, 0.0, "B"), vcol(BO, -1.0, None, OP.mult, None, "B")
-    cmpc, M8 = vcol(i8, gc, 0.5, EQ, OP.max), vcol(i8, 0.5, None, GT)
+    i16 = r(i8, 0, 16)
+    bo8, bo1, bo3 = [vcol(i16, gc, v, EQ, OP.mult, "B") for v in (1.0, 1.0 / 64, 3.0 / 64)]
+    half, nOne, nBO = new("F", 24), new("B", 128), vcol(yg, gc, -1.0, EQ, OP.mult, "B")
+    vm(half, 0.0)
+    vm(r(half, 8, 16, p0=64), 1.0e6)
+    vm(r(half, 16, 24, p1=64), 1.0e6)
+    vm(nOne, -1.0)
+    cmpc, M8 = vcol(i8, gc, 0.5, EQ, OP.max), vcol(i8, 0.5, None, GT, None, "B")
     cK = col(one, col(kc, -4.0, -4.0), 0.0, "B")
-    RS, D2 = new("F", 2 * L), vcol(r(i15, 0, L), 0.5, 2.0, GT, OP.mult)
-    vs(RS, vcol(i15, 0.5, -0.5, GT, OP.add), 2.0e9, None, OP.mult)
+    RS, D2 = vcol(i15, 0.5, -1.0e9, OP.is_lt, OP.mult, "B"), vcol(i15, 0.5, 2.0, GT, OP.mult, "B")
     e10, o10 = col(ec, 1024.0), col(oc, 1024.0)
     P = [[vcol(x128, pc, e10, EQ, OP.mult, "B"), vcol(x128, col(pc, 1.0, 16.0), e10, EQ, OP.mult, "B")],
          [vcol(x128, col(pc, 1.0, -16.0), o10, EQ, OP.mult, "B"), vcol(x128, pc, o10, EQ, OP.mult, "B")]]
     U1 = vcol(x144, c15, kk(0), EQ, OP.mult, "B")
-    p32 = col(oc, 16.0 / 1024, col(kc, 1.0 / 1024))
-    TK, TC = [new("F", 24) for t in range(VIS)], [None, new("F", 12), new("F", 12)]
-    for t in range(VIS):
-        act(r(TK[t], 0, 12), lnT, AF.Identity, 1.0 / 1024, col(p32, 1.0, -16324.0 + (NR + L * t - SO) / 1024))
-        for s in (0, 1):
-            act(r(TC[t], s, 12, 2) if t else r(TK[0], 12 + s, 24, 2), r(xF, 0, 6), AF.Identity, 0.0, r(tcol, 3 * s + t, 3 * s + t + 1))
+    p32 = col(oc, 16.0 / 1024, col(kc, 1.0 / 1024, -16324.0 + (NR - SO) / 1024))
+    act(cube("hb", 0, VIS, 0, 12), lnT, AF.Identity, 1.0 / 1024, p32)
     PD0, PD1 = new("F", 72), new("F", 72)
     vm(PD0, 1.0)
     vm(r(PD0, 0, 72, 6), 0.0)
+    vm(r(PD0, 1, 72, 6), 0.125)
     vm(r(PD0, 2, 72, 6), -1.0)
-    BI, dm1 = new("B", 128), col(diag, 1.0, -1.0)
-    vt(BI, vcol(I16, -2.0, None, OP.mult, None, "B"), BO, OP.add)
-    for m in range(16):
-        vs(r(SelI, 128 * m, 128 * m + 128), BI, r(dm1, m, m + 1), kk(m), OP.max, OP.min)
+    for x in range(4):
+        o = r(SelI, 512 * x, 512 * x + 512)
+        sel(o, r(Sel, 512 * x, 512 * x + 512), [[0, 4], [1, 128]], 0, -1, -1.0, NE)
+        sel(o, o, [[-1, 4], [1024, 8], [65, 16]], -4 * x, -64, 0.0, NE)
+    k12, twice = new("F", 2), new("U", 2)
+    for x in (0, 1):
+        vt(r(k12, x, x + 1), vcol(kc, 12.0 - 4 * x, -12.0, OP.is_ge, OP.mult), col(kc, 1.0, 4.0 * x), OP.add)
+    act(twice, k12, AF.Identity, 8.0, 7.0)
     TA, TL, TB, TH = [new("B", 128) for i in range(4)]
     sel(TA, nBO, [[1, 128]], 0, -1, 0.0, GT)
     sel(TL, TA, [[1, 128]], 0, -1, 1.0, NE)
     sel(TB, nBO, [[-1, 128]], 0, 1, 0.0, GT)
     sel(TH, TB, [[1, 128]], 0, -1, 1.0, NE)
-    kb1, kb2, pw15, vdb, edb = col(kc, 0.5, 0.5), col(kc, -0.5, 8.0), col(sc0, 32768.0), col(kc, -1.0, SO + DU), col(kc, -1.0, float(DU))
-    c64 = col(r(one, 0, 16), 64.0, 0.0, "B")
+    kb1, kb2, pw15, vdb = col(kc, 0.5, 0.5), col(kc, -0.5, 8.0), col(sc0, 32768.0), col(kc, -1.0, SO + DU)
+    c64 = new("B", 16)
+    vm(c64, 64.0)
     cur[0] = "po"
-    iota(("po_t", 0, RW), [[0, RW]], 0, 0)
-    poF = col(poI)
-    dma(lambda g, T: g.sync.dma_start(out=T.po_t[::16, DU:DU + NR], in_=ap(T, r(poF))), spans(r(poF)), [("po_t", DU, DU + NR, 1)], 1.8)
+    iota(("po_t", DU + NR, VIS * L), [[0, VIS * L]], 0, 0)
+    poF, fan_id = col(poI), ndma[0] + 1
+    dma(lambda g, T: g.sync.dma_start(out=T.po_t[::16, DU:DU + NR], in_=ap(T, r(poF))), spans(r(poF)), [("po_t", DU, DU + NR, 1)], 96)
+
+    def fan(g, T):
+        k = None
+        for i in range(1, 16):
+            k = g.sync.dma_start(out=T.po_t[i::16, DU:DU + NR], in_=T.po_t[::16, DU:DU + NR])
+            if i < 15:
+                k.then_inc(T.sem["d%d" % fan_id], 16)
+        return k
+    dma(fan, [("order", 0, 7, 1)], [("po_t", DU, DU + NR, 1)], 1440, 15)
     cur[0] = "celf"
     for x in (0, 1):
         gcopy(("cel_t", DU + 1024 * x, 1024), ("cel_i", 1024 * x, 1024))
-    h = r(thc, 0, 1)
+    hcol = lambda a, b: cube("hb", 0, 1, a, b)
     celw, celn, recw, recn, pow_ = ("cel_t", 0, CW), ("cel_t", DU, NC), ("rec_t", 0, DU + NR), ("rec_t", DU, NR), ("po_t", 0, DU + NR)
     dfad = [(new("B", 1024), new("B", 1024)) for x in range(6)]
 
@@ -310,15 +334,11 @@ def build(ne):
         mm([(r(q, m, 16 * w, 16), r(mats, 128 * m, 128 * m + 128), src, True, True) for m in range(16)])
         return q
 
-    def first(site, terms, accb, xd):
-        q, sc, win, x, o = place(site, L), new("F", L), new("F", 12), new("F", 12), new("U", 24)
-        mm([(q, a, b, i == 0, False) for i, (a, b) in enumerate(terms)] +
-           [(r(q, m, L, 16), r(Sel, 128 * m, 128 * m + 128), accb, False, m == 15) for m in range(16)])
-        vscan(sc, D2, q, 0.0, OP.mult, OP.max)
-        vs(win, r(sc, 15, L, 16), pw15, None, EQ)
-        vt(x, win, xd, OP.mult)
-        aff("a", r(o, 0, 24, 2), x, 1.0, kc)
-        return o
+    def unsel(q, o, a, kb):
+        if q == "a":
+            act(o, a, AF.Sign, -0.5, kb)
+        else:
+            vs(o, a, 0.5, kb, OP.mult, OP.is_lt)
 
     def send(src, dst_, sem):
         src, dst_ = ref(src), ref(dst_)
@@ -326,63 +346,64 @@ def build(ne):
         def fn(g, T, me, dst, topo):
             rid, pid, se = topo.addr(dst)
             return g.remote_dma(ap(T, dst_), ap(T, src), T.sem[sem], T.sem.ls, pid, rid, topo.mask(me, dst))
-        add("g", fn, spans(src), [(sem + "_sent", 0, 1, 1)], 0.6, "ls", ne)
-        add("net", None, [(sem + "_sent", 0, 1, 1)], spans(dst_), 1.8, sem, ne)
+        add("g", fn, spans(src), [(sem + "_sent", 0, 1, 1)], 0.6, "ls", ne, 0)
+        add("net", None, [(sem + "_sent", 0, 1, 1)], spans(dst_), 2.0, sem, ne, 0)
 
     for t in range(VIS):
         last = t == VIS - 1
         vis[:] = [t]
         cels = celn if t else ("cel_i", 0, NC)
         cur[0] = "h"
-        hm2, h5, hdead = col(h, -0.5, 256.0), col(h, 5.0, 2048.0 + 5 * 1281.0), new("H", 16)
-        act(hdead, bo8, AF.Identity, hm2)
+        h64, hm2, h5, hdead = hcol(24, 25), hcol(25, 26), hcol(26, 27), new("H", 16)
+        aff(ENG["hdead"], hdead, bo8, hm2, 0.0)
         cur[0] = "zrep"
         for k in range(16):
             o = r(("zrep", 0, 16 * L), k, 16 * L, 16)
             if t and k < ZG:
                 gcopy(o, z)
             else:
-                aff("v" if k >= 16 - ZV else "a", o, z)
+                aff("v" if k >= 16 - (0 if t else ZV) else "a", o, z)
         cur[0] = "u"
         uP = place("u", 12)
         msum(uP, [(r(UW, 15 - k, 143 - k), r(z, k, L, 16)) for k in range(16)])
-        uI, u, ma, kp, xx, mf, e = [new("I", 12) for i in range(7)]
+        uI, u, ma, xx, mf, e = [new("I", 12) for i in range(6)]
         cn, c16, e16, me = new("I", 24), new("U", 12), new("U", 12), new("F", 12)
-        c, w = r(cn, 0, 12), r(PD1, 1, 72, 6)
-        aff("a", uI, uP)
+        c, kp, w = r(cn, 0, 12), r(PD1, 0, 72, 6), r(PD1, 1, 72, 6)
+        aff(ENG["uI"], uI, uP)
         vs(u, uI, 4095, None, OP.bitwise_and)
         vs(r(cn, 12, 24), uI, 15, None, OP.bitwise_and)
-        aff("a", w, u, 1.0, 32.0)
+        aff(ENG["w"], w, u, 1.0, 32.0)
         cur[0] = "cell"
-        aff("v", kp, phi, 32.0, 32.0 * 77 * t - 262144.0)
+        aff(ENG["kp"], kp, phi, 32.0, 32.0 * 77 * t - 262144.0)
         vt(ma, phi, u, OP.mult)
         vt(xx, ma, kp, OP.add)
         vs(c, xx, 5, NC - 1, OP.arith_shift_right, OP.bitwise_and)
-        aff("v", c16, c)
+        aff(ENG["c16"], c16, c)
         sc16, se16 = new("U", L), new("U", L)
-        vc(sc16, ind(cels, c16))
+        aff(ENG["sc16"], sc16, ind(cels, c16))
         cur[0] = "ecell"
         vt(me, c, w, OP.mult)
         aff("v", mf, me, 1.0 / 32, 33.0 / 64 - 131072.0)
         vs(e, mf, NC - 1, None, OP.bitwise_and)
-        aff("a", e16, e)
-        act(se16, ind(cels, e16), AF.Copy)
+        aff(ENG["e16"], e16, e)
+        aff(ENG["se16"], se16, ind(cels, e16))
         dc = lambda a, b: r(place("dA", 128), a, b) if b <= 128 else r(place("dB", 64), a - 128, b - 128)
         for s16, dst in ((sc16, dc), (se16, lambda a, b: r(place("de", L), a, b))):
             for ch in range(3):
                 cur[0] = ("cg" if s16 is sc16 else "eg") + str(ch)
                 df, ad = dfad[ch + (0 if s16 is sc16 else 3)]
-                for x in range(0, 1024, GW):
+                cut, cuta = CUT[ch + (0 if s16 is sc16 else 3)]
+                for x, x1 in zip(cut, cut[1:]):
                     y = 1024 * ch + x
-                    vt(r(df, x, x + GW), ind(recn, r(s16, y // 16, (y + GW) // 16)), ("zrep", y, GW), OP.subtract)
-                    act(r(ad, x, x + GW), r(df, x, x + GW), AF.Abs)
+                    vt(r(df, x, x1), ind(recn, r(s16, y // 16, (y + x1 - x) // 16)), ("zrep", y, x1 - x), OP.subtract)
+                for x, x1 in zip(cuta, cuta[1:]):
+                    act(r(ad, x, x1), r(df, x, x1), AF.Abs)
                 msum(dst(64 * ch, 64 * ch + 64), [(r(U, 15 - k, 143 - k), r(ad, k, 1024, 16)) for k in range(16)])
         cur[0] = "early"
-        aff("a", r(PD1, 0, 72, 6), phi, 4.0, -32.0)
-        aff("a", r(PD1, 4, 72, 6), phi, 5.0, -32.0)
-        aff("a", r(PD1, 5, 72, 6), u, 1.0, 32.0)
+        aff(ENG["p5"], r(PD1, 4, 72, 6), phi, 5.0, -32.0)
+        aff(ENG["w2"], r(PD1, 5, 72, 6), u, 1.0, 32.0)
         s16c, cnh, cnd, nL32, nLh = new("H", L), new("H", 24), new("F", 24), new("F", L), new("H", L)
-        aff("a", s16c, sc16, 1.0, -SO)
+        aff(ENG["s16c"], s16c, sc16, 1.0, -SO)
         vt(cnd, cn, cnD, OP.add)
         cur[0] = "E1"
         vt(cnh, cn, cnH, OP.add)
@@ -401,56 +422,58 @@ def build(ne):
                 ms.append((r((bank, L * x, L), 0, 64, p0=64), r(F, 128, L, **pp), r(G, 128, L, **pp), True, True))
             mm(ms)
             for x in (0, 1):
-                act(("Z", 0, 12, 32 * a + 16 * x, 32 * a + 16 * x + 16, 0, 128), (bank, L * x, L), AF.Relu, 512.0, -1535.0)
+                act(cube("pair", 0, 12, 32 * a + 16 * x, 32 * a + 16 * x + 16), (bank, L * x, L), AF.Relu, 512.0, -1535.0)
         cur[0] = "n"
-        aff("a", nL32, r(xP, L, 2 * L), 1.0, SO)
-        aff("a", nLh, r(xP, L, 2 * L))
+        aff(ENG["nL32"], nL32, r(xP, L, 2 * L), 1.0, SO)
+        aff(ENG["nLh"], nLh, r(xP, L, 2 * L))
         cur[0] = "slots"
         a5, q2, sg = new("H", L), new("H", L), new("B", L)
         for a, b in ((0, 128), (128, L)):
-            act(r(q2, a, b), dc(a, b), AF.Relu, -1.0, h)
-            act(r(a5, a, b), dc(a, b), AF.Relu, -1.0, 512.0)
+            act(r(q2, a, b), dc(a, b), AF.Relu, -64.0, h64)
+            act(r(a5, a, b), dc(a, b), AF.Relu, -64.0, 32768.0)
             act(r(sg, a, b), dc(a, b), AF.Sign, 1.0, -512.0)
         cur[0] = "acc"
         sP, pas, q, yy, accS = place("sc", 24), new("B", 24), place("q", 96), new("F", 96), new("B", 96)
         for o, a, b, n in ((r(sP, 0, 16), 0, 128, 16), (r(sP, 16, 24), 64, L, 8)):
-            msum(o, [(nOne, r(hdead, 0, n)), (r(q2, a, b), r(bo3, 0, n)), (r(a5, a, b), r(bo8, 0, n)), (r(sg, a, b), r(hdead, 0, n))])
+            msum(o, [(nOne, r(hdead, 0, n)), (r(q2, a, b), r(bo3, 0, n)), (r(a5, a, b), r(bo1, 0, n)), (r(sg, a, b), r(hdead, 0, n))])
         vt(pas, sP, half, OP.is_ge)
         ms = []
         for b in range(12):
             o = r(q, 8 * b, 8 * b + 8)
-            ms.append((o, ("Z", b, b + 1, 0, 128, 0, 128), r(pas, 8, 16) if b < 4 else r(pas, 0, 8), True, b < 8))
+            ms.append((o, cube("pair", b, b + 1, 0, 128), r(pas, 8, 16) if b < 4 else r(pas, 0, 8), True, b < 8))
             if b >= 8:
-                ms.append((o, ("Z", b - 8, b - 7, 0, 128, 0, 128), r(pas, 16, 24), False, True))
+                ms.append((o, cube("pair", b - 8, b - 7, 0, 128), r(pas, 16, 24), False, True))
         mm(ms)
         vt(yy, q, cmpc, EQ)
         vscan(accS, M8, yy, 0.0, OP.mult, OP.add)
-        acc = r(accS, 7, 96, 8)
+        acc, acc2 = r(accS, 7, 96, 8), new("B", 32)
+        aff(ENG["acc2"], acc2, ind(accS, twice))
+        acc2 = r(acc2, 0, 24)
         cur[0] = "best"
         K, kt, ks, mx, rr, kh, bq = place("K", 2 * L), new("F", 2 * L), new("F", 2 * L), new("F", 24), new("F", 24), new("H", 36), place("best", 36)
-        msum(r(K, 0, L), [(I16, cK), (cI, one), (I64, q2), (sI, s16c)])
-        msum(r(K, L, 2 * L), [(I16, cK), (kI, sg), (nI64, a5), (sI, s16c)])
+        msum(r(K, 0, L), [(I16, cK), (cI, one), (I16, q2), (sI, s16c)])
+        msum(r(K, L, 2 * L), [(I16, cK), (kI, sg), (nI, a5), (sI, s16c)])
         vtr(kt, K)
-        vscan(ks, RS, kt, -1.0e9, OP.min, OP.max)
-        vt(mx, r(ks, 15, 2 * L, 16), TK[t], OP.max)
+        vscan(ks, RS, kt, 0.0, OP.add, OP.max)
+        vt(mx, r(ks, 15, 2 * L, 16), hcol(0, 24), OP.max)
         vs(rr, mx, M4, -M4, OP.add, OP.add)
         vt(r(kh, 0, 24), mx, rr, OP.subtract)
-        aff("a", r(kh, 24, 36), r(mx, 0, 12), 1.0 / 64, 1536.53125)
+        aff(ENG["kD"], r(kh, 24, 36), r(mx, 0, 12), 1.0 / 64, 1536.53125)
         mm([(r(bq, ih, 36, 2), P[ih][x], r(kh, x, 36, 2), x == 0, x == 1) for ih in (0, 1) for x in (0, 1)])
         cur[0] = "near"
         ny16, has, pog, pq = new("U", 12), new("F", 12), new("H", L), place("pos", 12)
-        aff("a", ny16, r(bq, 0, 12), 1.0, SO)
-        act(pog, ind(("po_t", DU, NR + L * (t + 1)), ny16), AF.Identity, 1.0, -2048.0)
+        aff(ENG["ny16"], ny16, r(bq, 0, 12), 1.0, SO)
+        aff(ENG["pog"], pog, ind(("po_t", DU, NR + L * (t + 1)), ny16), 1.0, -2048.0)
         msum(pq, [(r(U1, 15 - k, 143 - k), r(pog, k, L, 16)) for k in range(16)])
-        aff("a", r(PD1, 2, 72, 6), pq)
-        aff("a", r(PD1, 3, 72, 6), r(bq, 24, 36), -5.0 / 1024, h5)
+        aff(ENG["pos"], r(PD1, 2, 72, 6), pq, 1.0, 4.0 * 77 * t - 32768.0 + 32.0)
+        aff(ENG["d5"], r(PD1, 3, 72, 6), r(bq, 24, 36), -5.0 / 1024, h5)
         vs(has, r(bq, 24, 36), 1281.5 * 1024, None, GT)
         cur[0] = "newz"
         zP, rz, zm, zn = place("zP", L), new("B", L), new("B", L), new("B", L)
-        act(rz, ind(("rec_t", DU, NR + L * (t + 1)), ny16), AF.Copy)
-        msum(zP, [(hI, z), (hI, rz)])
-        aff("a", zm, zP, 1.0, 159.75)
-        aff("a", zn, zm, 1.0, -160.0)
+        aff(ENG["rz"], rz, ind(("rec_t", DU, NR + L * (t + 1)), ny16))
+        msum(zP, [(I16, z), (I16, rz)])
+        aff(ENG["zm"], zm, zP, 0.5, 159.75)
+        aff(ENG["zn"], zn, zm, 1.0, -160.0)
         send(zn, zin[t + 1], "rz%d" % (t + 1))
         cur[0] = "phase"
         px, phN, ph2, phL = new("I", 72), new("I", 12), new("H", 12), new("F", L)
@@ -460,37 +483,53 @@ def build(ne):
         if not last:
             send(phN, ("pl%d" % (t + 1), 0, 12), "rp%d" % (t + 1))
         cur[0] = "phL"
-        aff("a", ph2, phN, 1.0, -2048.0)
-        aff("a", phL, spread("lP", Sel, ph2, 12), 1.0, 2048.0)
+        aff(ENG["ph2"], ph2, phN, 1.0, -2048.0)
+        aff(ENG["phL"], phL, spread("lP", Sel, ph2, 12), 1.0, 2048.0)
         if last:
             send(phL, ("pend", 0, L), "rp%d" % VIS)
         else:
             cur[0] = "cnt"
-            aP, aS, aF, aY, aN = place("aP", 12), new("F", 12), new("F", 1), new("F", 1), new("F", 1)
+            aP, aS, aF, aY, aN, hx, hn = place("aP", 12), new("F", 12), new("F", 1), new("F", 1), new("F", 1), new("F", 27), new("F", 27)
             msum(aP, [(r(one, 0, 128), acc)])
             act(aS, aP, AF.Identity, 1.0, 0.0, aF)
             vs(aY, aF, -15.5, M32, OP.add, OP.add)
             vs(aN, aY, M32, aF, OP.subtract, OP.subtract)
-            hn = col(aN, -1.0, r(thc, t + 1, t + 2))
-            act(r(TK[t + 1], 12, 24), TC[t + 1], AF.Identity, 1.0, col(aN, -64.0))
+            aff(ENG["hx"], hx, coef, aN, 0.0)
+            vt(hn, hx, cube("hb", t + 1, t + 2, 0, 27), OP.add)
         cur[0] = "ev"
-        evh, thr, ed, vd = new("H", 24), new("B", 2 * L), new("F", 12), new("F", 12)
-        aff("a", r(evh, 0, 12), e)
-        aff("a", r(evh, 12, 24), r(bq, 12, 24))
-        aff("a", ed, e, 1.0, edb)
-        aff("a", vd, r(bq, 12, 24), 1.0, vdb)
+        evh, thr, evd = new("H", 24), new("B", 2 * L), new("F", 24)
+        aff(ENG["evh0"], r(evh, 0, 12), e, 1.0, -SO)
+        aff(ENG["evh1"], r(evh, 12, 24), r(bq, 12, 24))
+        aff(ENG["evd"], evd, evh, 1.0, vdb)
         act(thr, spread("ev", SelI, evh, 24), AF.Abs)
         cur[0] = "lists"
         tn, on, u24 = new("F", 24), new("F", 24), new("U", 24)
-        vt(r(tn, 0, 12), r(cnd, 0, 12), acc, OP.mult)
-        vt(r(tn, 12, 24), r(cnd, 12, 24), acc, OP.mult)
+        vt(tn, cnd, acc2, OP.mult)
         vt(on, tn, ln24, OP.add)
-        aff("a", u24, on)
+        aff(ENG["u24"], u24, on)
         cw, n16 = r(u24, 0, 12), r(u24, 12, 24)
+        cur[0] = "slote"
+        q2e, sge = new("H", L), new("B", L)
+        if ENG["q2e"] == "a":
+            act(q2e, place("de", L), AF.Relu, -64.0, h64)
+        else:
+            vs(q2e, place("de", L), 64.0, h64, OP.mult, OP.is_lt)
+        act(sge, place("de", L), AF.Sign, 1.0, -512.0)
+        tP, sc, win, wx, ev16 = place("t", 2 * L), new("F", 2 * L), new("F", 24), new("F", 24), new("U", 48)
+        for a, b in ((0, 2),) if JOINT[t] else ((1, 2), (0, 1)):
+            cur[0] = "vic" if a else "win"
+            o = r(tP, L * a, L * b) if b - a == 2 or a else r(place("t2", L))
+            mm([(o, nI, r(thr, L * a, L * b), True, False)] +
+               [(r(o, m, L * (b - a), 16), r(Sel, 128 * m, 128 * m + 128), r(acc2, 12 * a, 12 * b), False, a == 1 and m == 15) for m in range(16)])
+            if a == 0:
+                mm([(r(o, 0, L), nBO, q2e, False, True)])
+            vscan(r(sc, L * a, L * b), r(D2, L * a, L * b), o, 0.0, OP.mult, OP.max)
+            vs(r(win, 12 * a, 12 * b), r(sc, L * a + 15, L * b, 16), pw15, None, EQ)
+            vt(r(wx, 12 * a, 12 * b), r(win, 12 * a, 12 * b), r(evd, 12 * a, 12 * b), OP.mult)
+            aff(ENG["ev16"], r(ev16, 24 * a, 24 * b, 2), r(wx, 12 * a, 12 * b), 1.0, kc)
         cur[0] = "die"
-        v16 = first("t3", [(nI, r(thr, L, 2 * L))], acc, vd)
         for b in range(12):
-            vc(ind(recw, r(v16, 2 * b, 2 * b + 1)), c64)
+            vc(ind(recw, r(ev16, 24 + 2 * b, 25 + 2 * b)), c64)
         cur[0] = "born"
         vc(ind(recw, n16), zn)
         cur[0] = "bpo"
@@ -498,32 +537,26 @@ def build(ne):
         cur[0] = "ent1"
         N1, ch1, mP, DP = new("F", L), new("F", L), place("m1", L), place("D1", L)
         mm([(mP, TL, sg, True, True), (DP, I16, nLh, True, False), (DP, nI, s16c, False, True)])
-        act(N1, mP, AF.Sign, -0.5, kb1)
+        unsel(ENG["N1"], N1, mP, kb1)
         vt(ch1, N1, DP, OP.mult)
         vt(ind(celw, cw), nL32, ch1, OP.subtract)
-        cur[0] = "slote"
-        q2e, sge = new("H", L), new("B", L)
-        act(q2e, place("de", L), AF.Relu, -1.0, h)
-        act(sge, place("de", L), AF.Sign, 1.0, -512.0)
-        cur[0] = "win"
-        ew = first("t2", [(nI, r(thr, 0, L)), (nBO, q2e)], acc, ed)
         cur[0] = "ent2"
         N2, s16e, ch2, mP, DP = new("F", L), new("H", L), new("F", L), place("m2", L), place("D2", L)
         msum(mP, [(TH, sge)])
-        act(N2, mP, AF.Sign, -0.5, kb2)
-        act(s16e, ind(celn, e16), AF.Identity, 1.0, -SO)
+        unsel(ENG["N2"], N2, mP, kb2)
+        aff(ENG["s16e"], s16e, ind(celn, e16), 1.0, -SO)
         msum(DP, [(I16, nLh), (nI, s16e)])
         vt(ch2, N2, DP, OP.mult)
         for b in range(11, -1, -1):
-            vt(ind(celw, r(ew, 2 * b, 2 * b + 1)), r(nL32, 16 * b, 16 * b + 16), r(ch2, 16 * b, 16 * b + 16), OP.subtract)
+            vt(ind(celw, r(ev16, 2 * b, 2 * b + 1)), r(nL32, 16 * b, 16 * b + 16), r(ch2, 16 * b, 16 * b + 16), OP.subtract)
         if not last:
-            h, z, phi = hn, zin[t + 1], ("pl%d" % (t + 1), 0, 12)
+            hcol, z, phi = lambda a, b, hn=hn: r(hn, a, b), zin[t + 1], ("pl%d" % (t + 1), 0, 12)
     cur[0] = "out"
-    dma(lambda g, T: g.sync.dma_start(out=T.ypat[:], in_=T.zend[:]), [("zend", 0, L, 1)], [("ypat", 0, 1, 1)], 1.7)
-    dma(lambda g, T: g.sync.dma_start(out=T.yphi[:], in_=T.pend[::16, :]), [("pend", 0, L, 1)], [("yphi", 0, 1, 1)], 1.7)
-    dma(lambda g, T: g.sync.dma_start(out=T.ypo[:], in_=T.po_t[::16, DU:DU + NR]), [("po_t", DU, DU + NR, 1)], [("ypo", 0, 1, 1)], 2.5)
-    dma(lambda g, T: g.sync.dma_start(out=T.yrec[:], in_=T.rec_t[:, DU:DU + NR]), [("rec_t", DU, DU + NR, 1)], [("yrec", 0, 1, 1)], 4.0)
-    dma(lambda g, T: g.sync.dma_start(out=T.ycel[:], in_=T.cel_t[:, DU:CW]), [("cel_t", DU, CW, 1)], [("ycel", 0, 1, 1)], 5.0)
+    dma(lambda g, T: g.sync.dma_start(out=T.ypat[:], in_=T.zend[:]), [("zend", 0, L, 1)], [("ypat", 0, 1, 1)], 48)
+    dma(lambda g, T: g.sync.dma_start(out=T.yphi[:], in_=T.pend[::16, :]), [("pend", 0, L, 1)], [("yphi", 0, 1, 1)], 10)
+    dma(lambda g, T: g.sync.dma_start(out=T.ypo[:], in_=T.po_t[::16, DU:DU + NR]), [("po_t", DU, DU + NR, 1)], [("ypo", 0, 1, 1)], 96)
+    dma(lambda g, T: g.sync.dma_start(out=T.yrec[:], in_=T.rec_t[:, DU:DU + NR]), [("rec_t", DU, DU + NR, 1)], [("yrec", 0, 1, 1)], 768)
+    dma(lambda g, T: g.sync.dma_start(out=T.ycel[:], in_=T.cel_t[:, DU:CW]), [("cel_t", DU, CW, 1)], [("ycel", 0, 1, 1)], 1024)
     return ops
 
 
@@ -556,52 +589,132 @@ def depend(ops):
     return deps
 
 
-def schedule(ops, deps, bias):
-    n = len(ops)
-    succ = [[] for i in range(n)]
-    for i, d in enumerate(deps):
-        for k in d:
-            succ[k].append(i)
-    qs = [o["q"] for o in ops]
-    lat = lambda k, i: (0.0 if qs[k] == "p" else 0.08) if qs[k] == qs[i] else (0.18 if qs[k] != "net" else 0.3)
-    pr = [0.0] * n
+def sweep(ops, deps, succ, banks):
+    n, qs = len(ops), [o["q"] for o in ops]
+    key = [0.0] * n
     for i in range(n - 1, -1, -1):
-        pr[i] = ops[i]["cost"] + max([lat(i, j) + pr[j] for j in succ[i]] or [0.0])
-    key = [pr[i] + bias.get(ops[i]["tag"], bias.get(ops[i]["tag"].rstrip("012") if ops[i]["tag"][:2] not in ("cg", "eg") else ops[i]["tag"][:3], 0.0)) for i in range(n)]
+        t = ops[i]["tag"]
+        if t == "load":
+            key[i] = 100.0 - i
+        elif t[:-1] in DUE[qs[i]]:
+            key[i] = -DUE[qs[i]][t[:-1]] - 20.0 * int(t[-1]) - 1e-4 * i
+        else:
+            key[i] = ops[i]["cost"] + max([CROSS + key[j] for j in succ[i]] or [-60.0])
     left = [len(d) for d in deps]
-    cand = {q: [] for q in ("v", "a", "p", "g", "s", "net")}
-    for i in range(n):
-        if not left[i]:
-            cand[qs[i]].append(i)
-    banks = [sorted(set(s[0] for s in o["r"] + o["w"] if s[0] in BANKS)) for o in ops]
+    cand = {q: [i for i in range(n) if not left[i] and qs[i] == q] for q in DUE}
     rt, free, order, end, used = [0.0] * n, {}, [], [0.0] * n, {b: {} for b in BANKS}
     while len(order) < n:
-        pick = None
+        best = []
         for q, li in cand.items():
-            if not li:
-                continue
-            f = free.get(q, 0.0) if q != "net" else 0.0
-            at = {}
-            for i in li:
-                at[i] = max([f, rt[i]] + [end[k] + 0.18 for b in banks[i] for o, k in used[b].items() if o != q])
-            s0 = min(at.values())
-            b = max((i for i in li if at[i] <= s0 + 0.06), key=lambda i: (key[i], -i))
-            if pick is None or at[b] < pick[0]:
-                pick = (at[b], b, q)
-        s, i, q = pick
+            if li:
+                at = {i: max([free.get(q, 0.0), rt[i]] + [end[k] + CROSS for b in banks[i] for o, k in used[b].items() if o != q]) for i in li}
+                s0 = min(at.values()) + WIN
+                b = max((i for i in li if at[i] <= s0), key=lambda i: (key[i], -i))
+                if ops[b]["cost"] > 0.4:
+                    b = max((i for i in li if at[i] <= s0 + HOLD), key=lambda i: (key[i], -i))
+                best.append((at[b], b, q))
+        s, i, q = min(best)
         cand[q].remove(i)
-        free[q] = s + (0.1 if q == "s" else ops[i]["cost"])
         end[i] = s + ops[i]["cost"]
+        if q != "net":
+            free[q] = end[i] - (LAT if q == "s" else 0.0)
         order.append(i)
         for b in banks[i]:
-            deps[i] |= {k for o, k in used[b].items() if o != q}
             used[b][q] = i
         for j in succ[i]:
-            rt[j] = max(rt[j], end[i] + lat(i, j))
+            rt[j] = max(rt[j], end[i] + ((0.0 if q == "p" else SAME) if q == qs[j] else (CROSS if q != "net" else 0.3)))
             left[j] -= 1
             if not left[j]:
                 cand[qs[j]].append(j)
-    return order, max(end)
+    return order
+
+
+def improve(ops, deps, succ, banks, order, steps, heat, mean, nm, seed):
+    n, models, sd = len(ops), MODELS[:nm], [seed]
+    qs = [["v", "a", "p", "g", "s", "net"].index(o["q"]) for o in ops]
+    bk = [[3 * BANKS.index(b) for b in x] for x in banks]
+    cost = [[o["cost"] * (m[1] * (1.0, 1.0, m[2], m[3])[o["kind"]] if o["kind"] else 1.0) for o in ops] for m in models]
+    pre = [[[(k, (0.0 if qs[k] == 2 else m[4]) if qs[k] == qs[i] else (0.3 if qs[k] == 5 else m[5])) for k in deps[i]] for i in range(n)] for m in models]
+
+    def rnd():
+        sd[0] = sd[0] * 16807 % 2147483647
+        return sd[0] / 2147483647.0
+
+    def play(order, m, old, p0):
+        cs, cross, pr = cost[m], models[m][5], pre[m]
+        end, why = list(old[0]), list(old[1])
+        last, used = [-1] * 6, [-1] * (3 * len(BANKS))
+        for i in order[:p0]:
+            last[qs[i]] = i
+            for b in bk[i]:
+                used[b + qs[i]] = i
+        free = [0.0 if k < 0 else end[k] - (LAT if q == 4 else 0.0) for q, k in enumerate(last)]
+        free[5], last[5] = 0.0, -1
+        for i in order[p0:]:
+            q = qs[i]
+            s, y = free[q], last[q]
+            for k, l in pr[i]:
+                x = end[k] + l
+                if x > s:
+                    s, y = x, k
+            for b in bk[i]:
+                for o in (0, 1, 2):
+                    k = used[b + o]
+                    if o != q and k >= 0 and end[k] + cross > s:
+                        s, y = end[k] + cross, k
+                used[b + q] = i
+            e = end[i] = s + cs[i]
+            why[i] = y
+            if q < 5:
+                free[q], last[q] = (e if q < 4 else e - LAT), i
+        return end, why
+
+    def value(order, old, p0):
+        runs = [play(order, m, old[m], p0) for m in range(nm)]
+        return sum(m[0] * (max(e) + mean * sum(e) / n) for m, (e, y) in zip(models, runs)), runs
+    now, runs = value(order, [([0.0] * n, [-1] * n)] * nm, 0)
+    best = (sum(m[0] * max(e) for m, (e, y) in zip(models, runs)), order, runs)
+    for it in range(steps):
+        end, why = runs[int(rnd() * nm)]
+        i = end.index(max(end)) if rnd() < 0.7 else int(rnd() * n)
+        arcs = []
+        while why[i] >= 0:
+            if why[i] not in deps[i] and ops[i]["tag"] != "load":
+                arcs.append((why[i], i))
+            i = why[i]
+        if not arcs:
+            continue
+        a, b = arcs[int(rnd() * len(arcs))]
+        pa, pb, far = order.index(a), order.index(b), int(rnd() ** 2 * 5)
+        if rnd() < 0.5:
+            while far and pa > 0:
+                pa -= 1
+                far -= qs[order[pa]] == qs[a]
+            seg, take = order[pa:pb + 1], {b}
+            for x in reversed(seg):
+                if not take.isdisjoint(succ[x]):
+                    take.add(x)
+            if a in take:
+                continue
+            new = order[:pa] + [x for x in seg if x in take] + [x for x in seg if x not in take] + order[pb + 1:]
+        else:
+            while far and pb < n - 1:
+                pb += 1
+                far -= qs[order[pb]] == qs[a]
+            seg, take = order[pa:pb + 1], {a}
+            for x in seg:
+                if not take.isdisjoint(deps[x]):
+                    take.add(x)
+            if b in take:
+                continue
+            new = order[:pa] + [x for x in seg if x not in take] + [x for x in seg if x in take] + order[pb + 1:]
+        v, r = value(new, runs, pa)
+        if v <= now + heat * (1.0 - it / steps) * rnd() ** 2:
+            now, runs, order = v, r, new
+            x = sum(m[0] * max(e) for m, (e, y) in zip(models, runs))
+            if x < best[0]:
+                best = (x, new, runs)
+    return best[1], [max(e) for e, y in best[2]]
 
 
 QSEM = {"v": "sv", "a": "sa", "p": "sp"}
@@ -611,7 +724,19 @@ def plan(ne):
     if "plan" not in CACHE:
         ops = build(ne)
         deps = depend(ops)
-        order, span = schedule(ops, deps, BIAS)
+        succ = [set() for o in ops]
+        for i, d in enumerate(deps):
+            for k in d:
+                succ[k].add(i)
+        banks = [sorted(set(s[0] for s in o["r"] + o["w"] if s[0] in BANKS)) for o in ops]
+        order, span = sweep(ops, deps, succ, banks), None
+        for k, (steps, heat, mean, nm) in enumerate(ROUNDS):
+            order, span = improve(ops, deps, succ, banks, order, steps, heat, mean, nm, k + 1)
+        used = {b: {} for b in BANKS}
+        for i in order:
+            for b in banks[i]:
+                deps[i] = deps[i] | {k for o, k in used[b].items() if o != ops[i]["q"]}
+                used[b][ops[i]["q"]] = i
         CACHE["plan"] = (ops, deps, order, span)
     return CACHE["plan"]
 

@@ -19,27 +19,28 @@ for _k in POOLS:
 BANKS = ["b0", "b1", "b2", "b3", "b4", "b5", "e0", "e1"]
 for _b in BANKS:
     SCRATCH[_b] = ("psum", [128, 512], "float32")
-SITE = {"dA": ("b0", 0), "K": ("b0", 128), "cn": ("b1", 0), "dB": ("b1", 384), "u": ("b1", 448), "aP": ("b1", 464), "pos": ("b1", 480),
-        "de": ("b2", 0), "lP": ("b2", 192), "sc": ("b2", 384), "q": ("b2", 416), "fp": ("b3", 0), "zP": ("b3", 192), "best": ("b3", 384),
-        "ev": ("b4", 0), "t": ("b5", 0), "t2": ("b4", 0), "m1": ("e0", 0), "D1": ("e0", 192), "m2": ("e1", 0), "D2": ("e1", 192)}
+SITE = {"dA": ("b0", 0), "D1": ("b0", 128), "D2": ("b0", 320), "cn": ("b1", 0), "dB": ("b1", 384), "u": ("b1", 448), "aP": ("b1", 464), "ph": ("b1", 480),
+        "de": ("b2", 0), "lP": ("b2", 192), "sc": ("b2", 384), "q": ("b2", 416), "fp": ("b3", 0), "best": ("b3", 384),
+        "K1": ("b4", 0), "ev": ("b4", 0), "win": ("b4", 0), "K2": ("b5", 0), "vic": ("b5", 0), "m1": ("e0", 0), "m2": ("e0", 192), "zP": ("e1", 0)}
 SEMAPHORES = ["sv", "sa", "sp", "sg", "ls"] + ["d%d" % i for i in range(20)] + ["rz%d" % t for t in (1, 2, 3)] + ["rp%d" % t for t in (1, 2, 3)]
 M4, M32 = 50331648.0, 402653184.0
 ZG, ZV = 7, 8
 C1, C2, C3, C4 = [0, 1024], [0, 512, 1024], [0, 512, 768, 1024], [0, 768, 1024]
 CUT = [(C1, C1), (C1, C1), (C3, C3), (C2, C1), (C1, C1), (C4, C4)]
-JOINT = (True, True, False)
-ENG = {k: "a" for k in "kp c16 sc16 se16 hx uI w w2 p5 s16c nL32 nLh ny16 zm zn ph2 phL evh0 evh1 e16 pog rz s16e hdead N1 N2".split()}
-ENG.update({k: "v" for k in "acc2 ev16 evd kD pos d5 q2e u24".split()})
-NS, NP, LAT, BW, SAME, CROSS, WIN, HOLD = 0.85e-3, 0.5e-3, 1.5, 290.0, 0.09, 0.22, 0.06, 0.3
-MODELS = [(1.0, 1.0, 1.0, 1.0, SAME, CROSS), (0.5, 1.3, 1.15, 1.3, 0.08, 0.2), (0.6, 0.97, 0.8, 0.75, 0.11, 0.27)]
-ROUNDS = [(50000, 1.0, 5.0, 1), (40000, 0.6, 2.0, 1), (20000, 0.4, 1.0, 3)]
+ONV = ("kD", "pos", "uI")
+NS, NP, LAT, BW, SAME, CROSS, WIN, HOLD = 0.85e-3, 0.43e-3, 1.5, 340.0, 0.09, 0.22, 0.06, 0.3
+MODELS = [(1.0, 1.0, 1.0, 1.0, SAME, CROSS, 1.0, 1.0, 1.0), (0.5, 1.3, 1.15, 1.3, 0.08, 0.2, 1.2, 1.0, 1.0), (0.6, 0.97, 0.8, 0.75, 0.11, 0.27, 0.75, 1.0, 1.0),
+          (1.0, 1.0, 1.0, 1.0, 0.14, 0.21, 0.8, 0.9, 1.0), (0.7, 1.3, 1.1, 1.25, 0.14, 0.21, 1.0, 1.0, 1.0), (0.8, 0.95, 0.95, 0.95, 0.12, 0.26, 0.85, 1.1, 1.15)]
+SEED, ROUNDS = 9, [(12000, 0.7, 10.0, (0,), 0, 2000), (10000, 0.7, 5.0, (0,), 0, 2000), (8000, 0.3, 1.0, (0, 1, 2), 0, 0), (14000, 1.2, 4.0, (3, 5), 1, 0),
+                   (18000, 0.8, 2.0, (3, 4, 5), 1, 0)]
 DUE = {"a": dict(cell=-12, u=-11.5, zrep=-11, h=-9, cg0=-8, cg1=-7, cg2=-6, ecell=-5.5, slots=-5, early=-4.5, best=-4, near=-3, acc=-3, newz=-2, E1=0, n=1.5,
-                 ent1=2, ev=3, lists=3.5, slote=4, win=4, vic=4, ent2=4.5, eg0=5, eg1=6, eg2=7, cnt=10, phL=12),
-       "v": dict(u=-12.5, cell=-12, E1=-11, ecell=-10.5, zrep=-10, h=-10, best=-1, phase=-0.9, near=-0.8, newz=-0.6, acc=-0.5, cg0=0, cg1=1, cg2=2, early=2.6,
-                 n=2.7, ev=2.8, lists=3, slote=3.3, vic=3.4, win=3.5, ent1=4, eg0=5, eg1=6, eg2=7, cnt=8, phL=8.5, ent2=9.4, die=9.5, born=9.6, bpo=22.5),
-       "p": dict(u=-13, cg0=-5, cg1=-4.5, cg2=-4, best=-3, near=-2.5, acc=-2, newz=-1.5, E1=-1, ev=1, vic=1.5, win=2, eg0=3, eg1=4, eg2=5, ent2=5.5, ent1=6,
-                 cnt=8, phL=9),
+                 ent1=2, ev=3, lists=3.5, slote=4, ent2=4.5, eg0=5, eg1=6, eg2=7, cnt=10, phL=12),
+       "v": dict(u=-12.5, cell=-12, E1=-11, ecell=-10.5, zrep=-10, h=-10, best=-1, newz=-0.6, acc=-0.5, cg0=0, cg1=1, cg2=2, early=2.6, n=2.7, ev=2.8, slote=3.3,
+                 vic=3.4, win=3.5, eg0=5, eg1=6, eg2=7, near=7.2, phase=7.3, lists=7.4, ent1=7.5, cnt=8, phL=8.5, ent2=9.4, die=9.5, born=9.6, bpo=22.5),
+       "p": dict(u=-13, cg0=-5, cg1=-4.5, cg2=-4, best=-3, acc=-2, newz=-1.5, E1=-1, ev=1, vic=1.5, win=2, eg0=3, eg1=4, eg2=5, ent2=5.5, ent1=6, cnt=8, phL=9),
        "g": dict(zrep=-10, phase=0, newz=1, phL=2), "s": dict(out=0), "net": {}}
+CHAIN = ("slots", "best", "acc", "eg0", "eg1", "eg2", "slote", "win", "ev", "E1")
+PULL = [(8.0, CHAIN), (3.0, CHAIN + ("die", "ent2", "vic", "born"))]
 CACHE = {}
 
 
@@ -140,8 +141,8 @@ def build(ne):
             [s for y in (a, scale, bias) for s in spans(y)], spans(o) + spans(acc),
             (0.065 + ncol(o) * 1.55 * NS if x else 0.055 + max(64, ncol(o)) * NS) + (0.02 if acc else 0.0), kind=2 if x else 1)
 
-    def aff(q, o, a, scale=1.0, bias=0.0):
-        if q == "a":
+    def aff(name, o, a, scale=1.0, bias=0.0):
+        if name != "v" and name not in ONV:
             act(o, a, AF.Identity, scale, bias)
         elif scale == 1.0 and bias == 0.0:
             vc(o, a)
@@ -159,7 +160,7 @@ def build(ne):
                 k = g.tensor.matmul(ap(T, o), ap(T, a), ap(T, b), s, e)
             return k
         rd = sorted(set(s for o, a, b, x, e in ms for y in (a, b) for s in spans(y)))
-        add("p", fn, rd, sorted(set(s for m in ms for s in spans(m[0]))), sum(max(min(64, ncol(m[1])), ncol(m[2])) * NP + 0.007 for m in ms) + 0.055)
+        add("p", fn, rd, sorted(set(s for m in ms for s in spans(m[0]))), sum(max(min(64, ncol(m[1])), ncol(m[2])) * NP + 0.012 for m in ms) + 0.055)
 
     def msum(o, terms):
         mm([(o, a, b, i == 0, i == len(terms) - 1) for i, (a, b) in enumerate(terms)])
@@ -185,7 +186,7 @@ def build(ne):
 
     def load(name, o, kb):
         o = ref(o)
-        dma(lambda g, T: g.sync.dma_start(out=ap(T, o), in_=T[name][:]), [("loads", 0, 1, 1)], spans(o) + [("order", ndma[0], ndma[0] + 1, 1)], kb)
+        dma(lambda g, T: g.sync.dma_start(out=ap(T, o), in_=T[name][:]), [], spans(o) + [("order", ndma[0], ndma[0] + 1, 1)], kb)
     load("wt", wI, 10)
     load("pat", z, 48)
     load("phi", r(phI, p1=8), 10)
@@ -213,31 +214,40 @@ def build(ne):
     vs(r(pI, 1, 2), r(pI, 0, 1), 4, None, OP.arith_shift_right)
     vs(r(pI, 2, 3), r(pI, 0, 1), 15, None, OP.bitwise_and)
     vc(pk, pI)
-    pc, gc, kc = r(pk, 0, 1), r(pk, 1, 2), r(pk, 2, 3)
+    pc, gc, kc, pq4 = r(pk, 0, 1), r(pk, 1, 2), r(pk, 2, 3), new("F", 4)
+    iota(r(pq4, 0, 2), [[32, 2]], -16, 1)
+    iota(r(pq4, 2, 3), [[0, 1]], 15, 16)
+    iota(r(pq4, 3, 4), [[0, 1]], -1, 1)
     one, S8, ph16, th16, wc = new("B", L), new("H", 144), new("H", L), new("H", 3), col(wI)
     c15 = col(gc, 16.0, 15.0)
     x128, x144 = r(xF, 0, 128), r(xF, 0, 144)
     UW = vcol(x144, c15, wc, EQ, OP.mult, "B")
-    vs(r(S8, p1=8), r(xF, 0, 144, p1=8), r(col(pc, 16.0, 15.0), p1=8), None, EQ)
+    vs(r(S8, p1=8), r(xF, 0, 144, p1=8), r(pq4, 2, 3, p1=8), None, EQ)
     act(r(ph16, p1=8), r(phI, p1=8), AF.Identity, 1.0, -2048.0)
-    phi, pq = new("I", 12), place("pos", 12)
+    phi, pq = new("I", 12), place("ph", 12)
     msum(pq, [(r(S8, 15 - k, 143 - k, p1=8), r(ph16, k, L, 16, p1=8)) for k in range(16)])
     act(phi, pq, AF.Identity, 1.0, 2048.0)
     U = vcol(x144, c15, None, EQ, None, "B")
     vm(one, 1.0)
-    diag, BO = vcol(r(xF, 0, 16), kc, None, EQ), vcol(yg, gc, None, EQ, None, "B")
+    diag, nBO = vcol(r(xF, 0, 16), kc, None, EQ), vcol(yg, gc, -1.0, EQ, OP.mult, "B")
     kk = lambda j: r(diag, j, j + 1)
     Sel, SelI = new("B", 2048), new("B", 2048)
     for m in range(16):
-        aff("v", r(Sel, 128 * m, 128 * m + 128), BO, kk(m), 0.0)
+        vs(r(Sel, 128 * m, 128 * m + 128), nBO, kk(m), -1.0, OP.mult, OP.mult)
     I16, nI, sI, cI, kI = [vcol(x128, pc, v, EQ, OP.mult, "B") for v in (1.0, -1.0, 2.0 ** -10, -16320.0, -16512.0)]
-    b24, cnH, cnD = new("F", 24), new("F", 24), new("F", 24)
+    b24, cnH, LD0, LD1, ED0, ED1 = new("F", 24), new("F", 24), new("B", 112), new("I", 72), new("F", 96), new("H", 96)
     iota(b24, [[0, 2], [16, 12]], 0, 0)
     ln24 = col(b24, 1.0, kc)
     vm(r(cnH, 0, 12), 0.0)
     act(r(cnH, 12, 24), r(ln24, 0, 12), AF.Identity, 16.0, -SO)
-    act(r(cnD, 0, 12), r(ln24, 0, 12), AF.Identity, -1.0, float(DU))
-    act(r(cnD, 12, 24), r(ln24, 0, 12), AF.Identity, 15.0, float(DU))
+    act(r(LD1, 1, 36, 3), r(ln24, 0, 12), AF.Identity, -1.0, float(DU))
+    act(r(LD1, 37, 72, 3), r(ln24, 0, 12), AF.Identity, 15.0, float(DU))
+    act(r(LD1, 2, 72, 3), ln24)
+    act(r(ED1, 1, 96, 4), b24, AF.Identity, 0.0, col(kc, -1.0, SO + DU))
+    act(r(ED1, 2, 96, 4), b24, AF.Identity, 0.0, kc)
+    act(r(ED1, 3, 96, 4), b24, AF.Identity, 0.0)
+    iota(r(LD0, 0, 72), [[0, 24], [1, 3]], 0, 0)
+    iota(ED0, [[0, 24], [1, 4]], 0, 0)
     iota(i15, [[0, 24], [1, 16]], 0, 0)
     iota(i8, [[0, 12], [1, 8]], 0, 0)
     iota(lnT, [[L, VIS], [32, 6], [0, 2]], 0, 0)
@@ -246,16 +256,15 @@ def build(ne):
     for s in (0, 1):
         sel(r(selS, 128 * s, 128 * s + 128, p1=8), r(one, 0, 128, p1=8), [[-2, 4], [0, 32]], -s, 1, 0.0, EQ)
     act(r(th16, p1=8), r(thI, p1=8))
-    tp, coef = place("t", 39), new("F", 27)
+    tp, coef = place("vic", 39), new("F", 27)
     mm([(r(tp, 36, 39), r(sel8, p1=8), r(th16, p1=8), True, True)] +
        [(r(tp, x, x + 1), r(selS, 128 * (x & 1), 128 * (x & 1) + 128, p1=8), r(th16, x // 12, x // 12 + 1, p1=8), True, True) for x in range(36)])
     act(cube("hb", 0, VIS, 12, 24), r(tp, 0, 36), AF.Identity, 64.0, col(kc, 2.0 ** -10, -16320.0 - 1680.0 / 1024))
-    vm(r(coef, 0, 12), 0.0)
-    vm(r(coef, 12, 25), -64.0)
-    for x, a, b in ((24, 64.0, 0.0), (25, -0.5, 256.0), (26, 5.0, 2048.0 + 5 * 1281.0)):
+    iota(r(coef, 0, 24), [[-64, 2], [0, 12]], 0, 0)
+    iota(r(coef, 24, 26), [[59, 2]], -64, 0)
+    iota(r(coef, 26, 27), [[0, 1]], 1, 0)
+    for x, a, b in ((24, 64.0, 0.0), (25, 5.0, 2048.0 + 5 * 1281.0), (26, -1.0, 512.0)):
         act(cube("hb", 0, VIS, x, x + 1), r(tp, 36, 39), AF.Identity, a, b)
-        if x > 24:
-            vm(r(coef, x, x + 1), -a)
     gI = new("I", 1)
     vs(gI, r(pI, 1, 2), 1, None, OP.bitwise_and)
     oc = col(gI)
@@ -270,33 +279,32 @@ def build(ne):
     act(r(fsb, 0, 1), kk(13), AF.Identity, -1.0 / 512, klt)
     act(r(fsb, 1, 2), f11, AF.Identity, 1.0, kk(12))
     fe, fo, gs, gb = col(fsb, ec), col(fsb, oc), col(kk(12), 1.0 / 512, klt), col(f11, 1.0, kk(13))
-    L16, LA, laneC = new("B", 128), vcol(x128, col(pc, 1.0, -1.0), col(kv, -2.0), EQ, OP.mult, "B"), vcol(xF, col(kk(12), 1.0, kk(13)), None, OP.mult, None, "B")
-    vt(L16, LA, I16, OP.add)
-    i16 = r(i8, 0, 16)
-    bo8, bo1, bo3 = [vcol(i16, gc, v, EQ, OP.mult, "B") for v in (1.0, 1.0 / 64, 3.0 / 64)]
-    half, nOne, nBO = new("F", 24), new("B", 128), vcol(yg, gc, -1.0, EQ, OP.mult, "B")
-    vm(half, 0.0)
-    vm(r(half, 8, 16, p0=64), 1.0e6)
-    vm(r(half, 16, 24, p1=64), 1.0e6)
-    vm(nOne, -1.0)
+    LA = vcol(x128, r(pq4, 3, 4), col(kv, -2.0), EQ, OP.mult, "B")
+    laneC = vcol(xF, col(kk(12), 1.0, kk(13)), None, OP.mult, None, "B")
+    bo8, bo1, bo3 = [vcol(r(i8, 0, 16), gc, v, EQ, OP.mult, "B") for v in (0.5, 1.0 / 64, 3.0 / 64)]
+    half, nOne, c64 = new("F", 24), new("B", 128), new("B", 16)
+    iota(half, [[0, 24]], 0, 0)
+    sel(r(half, 8, 16), r(half, 8, 16), [[0, 8]], 63, -1, 1.0e6, OP.is_ge)
+    sel(r(half, 16, 24), r(half, 16, 24), [[0, 8]], -64, 1, 1.0e6, OP.is_ge)
+    iota(nOne, [[0, 128]], -1, 0)
+    iota(c64, [[0, 16]], 64, 0)
     cmpc, M8 = vcol(i8, gc, 0.5, EQ, OP.max), vcol(i8, 0.5, None, GT, None, "B")
-    cK = col(one, col(kc, -4.0, -4.0), 0.0, "B")
-    RS, D2 = vcol(i15, 0.5, -1.0e9, OP.is_lt, OP.mult, "B"), vcol(i15, 0.5, 2.0, GT, OP.mult, "B")
+    kb1, kb2, pw15 = col(kc, 4.0, 4.0), col(kc, -4.0, 64.0), col(sc0, 32768.0)
+    cK, i16 = vcol(one, kb1, None, OP.mult, None, "B"), r(i15, 0, L)
+    RS, D2 = vcol(i15, 0.5, -1.0e9, OP.is_lt, OP.mult, "B"), vcol(i16, 0.5, 2.0, GT, OP.mult, "B")
+    diagL, M16 = vcol(i16, kc, None, EQ, None, "B"), vcol(i16, 0.5, None, GT, None, "B")
     e10, o10 = col(ec, 1024.0), col(oc, 1024.0)
-    P = [[vcol(x128, pc, e10, EQ, OP.mult, "B"), vcol(x128, col(pc, 1.0, 16.0), e10, EQ, OP.mult, "B")],
-         [vcol(x128, col(pc, 1.0, -16.0), o10, EQ, OP.mult, "B"), vcol(x128, pc, o10, EQ, OP.mult, "B")]]
-    U1 = vcol(x144, c15, kk(0), EQ, OP.mult, "B")
-    p32 = col(oc, 16.0 / 1024, col(kc, 1.0 / 1024, -16324.0 + (NR - SO) / 1024))
-    act(cube("hb", 0, VIS, 0, 12), lnT, AF.Identity, 1.0 / 1024, p32)
+    P = [[vcol(x128, pc, e10, EQ, OP.mult, "B"), vcol(x128, r(pq4, 1, 2), e10, EQ, OP.mult, "B")],
+         [vcol(x128, r(pq4, 0, 1), o10, EQ, OP.mult, "B"), vcol(x128, pc, o10, EQ, OP.mult, "B")]]
+    act(cube("hb", 0, VIS, 0, 12), lnT, AF.Identity, 1.0 / 1024, col(oc, 16.0 / 1024, col(kc, 1.0 / 1024, -16324.0 + (NR - SO) / 1024)))
     PD0, PD1 = new("F", 72), new("F", 72)
-    vm(PD0, 1.0)
-    vm(r(PD0, 0, 72, 6), 0.0)
+    iota(r(PD0, 0, 72, 2), [[0, 12], [-1, 3]], 0, 0)
+    iota(r(PD0, 3, 72, 2), [[0, 35]], 1, 0)
     vm(r(PD0, 1, 72, 6), 0.125)
-    vm(r(PD0, 2, 72, 6), -1.0)
     for x in range(4):
-        o = r(SelI, 512 * x, 512 * x + 512)
-        sel(o, r(Sel, 512 * x, 512 * x + 512), [[0, 4], [1, 128]], 0, -1, -1.0, NE)
-        sel(o, o, [[-1, 4], [1024, 8], [65, 16]], -4 * x, -64, 0.0, NE)
+        sel(r(SelI, 512 * x, 512 * x + 512), r(Sel, 512 * x, 512 * x + 512), [[0, 4], [1, 128]], 0, -1, -1.0, NE)
+    for x in range(8):
+        sel(r(SelI, 16 * x, 2048, 129), r(SelI, 16 * x, 2048, 129), [[-1, 16]], -16 * x, 1, 0.0, NE)
     k12, twice = new("F", 2), new("U", 2)
     for x in (0, 1):
         vt(r(k12, x, x + 1), vcol(kc, 12.0 - 4 * x, -12.0, OP.is_ge, OP.mult), col(kc, 1.0, 4.0 * x), OP.add)
@@ -306,9 +314,6 @@ def build(ne):
     sel(TL, TA, [[1, 128]], 0, -1, 1.0, NE)
     sel(TB, nBO, [[-1, 128]], 0, 1, 0.0, GT)
     sel(TH, TB, [[1, 128]], 0, -1, 1.0, NE)
-    kb1, kb2, pw15, vdb = col(kc, 0.5, 0.5), col(kc, -0.5, 8.0), col(sc0, 32768.0), col(kc, -1.0, SO + DU)
-    c64 = new("B", 16)
-    vm(c64, 64.0)
     cur[0] = "po"
     iota(("po_t", DU + NR, VIS * L), [[0, VIS * L]], 0, 0)
     poF, fan_id = col(poI), ndma[0] + 1
@@ -329,16 +334,8 @@ def build(ne):
     celw, celn, recw, recn, pow_ = ("cel_t", 0, CW), ("cel_t", DU, NC), ("rec_t", 0, DU + NR), ("rec_t", DU, NR), ("po_t", 0, DU + NR)
     dfad = [(new("B", 1024), new("B", 1024)) for x in range(6)]
 
-    def spread(site, mats, src, w):
-        q = place(site, 16 * w)
-        mm([(r(q, m, 16 * w, 16), r(mats, 128 * m, 128 * m + 128), src, True, True) for m in range(16)])
-        return q
-
-    def unsel(q, o, a, kb):
-        if q == "a":
-            act(o, a, AF.Sign, -0.5, kb)
-        else:
-            vs(o, a, 0.5, kb, OP.mult, OP.is_lt)
+    def spread(q, mats, src, start=True, stop=True):
+        return [(r(q, m, None, 16), r(mats, 128 * m, 128 * m + 128), src, start, stop and (start or m == 15)) for m in range(16)]
 
     def send(src, dst_, sem):
         src, dst_ = ref(src), ref(dst_)
@@ -354,8 +351,8 @@ def build(ne):
         vis[:] = [t]
         cels = celn if t else ("cel_i", 0, NC)
         cur[0] = "h"
-        h64, hm2, h5, hdead = hcol(24, 25), hcol(25, 26), hcol(26, 27), new("H", 16)
-        aff(ENG["hdead"], hdead, bo8, hm2, 0.0)
+        h64, h5, hm, hdead = hcol(24, 25), hcol(25, 26), hcol(26, 27), new("H", 16)
+        aff("hdead", hdead, bo8, hm, 0.0)
         cur[0] = "zrep"
         for k in range(16):
             o = r(("zrep", 0, 16 * L), k, 16 * L, 16)
@@ -367,32 +364,31 @@ def build(ne):
         uP = place("u", 12)
         msum(uP, [(r(UW, 15 - k, 143 - k), r(z, k, L, 16)) for k in range(16)])
         uI, u, ma, xx, mf, e = [new("I", 12) for i in range(6)]
-        cn, c16, e16, me = new("I", 24), new("U", 12), new("U", 12), new("F", 12)
+        cn, c16, e16, me = r(LD1, 0, 72, 3), new("U", 12), new("U", 12), new("F", 12)
         c, kp, w = r(cn, 0, 12), r(PD1, 0, 72, 6), r(PD1, 1, 72, 6)
-        aff(ENG["uI"], uI, uP)
+        aff("uI", uI, uP)
         vs(u, uI, 4095, None, OP.bitwise_and)
         vs(r(cn, 12, 24), uI, 15, None, OP.bitwise_and)
-        aff(ENG["w"], w, u, 1.0, 32.0)
+        aff("w", w, u, 1.0, 32.0)
         cur[0] = "cell"
-        aff(ENG["kp"], kp, phi, 32.0, 32.0 * 77 * t - 262144.0)
+        aff("kp", kp, phi, 32.0, 32.0 * 77 * t - 262144.0)
         vt(ma, phi, u, OP.mult)
         vt(xx, ma, kp, OP.add)
         vs(c, xx, 5, NC - 1, OP.arith_shift_right, OP.bitwise_and)
-        aff(ENG["c16"], c16, c)
+        aff("c16", c16, c)
         sc16, se16 = new("U", L), new("U", L)
-        aff(ENG["sc16"], sc16, ind(cels, c16))
+        aff("sc16", sc16, ind(cels, c16))
         cur[0] = "ecell"
         vt(me, c, w, OP.mult)
         aff("v", mf, me, 1.0 / 32, 33.0 / 64 - 131072.0)
         vs(e, mf, NC - 1, None, OP.bitwise_and)
-        aff(ENG["e16"], e16, e)
-        aff(ENG["se16"], se16, ind(cels, e16))
+        aff("e16", e16, e)
+        aff("se16", se16, ind(cels, e16))
         dc = lambda a, b: r(place("dA", 128), a, b) if b <= 128 else r(place("dB", 64), a - 128, b - 128)
-        for s16, dst in ((sc16, dc), (se16, lambda a, b: r(place("de", L), a, b))):
+        for x0, s16, dst in ((0, sc16, dc), (3, se16, lambda a, b: r(place("de", L), a, b))):
             for ch in range(3):
-                cur[0] = ("cg" if s16 is sc16 else "eg") + str(ch)
-                df, ad = dfad[ch + (0 if s16 is sc16 else 3)]
-                cut, cuta = CUT[ch + (0 if s16 is sc16 else 3)]
+                cur[0] = ("eg" if x0 else "cg") + str(ch)
+                (df, ad), (cut, cuta) = dfad[x0 + ch], CUT[x0 + ch]
                 for x, x1 in zip(cut, cut[1:]):
                     y = 1024 * ch + x
                     vt(r(df, x, x1), ind(recn, r(s16, y // 16, (y + x1 - x) // 16)), ("zrep", y, x1 - x), OP.subtract)
@@ -400,16 +396,16 @@ def build(ne):
                     act(r(ad, x, x1), r(df, x, x1), AF.Abs)
                 msum(dst(64 * ch, 64 * ch + 64), [(r(U, 15 - k, 143 - k), r(ad, k, 1024, 16)) for k in range(16)])
         cur[0] = "early"
-        aff(ENG["p5"], r(PD1, 4, 72, 6), phi, 5.0, -32.0)
-        aff(ENG["w2"], r(PD1, 5, 72, 6), u, 1.0, 32.0)
-        s16c, cnh, cnd, nL32, nLh = new("H", L), new("H", 24), new("F", 24), new("F", L), new("H", L)
-        aff(ENG["s16c"], s16c, sc16, 1.0, -SO)
-        vt(cnd, cn, cnD, OP.add)
+        aff("p5", r(PD1, 4, 72, 6), phi, 5.0, -32.0)
+        aff("w2", r(PD1, 5, 72, 6), u, 1.0, 32.0)
+        s16c, cnh, nL32, nLh = new("H", L), new("H", 24), new("F", L), new("H", L)
+        aff("s16c", s16c, sc16, 1.0, -SO)
         cur[0] = "E1"
         vt(cnh, cn, cnH, OP.add)
-        xP, fp, Vh = spread("cn", Sel, cnh, 24), place("fp", L), new("H", L)
+        xP, fp, Vh = place("cn", 2 * L), place("fp", L), new("H", L)
+        mm(spread(xP, Sel, cnh))
         act(Vh, r(xP, 0, L), AF.Identity, scol, b11)
-        msum(fp, [(L16, Vh), (I16, laneC)])
+        msum(fp, [(I16, laneC), (I16, Vh), (LA, Vh)])
         G, Fe, Fo = new("B", L), new("B", L), new("B", L)
         act(G, fp, AF.Identity, gs, gb)
         act(Fe, fp, AF.Identity, r(fe, 0, 1), r(fe, 1, 2))
@@ -424,8 +420,8 @@ def build(ne):
             for x in (0, 1):
                 act(cube("pair", 0, 12, 32 * a + 16 * x, 32 * a + 16 * x + 16), (bank, L * x, L), AF.Relu, 512.0, -1535.0)
         cur[0] = "n"
-        aff(ENG["nL32"], nL32, r(xP, L, 2 * L), 1.0, SO)
-        aff(ENG["nLh"], nLh, r(xP, L, 2 * L))
+        aff("nL32", nL32, r(xP, L, 2 * L), 1.0, SO)
+        aff("nLh", nLh, r(xP, L, 2 * L))
         cur[0] = "slots"
         a5, q2, sg = new("H", L), new("H", L), new("B", L)
         for a, b in ((0, 128), (128, L)):
@@ -446,45 +442,48 @@ def build(ne):
         mm(ms)
         vt(yy, q, cmpc, EQ)
         vscan(accS, M8, yy, 0.0, OP.mult, OP.add)
-        acc, acc2 = r(accS, 7, 96, 8), new("B", 32)
-        aff(ENG["acc2"], acc2, ind(accS, twice))
-        acc2 = r(acc2, 0, 24)
+        acc = r(accS, 7, 96, 8)
         cur[0] = "best"
-        K, kt, ks, mx, rr, kh, bq = place("K", 2 * L), new("F", 2 * L), new("F", 2 * L), new("F", 24), new("F", 24), new("H", 36), place("best", 36)
-        msum(r(K, 0, L), [(I16, cK), (cI, one), (I16, q2), (sI, s16c)])
-        msum(r(K, L, 2 * L), [(I16, cK), (kI, sg), (nI, a5), (sI, s16c)])
-        vtr(kt, K)
+        K1, K2, bq = place("K1", L), place("K2", L), place("best", 36)
+        kt, ks, mx, rr, kh = new("F", 2 * L), new("F", 2 * L), new("F", 24), new("F", 24), new("H", 36)
+        mm([(K1, nI, cK, True, False), (K1, cI, one, False, False), (K2, nI, cK, True, False)])
+        mm([(K1, I16, q2, False, False), (K1, sI, s16c, False, True)])
+        mm([(K2, kI, sg, False, False), (K2, nI, a5, False, False), (K2, sI, s16c, False, True)])
+        vtr(r(kt, 0, L), K1)
+        vtr(r(kt, L, 2 * L), K2)
         vscan(ks, RS, kt, 0.0, OP.add, OP.max)
         vt(mx, r(ks, 15, 2 * L, 16), hcol(0, 24), OP.max)
         vs(rr, mx, M4, -M4, OP.add, OP.add)
         vt(r(kh, 0, 24), mx, rr, OP.subtract)
-        aff(ENG["kD"], r(kh, 24, 36), r(mx, 0, 12), 1.0 / 64, 1536.53125)
+        aff("kD", r(kh, 24, 36), r(mx, 0, 12), 1.0 / 64, 1536.53125)
         mm([(r(bq, ih, 36, 2), P[ih][x], r(kh, x, 36, 2), x == 0, x == 1) for ih in (0, 1) for x in (0, 1)])
         cur[0] = "near"
-        ny16, has, pog, pq = new("U", 12), new("F", 12), new("H", L), place("pos", 12)
-        aff(ENG["ny16"], ny16, r(bq, 0, 12), 1.0, SO)
-        aff(ENG["pog"], pog, ind(("po_t", DU, NR + L * (t + 1)), ny16), 1.0, -2048.0)
-        msum(pq, [(r(U1, 15 - k, 143 - k), r(pog, k, L, 16)) for k in range(16)])
-        aff(ENG["pos"], r(PD1, 2, 72, 6), pq, 1.0, 4.0 * 77 * t - 32768.0 + 32.0)
-        aff(ENG["d5"], r(PD1, 3, 72, 6), r(bq, 24, 36), -5.0 / 1024, h5)
-        vs(has, r(bq, 24, 36), 1281.5 * 1024, None, GT)
+        ny16, has, pog, pos = new("U", 12), new("F", 12), new("F", L), new("F", L)
+        aff("ny16", ny16, r(bq, 0, 12), 1.0, SO)
+        vt(pog, ind(("po_t", DU, NR + L * (t + 1)), ny16), diagL, OP.mult)
+        vscan(pos, M16, pog, 0.0, OP.mult, OP.add)
+        aff("pos", r(PD1, 2, 72, 6), r(pos, 15, L, 16), 1.0, 4.0 * 77 * t - 32768.0 + 32.0 - 2048.0)
+        aff("d5", r(PD1, 3, 72, 6), r(bq, 24, 36), -5.0 / 1024, h5)
+        act(has, r(bq, 24, 36), AF.Sign, 1.0 / 1024, -1281.0)
         cur[0] = "newz"
         zP, rz, zm, zn = place("zP", L), new("B", L), new("B", L), new("B", L)
-        aff(ENG["rz"], rz, ind(("rec_t", DU, NR + L * (t + 1)), ny16))
-        msum(zP, [(I16, z), (I16, rz)])
-        aff(ENG["zm"], zm, zP, 0.5, 159.75)
-        aff(ENG["zn"], zn, zm, 1.0, -160.0)
+        aff("rz", rz, ind(("rec_t", DU, NR + L * (t + 1)), ny16))
+        mm([(zP, I16, z, True, False)])
+        mm([(zP, I16, rz, False, True)])
+        aff("zm", zm, zP, 0.5, 159.75)
+        aff("zn", zn, zm, 1.0, -160.0)
         send(zn, zin[t + 1], "rz%d" % (t + 1))
         cur[0] = "phase"
-        px, phN, ph2, phL = new("I", 72), new("I", 12), new("H", 12), new("F", L)
+        px, phN, ph2, phL, lP = new("I", 72), new("I", 12), new("H", 12), new("F", L), place("lP", L)
         vt(r(PD0, 4, 72, 6), has, acc, OP.mult)
         vscan(px, PD0, PD1, 0.0, OP.mult, OP.add)
         vs(phN, r(px, 5, 72, 6), 4095, None, OP.bitwise_and)
         if not last:
             send(phN, ("pl%d" % (t + 1), 0, 12), "rp%d" % (t + 1))
         cur[0] = "phL"
-        aff(ENG["ph2"], ph2, phN, 1.0, -2048.0)
-        aff(ENG["phL"], phL, spread("lP", Sel, ph2, 12), 1.0, 2048.0)
+        aff("ph2", ph2, phN, 1.0, -2048.0)
+        mm(spread(lP, Sel, ph2))
+        aff("phL", phL, lP, 1.0, 2048.0)
         if last:
             send(phL, ("pend", 0, L), "rp%d" % VIS)
         else:
@@ -494,61 +493,56 @@ def build(ne):
             act(aS, aP, AF.Identity, 1.0, 0.0, aF)
             vs(aY, aF, -15.5, M32, OP.add, OP.add)
             vs(aN, aY, M32, aF, OP.subtract, OP.subtract)
-            aff(ENG["hx"], hx, coef, aN, 0.0)
+            aff("hx", hx, coef, aN, 0.0)
             vt(hn, hx, cube("hb", t + 1, t + 2, 0, 27), OP.add)
         cur[0] = "ev"
-        evh, thr, evd = new("H", 24), new("B", 2 * L), new("F", 24)
-        aff(ENG["evh0"], r(evh, 0, 12), e, 1.0, -SO)
-        aff(ENG["evh1"], r(evh, 12, 24), r(bq, 12, 24))
-        aff(ENG["evd"], evd, evh, 1.0, vdb)
-        act(thr, spread("ev", SelI, evh, 24), AF.Abs)
+        evh, thr, eP = r(ED1, 0, 96, 4), new("B", 2 * L), place("ev", 2 * L)
+        aff("evh0", r(evh, 0, 12), e, 1.0, -SO)
+        aff("evh1", r(evh, 12, 24), r(bq, 12, 24))
+        mm(spread(eP, SelI, evh))
+        act(thr, eP, AF.Abs)
         cur[0] = "lists"
-        tn, on, u24 = new("F", 24), new("F", 24), new("U", 24)
-        vt(tn, cnd, acc2, OP.mult)
-        vt(on, tn, ln24, OP.add)
-        aff(ENG["u24"], u24, on)
+        on, u24 = new("F", 72), new("U", 24)
+        aff("acc2", r(LD0, 2, 98, 3), ind(accS, twice))
+        vscan(on, r(LD0, 0, 72), LD1, 0.0, OP.mult, OP.add)
+        aff("u24", u24, r(on, 2, 72, 3))
         cw, n16 = r(u24, 0, 12), r(u24, 12, 24)
         cur[0] = "slote"
-        q2e, sge = new("H", L), new("B", L)
-        if ENG["q2e"] == "a":
-            act(q2e, place("de", L), AF.Relu, -64.0, h64)
-        else:
-            vs(q2e, place("de", L), 64.0, h64, OP.mult, OP.is_lt)
+        q2e, sge, ev16 = new("H", L), new("B", L), new("U", 96)
+        act(q2e, place("de", L), AF.Relu, -64.0, h64)
         act(sge, place("de", L), AF.Sign, 1.0, -512.0)
-        tP, sc, win, wx, ev16 = place("t", 2 * L), new("F", 2 * L), new("F", 24), new("F", 24), new("U", 48)
-        for a, b in ((0, 2),) if JOINT[t] else ((1, 2), (0, 1)):
+        for a in (1, 0):
             cur[0] = "vic" if a else "win"
-            o = r(tP, L * a, L * b) if b - a == 2 or a else r(place("t2", L))
-            mm([(o, nI, r(thr, L * a, L * b), True, False)] +
-               [(r(o, m, L * (b - a), 16), r(Sel, 128 * m, 128 * m + 128), r(acc2, 12 * a, 12 * b), False, a == 1 and m == 15) for m in range(16)])
+            o, sc = place(cur[0], L), new("F", L)
+            mm([(o, nI, r(thr, L * a, L * a + L), True, False)] + spread(o, Sel, acc, False, a == 1))
             if a == 0:
-                mm([(r(o, 0, L), nBO, q2e, False, True)])
-            vscan(r(sc, L * a, L * b), r(D2, L * a, L * b), o, 0.0, OP.mult, OP.max)
-            vs(r(win, 12 * a, 12 * b), r(sc, L * a + 15, L * b, 16), pw15, None, EQ)
-            vt(r(wx, 12 * a, 12 * b), r(win, 12 * a, 12 * b), r(evd, 12 * a, 12 * b), OP.mult)
-            aff(ENG["ev16"], r(ev16, 24 * a, 24 * b, 2), r(wx, 12 * a, 12 * b), 1.0, kc)
+                mm([(o, nBO, q2e, False, True)])
+            vscan(sc, D2, o, 0.0, OP.mult, OP.max)
+            vs(r(ED0, 48 * a + 2, 48 * a + 48, 4), r(sc, 15, L, 16), pw15, None, EQ)
+            vscan(r(ev16, 48 * a, 48 * a + 48), r(ED0, 48 * a, 48 * a + 48), r(ED1, 48 * a, 48 * a + 48), 0.0, OP.mult, OP.add)
         cur[0] = "die"
         for b in range(12):
-            vc(ind(recw, r(ev16, 24 + 2 * b, 25 + 2 * b)), c64)
+            vc(ind(recw, r(ev16, 50 + 4 * b, 51 + 4 * b)), c64)
         cur[0] = "born"
         vc(ind(recw, n16), zn)
         cur[0] = "bpo"
         vc(ind(pow_, n16), phL)
         cur[0] = "ent1"
         N1, ch1, mP, DP = new("F", L), new("F", L), place("m1", L), place("D1", L)
-        mm([(mP, TL, sg, True, True), (DP, I16, nLh, True, False), (DP, nI, s16c, False, True)])
-        unsel(ENG["N1"], N1, mP, kb1)
+        msum(DP, [(I16, nLh), (nI, s16c)])
+        msum(mP, [(TL, sg)])
+        act(N1, mP, AF.Sign, -4.0, kb1)
         vt(ch1, N1, DP, OP.mult)
         vt(ind(celw, cw), nL32, ch1, OP.subtract)
         cur[0] = "ent2"
         N2, s16e, ch2, mP, DP = new("F", L), new("H", L), new("F", L), place("m2", L), place("D2", L)
         msum(mP, [(TH, sge)])
-        unsel(ENG["N2"], N2, mP, kb2)
-        aff(ENG["s16e"], s16e, ind(celn, e16), 1.0, -SO)
+        act(N2, mP, AF.Sign, -4.0, kb2)
+        aff("s16e", s16e, ind(celn, e16), 1.0, -SO)
         msum(DP, [(I16, nLh), (nI, s16e)])
         vt(ch2, N2, DP, OP.mult)
         for b in range(11, -1, -1):
-            vt(ind(celw, r(ev16, 2 * b, 2 * b + 1)), r(nL32, 16 * b, 16 * b + 16), r(ch2, 16 * b, 16 * b + 16), OP.subtract)
+            vt(ind(celw, r(ev16, 4 * b + 2, 4 * b + 3)), r(nL32, 16 * b, 16 * b + 16), r(ch2, 16 * b, 16 * b + 16), OP.subtract)
         if not last:
             hcol, z, phi = lambda a, b, hn=hn: r(hn, a, b), zin[t + 1], ("pl%d" % (t + 1), 0, 12)
     cur[0] = "out"
@@ -629,16 +623,41 @@ def sweep(ops, deps, succ, banks):
     return order
 
 
-def improve(ops, deps, succ, banks, order, steps, heat, mean, nm, seed):
-    n, models, sd = len(ops), MODELS[:nm], [seed]
-    qs = [["v", "a", "p", "g", "s", "net"].index(o["q"]) for o in ops]
-    bk = [[3 * BANKS.index(b) for b in x] for x in banks]
-    cost = [[o["cost"] * (m[1] * (1.0, 1.0, m[2], m[3])[o["kind"]] if o["kind"] else 1.0) for o in ops] for m in models]
-    pre = [[[(k, (0.0 if qs[k] == 2 else m[4]) if qs[k] == qs[i] else (0.3 if qs[k] == 5 else m[5])) for k in deps[i]] for i in range(n)] for m in models]
+def dice(seed):
+    sd = [seed]
 
     def rnd():
         sd[0] = sd[0] * 16807 % 2147483647
         return sd[0] / 2147483647.0
+    return rnd
+
+
+def move(order, pa, pb, a, b, ahead, deps, succ):
+    seg, take = order[pa:pb + 1], {b if ahead else a}
+    for x in reversed(seg) if ahead else seg:
+        if not take.isdisjoint(succ[x] if ahead else deps[x]):
+            take.add(x)
+    if a in take and b in take:
+        return None
+    return order[:pa] + [x for x in seg if (x in take) == ahead] + [x for x in seg if (x in take) != ahead] + order[pb + 1:]
+
+
+def improve(ops, deps, succ, banks, order, steps, heat, mean, nm, seed, pull=0):
+    n, models, rnd, nm = len(ops), [MODELS[x] for x in nm], dice(seed), len(nm)
+    qs = [["v", "a", "p", "g", "s", "net"].index(o["q"]) for o in ops]
+    bk = [[3 * BANKS.index(b) for b in x] for x in banks]
+    cost = [[o["cost"] * m[1] * (m[8] if o["q"] == "p" else (1.0, 1.0, m[2], m[3])[o["kind"]]) if o["kind"] else LAT + (o["cost"] - LAT) * m[6] if o["q"] == "s" else
+             o["cost"] * m[7] for o in ops] for m in models]
+    pre = [[[(k, (0.0 if qs[k] == 2 else m[4]) if qs[k] == qs[i] else (0.3 if qs[k] == 5 else m[5])) for k in deps[i]] for i in range(n)] for m in models]
+    wt = [PULL[pull][0] if o["tag"][:-1] in PULL[pull][1] else 1.0 for o in ops]
+    wt = [mean * x / sum(wt) for x in wt]
+    name, vis, twin, seen = [], [], {}, {}
+    for o in ops:
+        k = (o["tag"], o["q"])
+        seen[k] = seen.get(k, 0) + 1
+        name.append((o["tag"][:-1], o["q"], seen[k]))
+        vis.append(int(o["tag"][-1]) if o["tag"][-1] in "012" else 9 + 9 * len(name))
+        twin[(name[-1], vis[-1])] = o["i"]
 
     def play(order, m, old, p0):
         cs, cross, pr = cost[m], models[m][5], pre[m]
@@ -671,7 +690,7 @@ def improve(ops, deps, succ, banks, order, steps, heat, mean, nm, seed):
 
     def value(order, old, p0):
         runs = [play(order, m, old[m], p0) for m in range(nm)]
-        return sum(m[0] * (max(e) + mean * sum(e) / n) for m, (e, y) in zip(models, runs)), runs
+        return sum(m[0] * (max(e) + sum(map(lambda a, b: a * b, e, wt))) for m, (e, y) in zip(models, runs)), runs
     now, runs = value(order, [([0.0] * n, [-1] * n)] * nm, 0)
     best = (sum(m[0] * max(e) for m, (e, y) in zip(models, runs)), order, runs)
     for it in range(steps):
@@ -685,36 +704,99 @@ def improve(ops, deps, succ, banks, order, steps, heat, mean, nm, seed):
         if not arcs:
             continue
         a, b = arcs[int(rnd() * len(arcs))]
-        pa, pb, far = order.index(a), order.index(b), int(rnd() ** 2 * 5)
-        if rnd() < 0.5:
-            while far and pa > 0:
-                pa -= 1
-                far -= qs[order[pa]] == qs[a]
-            seg, take = order[pa:pb + 1], {b}
-            for x in reversed(seg):
-                if not take.isdisjoint(succ[x]):
-                    take.add(x)
-            if a in take:
-                continue
-            new = order[:pa] + [x for x in seg if x in take] + [x for x in seg if x not in take] + order[pb + 1:]
-        else:
-            while far and pb < n - 1:
-                pb += 1
-                far -= qs[order[pb]] == qs[a]
-            seg, take = order[pa:pb + 1], {a}
-            for x in seg:
-                if not take.isdisjoint(deps[x]):
-                    take.add(x)
-            if b in take:
-                continue
-            new = order[:pa] + [x for x in seg if x not in take] + [x for x in seg if x in take] + order[pb + 1:]
-        v, r = value(new, runs, pa)
+        far, ahead, new, p0 = int(rnd() ** 2 * 14), rnd() < 0.5, order, n
+        for a, b in [(a, b)] + ([(twin.get((name[a], vis[a] + d)), twin.get((name[b], vis[b] + d))) for d in (-2, -1, 1, 2)] if rnd() < 0.3 else []):
+            if a is not None and b is not None and new.index(a) < new.index(b):
+                pa, pb, f = new.index(a), new.index(b), far
+                while f and (pa > 0 if ahead else pb < n - 1):
+                    pa, pb = (pa - 1, pb) if ahead else (pa, pb + 1)
+                    f -= qs[new[pa if ahead else pb]] == qs[a]
+                x = move(new, pa, pb, a, b, ahead, deps, succ)
+                if x:
+                    new, p0 = x, min(p0, pa)
+        if p0 == n:
+            continue
+        v, r = value(new, runs, p0)
         if v <= now + heat * (1.0 - it / steps) * rnd() ** 2:
             now, runs, order = v, r, new
             x = sum(m[0] * max(e) for m, (e, y) in zip(models, runs))
             if x < best[0]:
                 best = (x, new, runs)
     return best[1], [max(e) for e, y in best[2]]
+
+
+def swaps(ops, deps, succ, banks, order, steps, seed):
+    n, rnd, cost = len(ops), dice(seed), [o["cost"] for o in ops]
+    qs = [["v", "a", "p", "g", "s", "net"].index(o["q"]) for o in ops]
+    res = [([qs[i]] if qs[i] < 5 else []) + [5 + BANKS.index(b) for b in banks[i]] for i in range(n)]
+    lat = lambda k, i: (0.0 if qs[k] == 2 else SAME) if qs[k] == qs[i] else (0.3 if qs[k] == 5 else CROSS)
+    gap = lambda r, k, i: (-LAT if r == 4 else 0.0) if r < 5 or qs[k] == qs[i] else CROSS
+    pre, suc = [[(k, lat(k, i)) for k in deps[i]] for i in range(n)], [[(j, lat(i, j)) for j in succ[i]] for i in range(n)]
+
+    def times(order):
+        head, tail, last = [0.0] * n, [0.0] * n, {}
+        rp, rn = [[] for i in range(n)], [[] for i in range(n)]
+        for i in order:
+            for r in res[i]:
+                if r in last:
+                    rp[i].append((r, last[r], gap(r, last[r], i)))
+                    rn[last[r]].append((r, i, rp[i][-1][2]))
+                last[r] = i
+            head[i] = max([0.0] + [head[k] + cost[k] + l for k, l in pre[i]] + [head[k] + cost[k] + l for r, k, l in rp[i]])
+        for i in reversed(order):
+            tail[i] = cost[i] + max([0.0] + [tail[j] + l for j, l in suc[i]] + [tail[j] + l for r, j, l in rn[i]])
+        return head, tail, rp, rn
+
+    def guess(seq, r, before, after):
+        h, t, inside, top = {}, {}, set(seq), 0.0
+        for k, i in zip(before + seq[:-1] if before else [None] + seq[:-1], seq):
+            h[i] = max([0.0 if k is None else h.get(k, head[k]) + cost[k] + gap(r, k, i)] + [h.get(p, head[p]) + cost[p] + l for p, l in pre[i]] +
+                       [head[p] + cost[p] + l for q, p, l in rp[i] if q != r and p not in inside])
+        for i, k in reversed(list(zip(seq, seq[1:] + (after or [None])))):
+            t[i] = cost[i] + max([0.0 if k is None else t.get(k, tail[k]) + gap(r, i, k)] + [t.get(j, tail[j]) + l for j, l in suc[i]] +
+                                 [tail[j] + l for q, j, l in rn[i] if q != r and j not in inside])
+            top = max(top, h[i] + t[i])
+        return top
+    head, tail, rp, rn = times(order)
+    best, forbid, since = (max(tail), order), {}, 0
+    for it in range(steps):
+        i, runs, cand, rated = tail.index(max(tail)), [], [], []
+        while True:
+            nx = [(r, j) for r, j, l in rn[i] if j not in succ[i] and abs(tail[i] - cost[i] - l - tail[j]) < 1e-9] + \
+                 [(-1, j) for j, l in suc[i] if abs(tail[i] - cost[i] - l - tail[j]) < 1e-9]
+            if not nx:
+                break
+            r, j = nx[int(rnd() * len(nx))]
+            if r >= 0 and runs and runs[-1][0] == r and runs[-1][1][-1] == i:
+                runs[-1][1].append(j)
+            elif r >= 0:
+                runs.append((r, [i, j]))
+            i = j
+        for r, run in runs:
+            for x in range(len(run) - 1 if ops[run[-1]]["tag"] != "load" else 0):
+                for y in sorted(set((x + 1, min(len(run) - 1, x + 1 + int(rnd() * 16)), len(run) - 1 if len(run) - x <= 17 else x + 1))):
+                    cand += [(r, run[x:y + 1], True)] + ([(r, run[x:y + 1], False)] if y > x + 1 else [])
+        for r, part, ahead in cand if len(cand) <= 30 else [cand[int(rnd() * len(cand))] for x in range(30)]:
+            a, b = part[0], part[-1]
+            if (deps[b] if ahead else succ[a]).isdisjoint(part):
+                v = guess([b] + part[:-1] if ahead else part[1:] + [a], r, [k for q, k, l in rp[a] if q == r], [j for q, j, l in rn[b] if q == r])
+                if forbid.get((b, a), -1) < it or v < best[0] - 1e-9:
+                    rated.append((v + 1e-3 * rnd(), a, b, ahead, part))
+        for v, a, b, ahead, part in sorted(rated):
+            new = move(order, order.index(a), order.index(b), a, b, ahead, deps, succ)
+            if new:
+                for x in part[:-1] if ahead else part[1:]:
+                    forbid[(x, b) if ahead else (a, x)] = it + 12 + int(rnd() * 12)
+                order = new
+                break
+        head, tail, rp, rn = times(order)
+        since += 1
+        if max(tail) < best[0] - 1e-9:
+            best, since = (max(tail), order), 0
+        elif since > 1500:
+            order, since, forbid = best[1], 0, {}
+            head, tail, rp, rn = times(order)
+    return best[1]
 
 
 QSEM = {"v": "sv", "a": "sa", "p": "sp"}
@@ -730,8 +812,9 @@ def plan(ne):
                 succ[k].add(i)
         banks = [sorted(set(s[0] for s in o["r"] + o["w"] if s[0] in BANKS)) for o in ops]
         order, span = sweep(ops, deps, succ, banks), None
-        for k, (steps, heat, mean, nm) in enumerate(ROUNDS):
-            order, span = improve(ops, deps, succ, banks, order, steps, heat, mean, nm, k + 1)
+        for k, (steps, heat, mean, nm, pull, more) in enumerate(ROUNDS):
+            order, span = improve(ops, deps, succ, banks, order, steps, heat, mean, nm, SEED + 2 * k, pull)
+            order = swaps(ops, deps, succ, banks, order, more, SEED + 2 * k + 1)
         used = {b: {} for b in BANKS}
         for i in order:
             for b in banks[i]:

from concourse.mybir import AluOpType, AxisListType, ActivationFunctionType

OP = AluOpType
AF = ActivationFunctionType
L, NR, NC, VIS, STEP = 192, 3072, 2048, 3, 3
DU = L
RW, CW = DU + NR + VIS * L, DU + NC
SO = 1664.0
POOLS = {"F": 14000, "I": 2400, "U": 2000, "B": 32000, "H": 7000}
DTN = {"F": "float32", "I": "int32", "U": "uint16", "B": "bfloat16", "H": "float16"}
SCRATCH = {
    "rec_t": ("sbuf", [128, RW], "bfloat16"), "cel_t": ("sbuf", [128, CW], "float32"), "po_t": ("sbuf", [128, RW], "float32"),
    "cel_i": ("sbuf", [128, NC], "int32"), "zrep": ("sbuf", [128, 16 * L], "bfloat16"), "pair": ("sbuf", [128, 12, 128], "bfloat16"),
    "zend": ("sbuf", [128, L], "bfloat16"), "pend": ("sbuf", [128, L], "float32"),
    "hb": ("sbuf", [128, VIS, 32], "float32"), "pl1": ("sbuf", [128, 12], "int32"), "pl2": ("sbuf", [128, 12], "int32"),
}
for _k in POOLS:
    SCRATCH["pool" + _k] = ("sbuf", [128, POOLS[_k]], DTN[_k])
BANKS = ["b0", "b1", "b2", "b3", "b4", "b5", "e0", "e1"]
for _b in BANKS:
    SCRATCH[_b] = ("psum", [128, 512], "float32")
SITE = {"dA": ("b0", 0), "D1": ("b0", 128), "D2": ("b0", 320), "cn": ("b1", 0), "dB": ("b1", 384), "u": ("b1", 448), "aP": ("b1", 464), "ph": ("b1", 480),
        "de": ("b2", 0), "lP": ("b2", 192), "sc": ("b2", 384), "q": ("b2", 416), "fp": ("b3", 0), "best": ("b3", 384),
        "K1": ("b4", 0), "ev": ("b4", 0), "win": ("b4", 0), "K2": ("b5", 0), "vic": ("b5", 0), "m1": ("e0", 0), "m2": ("e0", 192), "zP": ("e1", 0)}
SEMAPHORES = ["sv", "sa", "sp", "sg", "ls"] + ["d%d" % i for i in range(20)] + ["rz%d" % t for t in (1, 2, 3)] + ["rp%d" % t for t in (1, 2, 3)]
M4, M32 = 50331648.0, 402653184.0
ZG, ZV = 7, 8
C1, C2, C3, C4 = [0, 1024], [0, 512, 1024], [0, 512, 768, 1024], [0, 768, 1024]
CUT = [(C1, C1), (C1, C1), (C3, C3), (C2, C1), (C1, C1), (C4, C4)]
ONV = ("kD", "pos", "uI")
NS, NP, LAT, BW, SAME, CROSS, WIN, HOLD = 0.85e-3, 0.43e-3, 1.5, 340.0, 0.09, 0.22, 0.06, 0.3
MODELS = [(1.0, 1.0, 1.0, 1.0, SAME, CROSS, 1.0, 1.0, 1.0), (0.5, 1.3, 1.15, 1.3, 0.08, 0.2, 1.2, 1.0, 1.0), (0.6, 0.97, 0.8, 0.75, 0.11, 0.27, 0.75, 1.0, 1.0),
          (1.0, 1.0, 1.0, 1.0, 0.14, 0.21, 0.8, 0.9, 1.0), (0.7, 1.3, 1.1, 1.25, 0.14, 0.21, 1.0, 1.0, 1.0), (0.8, 0.95, 0.95, 0.95, 0.12, 0.26, 0.85, 1.1, 1.15)]
SEED, ROUNDS = 9, [(12000, 0.7, 10.0, (0,), 0, 2000), (10000, 0.7, 5.0, (0,), 0, 2000), (8000, 0.3, 1.0, (0, 1, 2), 0, 0), (14000, 1.2, 4.0, (3, 5), 1, 0),
                   (18000, 0.8, 2.0, (3, 4, 5), 1, 0)]
DUE = {"a": dict(cell=-12, u=-11.5, zrep=-11, h=-9, cg0=-8, cg1=-7, cg2=-6, ecell=-5.5, slots=-5, early=-4.5, best=-4, near=-3, acc=-3, newz=-2, E1=0, n=1.5,
                 ent1=2, ev=3, lists=3.5, slote=4, ent2=4.5, eg0=5, eg1=6, eg2=7, cnt=10, phL=12),
       "v": dict(u=-12.5, cell=-12, E1=-11, ecell=-10.5, zrep=-10, h=-10, best=-1, newz=-0.6, acc=-0.5, cg0=0, cg1=1, cg2=2, early=2.6, n=2.7, ev=2.8, slote=3.3,
                 vic=3.4, win=3.5, eg0=5, eg1=6, eg2=7, near=7.2, phase=7.3, lists=7.4, ent1=7.5, cnt=8, phL=8.5, ent2=9.4, die=9.5, born=9.6, bpo=22.5),
       "p": dict(u=-13, cg0=-5, cg1=-4.5, cg2=-4, best=-3, acc=-2, newz=-1.5, E1=-1, ev=1, vic=1.5, win=2, eg0=3, eg1=4, eg2=5, ent2=5.5, ent1=6, cnt=8, phL=9),
       "g": dict(zrep=-10, phase=0, newz=1, phL=2), "s": dict(out=0), "net": {}}
CHAIN = ("slots", "best", "acc", "eg0", "eg1", "eg2", "slote", "win", "ev", "E1")
PULL = [(8.0, CHAIN), (3.0, CHAIN + ("die", "ent2", "vic", "born"))]
CACHE = {}


def build(ne):
    ops, top, ndma, cur, vis = [], {k: 0 for k in POOLS}, [0], ["load"], []

    def new(k, w):
        o = top[k]
        top[k] = o + (w + 15) // 16 * 16
        if top[k] > POOLS[k]:
            raise ValueError("pool %s is full" % k)
        return ("pool" + k, o, w)

    def r(t, c0=0, c1=None, st=1, p0=0, p1=128):
        if t[0] == "R":
            return ("R", t[1], t[2] + c0 * t[4], t[3] if c1 is None else t[2] + c1 * t[4], st * t[4], p0, p1)
        return ("R", t[0], t[1] + c0, t[1] + (t[2] if c1 is None else c1), st, p0, p1)

    def ref(x):
        return x if isinstance(x, (int, float)) or x is None or x[0] in ("R", "X", "Z") else r(x)

    def ind(win, off):
        return ("X", ref(win), ref(off))

    def cube(name, a, b, c0, c1):
        return ("Z", a, b, c0, c1, name)

    def place(site, w):
        return (SITE[site][0], SITE[site][1], w)

    def spans(x):
        if x is None or isinstance(x, (int, float)):
            return []
        if x[0] == "X":
            return spans(x[1]) + spans(x[2])
        if x[0] == "Z":
            w = SCRATCH[x[5]][1][2]
            return [(x[5], w * b + x[3], w * b + x[4], 1) for b in range(x[1], x[2])]
        return [(x[1], x[2], x[3], x[4])]

    def ncol(x):
        if x[0] == "Z":
            return (x[2] - x[1]) * (x[4] - x[3])
        return 16 * ncol(x[2]) if x[0] == "X" else (x[3] - x[2] + x[4] - 1) // x[4]

    def ap(T, x):
        if x is None or isinstance(x, (int, float)):
            return x
        if x[0] == "X":
            return ap(T, x[1]).indirect(ap(T, x[2]))
        if x[0] == "Z":
            return T[x[5]][:, x[1], x[3]:x[4]] if x[2] == x[1] + 1 else T[x[5]][:, x[1]:x[2], x[3]:x[4]]
        t = T[x[1]]
        return t[x[5]:x[6], x[2]:x[3]] if x[4] == 1 else t[x[5]:x[6], x[2]:x[3]:x[4]]

    def two(x):
        return x[0] == "R" and x[1] in ("poolB", "poolH", "poolU", "zrep", "rec_t")

    def add(q, fn, reads, writes, cost, sem=None, val=1, kind=1):
        ops.append({"q": q, "fn": fn, "r": reads, "w": writes, "cost": cost, "sem": sem, "val": val, "i": len(ops), "kind": kind,
                    "tag": cur[0] + (str(vis[0]) if vis else "")})

    def vop(fn, o, ins, rate):
        n, kind = ncol(o), 3 if o[0] == "X" else 2 if any(x[0] == "X" for x in ins if isinstance(x, tuple)) else 1
        add("v", fn, [s for x in ins for s in spans(x)] + (spans(o[2]) if kind == 3 else []), spans(o[1] if kind == 3 else o),
            0.05 + n * (3.5 if kind == 3 else 1.55) * NS if kind > 1 else 0.045 + max(64, n * rate) * NS, kind=kind)

    def vt(o, a, b, op):
        o, a, b = ref(o), ref(a), ref(b)
        vop(lambda g, T: g.vector.tensor_tensor(out=ap(T, o), in0=ap(T, a), in1=ap(T, b), op=op), o, [a, b], 1 if a[1] in BANKS or b[1] in BANKS else 2)

    def vs(o, a, s1, s2, op0, op1=None):
        o, a, s1, s2 = ref(o), ref(a), ref(s1), ref(s2)
        ex = {} if op1 is None else {"op1": op1}
        vop(lambda g, T: g.vector.tensor_scalar(out=ap(T, o), in0=ap(T, a), scalar1=ap(T, s1), scalar2=ap(T, s2), op0=op0, **ex),
            o, [a, s1, s2], 0.5 if two(o) and two(a) else 1)

    def vc(o, a):
        o, a = ref(o), ref(a)
        vop(lambda g, T: g.vector.tensor_copy(out=ap(T, o), in_=ap(T, a)), o, [a], 0.5 if two(o) and two(a) else 1)

    def vm(o, v):
        o = ref(o)
        vop(lambda g, T: g.vector.memset(ap(T, o), v), o, [], 0.5 if two(o) else 1)

    def vscan(o, d0, d1, init, o0, o1):
        o, d0, d1 = ref(o), ref(d0), ref(d1)
        vop(lambda g, T: g.vector.tensor_tensor_scan(out=ap(T, o), data0=ap(T, d0), data1=ap(T, d1), initial=init, op0=o0, op1=o1), o, [d0, d1], 1)

    def vtr(o, a):
        o, a = ref(o), ref(a)
        vop(lambda g, T: g.vector.transpose(out=ap(T, o), in_=ap(T, a)), o, [a], 1)

    def act(o, a, f=AF.Identity, scale=1.0, bias=0.0, acc=None):
        o, a, scale, bias, acc = ref(o), ref(a), ref(scale), ref(bias), ref(acc)
        x, ex = a[0] == "X", lambda T: {} if acc is None else {"accum_out": ap(T, acc)}
        add("a", lambda g, T: g.scalar.activation(out=ap(T, o), in_=ap(T, a), func=f, bias=ap(T, bias), scale=ap(T, scale), **ex(T)),
            [s for y in (a, scale, bias) for s in spans(y)], spans(o) + spans(acc),
            (0.065 + ncol(o) * 1.55 * NS if x else 0.055 + max(64, ncol(o)) * NS) + (0.02 if acc else 0.0), kind=2 if x else 1)

    def aff(name, o, a, scale=1.0, bias=0.0):
        if name != "v" and name not in ONV:
            act(o, a, AF.Identity, scale, bias)
        elif scale == 1.0 and bias == 0.0:
            vc(o, a)
        elif scale == 1.0:
            vs(o, a, bias, None, OP.add)
        else:
            vs(o, a, scale, bias, OP.mult, OP.add)

    def mm(ms):
        ms = [(ref(o), ref(a), ref(b), s, e) for o, a, b, s, e in ms]

        def fn(g, T):
            k = None
            for o, a, b, s, e in ms:
                k = g.tensor.matmul(ap(T, o), ap(T, a), ap(T, b), s, e)
            return k
        rd = sorted(set(s for o, a, b, x, e in ms for y in (a, b) for s in spans(y)))
        add("p", fn, rd, sorted(set(s for m in ms for s in spans(m[0]))), sum(max(min(64, ncol(m[1])), ncol(m[2])) * NP + 0.012 for m in ms) + 0.055)

    def msum(o, terms):
        mm([(o, a, b, i == 0, i == len(terms) - 1) for i, (a, b) in enumerate(terms)])

    def iota(o, pat, base, cm):
        o = ref(o)
        ex = {} if o[1] == "poolI" else {"allow_small_or_imprecise_dtypes": True}
        add("g", lambda g, T: g.iota(ap(T, o), pat, base, cm, **ex), [], spans(o), 0.13 + 2 * ncol(o) * NS)

    def sel(o, a, pat, base, cm, fill, cmp_):
        o, a = ref(o), ref(a)
        add("g", lambda g, T: g.affine_select(ap(T, o), ap(T, a), pat, cmp_, fill, base, cm), spans(a), spans(o), 0.17 + 2 * ncol(o) * NS)

    def gcopy(o, a):
        sel(o, a, [[0, ncol(ref(o))]], 1, 0, 0.0, OP.is_gt)

    def dma(fn, reads, writes, kb, n=1):
        add("s", fn, reads, writes, LAT + 0.1 * n + kb / BW, "d%d" % ndma[0], 16 * n, 0)
        ndma[0] += 1

    zin = [("rec_t", DU + NR + L * t, L) for t in range(VIS)] + [("zend", 0, L)]
    z, wI, thI, phI, poI = zin[0], new("I", 1), new("I", 3), new("I", L), new("I", L)

    def load(name, o, kb):
        o = ref(o)
        dma(lambda g, T: g.sync.dma_start(out=ap(T, o), in_=T[name][:]), [], spans(o) + [("order", ndma[0], ndma[0] + 1, 1)], kb)
    load("wt", wI, 10)
    load("pat", z, 48)
    load("phi", r(phI, p1=8), 10)
    load("po", poI, 96)
    load("cel", ("cel_i", 0, NC), 1024)
    load("rec", ("rec_t", DU, NR), 768)
    load("th", r(thI, p1=8), 5)

    cur[0] = "const"

    def col(a, scale=1.0, bias=0.0, k="F"):
        o = new(k, ncol(ref(a)))
        act(o, a, AF.Identity, scale, bias)
        return o

    def vcol(a, s1, s2, op0, op1=None, k="F"):
        o = new(k, ncol(ref(a)))
        vs(o, a, s1, s2, op0, op1)
        return o
    EQ, NE, GT = OP.is_equal, OP.not_equal, OP.is_gt
    pI, pk, xF, yg, i15, i8, lnT = new("I", 3), new("F", 3), new("B", L), new("B", 128), new("B", 2 * L), new("B", 96), new("F", 36)
    iota(r(pI, 0, 1), [[0, 1]], 0, 1)
    iota(xF, [[1, L]], 0, 0)
    iota(yg, [[1, 8], [0, 16]], 0, 0)
    vs(r(pI, 1, 2), r(pI, 0, 1), 4, None, OP.arith_shift_right)
    vs(r(pI, 2, 3), r(pI, 0, 1), 15, None, OP.bitwise_and)
    vc(pk, pI)
    pc, gc, kc, pq4 = r(pk, 0, 1), r(pk, 1, 2), r(pk, 2, 3), new("F", 4)
    iota(r(pq4, 0, 2), [[32, 2]], -16, 1)
    iota(r(pq4, 2, 3), [[0, 1]], 15, 16)
    iota(r(pq4, 3, 4), [[0, 1]], -1, 1)
    one, S8, ph16, th16, wc = new("B", L), new("H", 144), new("H", L), new("H", 3), col(wI)
    c15 = col(gc, 16.0, 15.0)
    x128, x144 = r(xF, 0, 128), r(xF, 0, 144)
    UW = vcol(x144, c15, wc, EQ, OP.mult, "B")
    vs(r(S8, p1=8), r(xF, 0, 144, p1=8), r(pq4, 2, 3, p1=8), None, EQ)
    act(r(ph16, p1=8), r(phI, p1=8), AF.Identity, 1.0, -2048.0)
    phi, pq = new("I", 12), place("ph", 12)
    msum(pq, [(r(S8, 15 - k, 143 - k, p1=8), r(ph16, k, L, 16, p1=8)) for k in range(16)])
    act(phi, pq, AF.Identity, 1.0, 2048.0)
    U = vcol(x144, c15, None, EQ, None, "B")
    vm(one, 1.0)
    diag, nBO = vcol(r(xF, 0, 16), kc, None, EQ), vcol(yg, gc, -1.0, EQ, OP.mult, "B")
    kk = lambda j: r(diag, j, j + 1)
    Sel, SelI = new("B", 2048), new("B", 2048)
    for m in range(16):
        vs(r(Sel, 128 * m, 128 * m + 128), nBO, kk(m), -1.0, OP.mult, OP.mult)
    I16, nI, sI, cI, kI = [vcol(x128, pc, v, EQ, OP.mult, "B") for v in (1.0, -1.0, 2.0 ** -10, -16320.0, -16512.0)]
    b24, cnH, LD0, LD1, ED0, ED1 = new("F", 24), new("F", 24), new("B", 112), new("I", 72), new("F", 96), new("H", 96)
    iota(b24, [[0, 2], [16, 12]], 0, 0)
    ln24 = col(b24, 1.0, kc)
    vm(r(cnH, 0, 12), 0.0)
    act(r(cnH, 12, 24), r(ln24, 0, 12), AF.Identity, 16.0, -SO)
    act(r(LD1, 1, 36, 3), r(ln24, 0, 12), AF.Identity, -1.0, float(DU))
    act(r(LD1, 37, 72, 3), r(ln24, 0, 12), AF.Identity, 15.0, float(DU))
    act(r(LD1, 2, 72, 3), ln24)
    act(r(ED1, 1, 96, 4), b24, AF.Identity, 0.0, col(kc, -1.0, SO + DU))
    act(r(ED1, 2, 96, 4), b24, AF.Identity, 0.0, kc)
    act(r(ED1, 3, 96, 4), b24, AF.Identity, 0.0)
    iota(r(LD0, 0, 72), [[0, 24], [1, 3]], 0, 0)
    iota(ED0, [[0, 24], [1, 4]], 0, 0)
    iota(i15, [[0, 24], [1, 16]], 0, 0)
    iota(i8, [[0, 12], [1, 8]], 0, 0)
    iota(lnT, [[L, VIS], [32, 6], [0, 2]], 0, 0)
    sel8, selS = new("H", 128), new("H", 256)
    vs(r(sel8, p1=8), r(yg, p1=8), r(pc, p1=8), None, EQ)
    for s in (0, 1):
        sel(r(selS, 128 * s, 128 * s + 128, p1=8), r(one, 0, 128, p1=8), [[-2, 4], [0, 32]], -s, 1, 0.0, EQ)
    act(r(th16, p1=8), r(thI, p1=8))
    tp, coef = place("vic", 39), new("F", 27)
    mm([(r(tp, 36, 39), r(sel8, p1=8), r(th16, p1=8), True, True)] +
       [(r(tp, x, x + 1), r(selS, 128 * (x & 1), 128 * (x & 1) + 128, p1=8), r(th16, x // 12, x // 12 + 1, p1=8), True, True) for x in range(36)])
    act(cube("hb", 0, VIS, 12, 24), r(tp, 0, 36), AF.Identity, 64.0, col(kc, 2.0 ** -10, -16320.0 - 1680.0 / 1024))
    iota(r(coef, 0, 24), [[-64, 2], [0, 12]], 0, 0)
    iota(r(coef, 24, 26), [[59, 2]], -64, 0)
    iota(r(coef, 26, 27), [[0, 1]], 1, 0)
    for x, a, b in ((24, 64.0, 0.0), (25, 5.0, 2048.0 + 5 * 1281.0), (26, -1.0, 512.0)):
        act(cube("hb", 0, VIS, x, x + 1), r(tp, 36, 39), AF.Identity, a, b)
    gI = new("I", 1)
    vs(gI, r(pI, 1, 2), 1, None, OP.bitwise_and)
    oc = col(gI)
    ec = col(oc, -1.0, 1.0)
    hv, pw = vcol(r(xF, 0, 16), kc, 0.5, OP.is_ge, OP.max), new("F", 16)
    vscan(pw, hv, hv, 1.0, OP.mult, OP.min)
    sc0 = r(pw, 15, 16)
    klt = vcol(kc, 11.5, None, OP.is_lt)
    kv, scol = vcol(kc, 0.5, klt, GT, OP.mult), col(sc0, klt)
    b11 = col(col(sc0, 0.5, 1024.5), kv)
    f11, fsb = col(kk(11), -2050.0, col(kk(0), 1025.0, col(klt, 1024.5))), new("F", 2)
    act(r(fsb, 0, 1), kk(13), AF.Identity, -1.0 / 512, klt)
    act(r(fsb, 1, 2), f11, AF.Identity, 1.0, kk(12))
    fe, fo, gs, gb = col(fsb, ec), col(fsb, oc), col(kk(12), 1.0 / 512, klt), col(f11, 1.0, kk(13))
    LA = vcol(x128, r(pq4, 3, 4), col(kv, -2.0), EQ, OP.mult, "B")
    laneC = vcol(xF, col(kk(12), 1.0, kk(13)), None, OP.mult, None, "B")
    bo8, bo1, bo3 = [vcol(r(i8, 0, 16), gc, v, EQ, OP.mult, "B") for v in (0.5, 1.0 / 64, 3.0 / 64)]
    half, nOne, c64 = new("F", 24), new("B", 128), new("B", 16)
    iota(half, [[0, 24]], 0, 0)
    sel(r(half, 8, 16), r(half, 8, 16), [[0, 8]], 63, -1, 1.0e6, OP.is_ge)
    sel(r(half, 16, 24), r(half, 16, 24), [[0, 8]], -64, 1, 1.0e6, OP.is_ge)
    iota(nOne, [[0, 128]], -1, 0)
    iota(c64, [[0, 16]], 64, 0)
    cmpc, M8 = vcol(i8, gc, 0.5, EQ, OP.max), vcol(i8, 0.5, None, GT, None, "B")
    kb1, kb2, pw15 = col(kc, 4.0, 4.0), col(kc, -4.0, 64.0), col(sc0, 32768.0)
    cK, i16 = vcol(one, kb1, None, OP.mult, None, "B"), r(i15, 0, L)
    RS, D2 = vcol(i15, 0.5, -1.0e9, OP.is_lt, OP.mult, "B"), vcol(i16, 0.5, 2.0, GT, OP.mult, "B")
    diagL, M16 = vcol(i16, kc, None, EQ, None, "B"), vcol(i16, 0.5, None, GT, None, "B")
    e10, o10 = col(ec, 1024.0), col(oc, 1024.0)
    P = [[vcol(x128, pc, e10, EQ, OP.mult, "B"), vcol(x128, r(pq4, 1, 2), e10, EQ, OP.mult, "B")],
         [vcol(x128, r(pq4, 0, 1), o10, EQ, OP.mult, "B"), vcol(x128, pc, o10, EQ, OP.mult, "B")]]
    act(cube("hb", 0, VIS, 0, 12), lnT, AF.Identity, 1.0 / 1024, col(oc, 16.0 / 1024, col(kc, 1.0 / 1024, -16324.0 + (NR - SO) / 1024)))
    PD0, PD1 = new("F", 72), new("F", 72)
    iota(r(PD0, 0, 72, 2), [[0, 12], [-1, 3]], 0, 0)
    iota(r(PD0, 3, 72, 2), [[0, 35]], 1, 0)
    vm(r(PD0, 1, 72, 6), 0.125)
    for x in range(4):
        sel(r(SelI, 512 * x, 512 * x + 512), r(Sel, 512 * x, 512 * x + 512), [[0, 4], [1, 128]], 0, -1, -1.0, NE)
    for x in range(8):
        sel(r(SelI, 16 * x, 2048, 129), r(SelI, 16 * x, 2048, 129), [[-1, 16]], -16 * x, 1, 0.0, NE)
    k12, twice = new("F", 2), new("U", 2)
    for x in (0, 1):
        vt(r(k12, x, x + 1), vcol(kc, 12.0 - 4 * x, -12.0, OP.is_ge, OP.mult), col(kc, 1.0, 4.0 * x), OP.add)
    act(twice, k12, AF.Identity, 8.0, 7.0)
    TA, TL, TB, TH = [new("B", 128) for i in range(4)]
    sel(TA, nBO, [[1, 128]], 0, -1, 0.0, GT)
    sel(TL, TA, [[1, 128]], 0, -1, 1.0, NE)
    sel(TB, nBO, [[-1, 128]], 0, 1, 0.0, GT)
    sel(TH, TB, [[1, 128]], 0, -1, 1.0, NE)
    cur[0] = "po"
    iota(("po_t", DU + NR, VIS * L), [[0, VIS * L]], 0, 0)
    poF, fan_id = col(poI), ndma[0] + 1
    dma(lambda g, T: g.sync.dma_start(out=T.po_t[::16, DU:DU + NR], in_=ap(T, r(poF))), spans(r(poF)), [("po_t", DU, DU + NR, 1)], 96)

    def fan(g, T):
        k = None
        for i in range(1, 16):
            k = g.sync.dma_start(out=T.po_t[i::16, DU:DU + NR], in_=T.po_t[::16, DU:DU + NR])
            if i < 15:
                k.then_inc(T.sem["d%d" % fan_id], 16)
        return k
    dma(fan, [("order", 0, 7, 1)], [("po_t", DU, DU + NR, 1)], 1440, 15)
    cur[0] = "celf"
    for x in (0, 1):
        gcopy(("cel_t", DU + 1024 * x, 1024), ("cel_i", 1024 * x, 1024))
    hcol = lambda a, b: cube("hb", 0, 1, a, b)
    celw, celn, recw, recn, pow_ = ("cel_t", 0, CW), ("cel_t", DU, NC), ("rec_t", 0, DU + NR), ("rec_t", DU, NR), ("po_t", 0, DU + NR)
    dfad = [(new("B", 1024), new("B", 1024)) for x in range(6)]

    def spread(q, mats, src, start=True, stop=True):
        return [(r(q, m, None, 16), r(mats, 128 * m, 128 * m + 128), src, start, stop and (start or m == 15)) for m in range(16)]

    def send(src, dst_, sem):
        src, dst_ = ref(src), ref(dst_)

        def fn(g, T, me, dst, topo):
            rid, pid, se = topo.addr(dst)
            return g.remote_dma(ap(T, dst_), ap(T, src), T.sem[sem], T.sem.ls, pid, rid, topo.mask(me, dst))
        add("g", fn, spans(src), [(sem + "_sent", 0, 1, 1)], 0.6, "ls", ne, 0)
        add("net", None, [(sem + "_sent", 0, 1, 1)], spans(dst_), 2.0, sem, ne, 0)

    for t in range(VIS):
        last = t == VIS - 1
        vis[:] = [t]
        cels = celn if t else ("cel_i", 0, NC)
        cur[0] = "h"
        h64, h5, hm, hdead = hcol(24, 25), hcol(25, 26), hcol(26, 27), new("H", 16)
        aff("hdead", hdead, bo8, hm, 0.0)
        cur[0] = "zrep"
        for k in range(16):
            o = r(("zrep", 0, 16 * L), k, 16 * L, 16)
            if t and k < ZG:
                gcopy(o, z)
            else:
                aff("v" if k >= 16 - (0 if t else ZV) else "a", o, z)
        cur[0] = "u"
        uP = place("u", 12)
        msum(uP, [(r(UW, 15 - k, 143 - k), r(z, k, L, 16)) for k in range(16)])
        uI, u, ma, xx, mf, e = [new("I", 12) for i in range(6)]
        cn, c16, e16, me = r(LD1, 0, 72, 3), new("U", 12), new("U", 12), new("F", 12)
        c, kp, w = r(cn, 0, 12), r(PD1, 0, 72, 6), r(PD1, 1, 72, 6)
        aff("uI", uI, uP)
        vs(u, uI, 4095, None, OP.bitwise_and)
        vs(r(cn, 12, 24), uI, 15, None, OP.bitwise_and)
        aff("w", w, u, 1.0, 32.0)
        cur[0] = "cell"
        aff("kp", kp, phi, 32.0, 32.0 * 77 * t - 262144.0)
        vt(ma, phi, u, OP.mult)
        vt(xx, ma, kp, OP.add)
        vs(c, xx, 5, NC - 1, OP.arith_shift_right, OP.bitwise_and)
        aff("c16", c16, c)
        sc16, se16 = new("U", L), new("U", L)
        aff("sc16", sc16, ind(cels, c16))
        cur[0] = "ecell"
        vt(me, c, w, OP.mult)
        aff("v", mf, me, 1.0 / 32, 33.0 / 64 - 131072.0)
        vs(e, mf, NC - 1, None, OP.bitwise_and)
        aff("e16", e16, e)
        aff("se16", se16, ind(cels, e16))
        dc = lambda a, b: r(place("dA", 128), a, b) if b <= 128 else r(place("dB", 64), a - 128, b - 128)
        for x0, s16, dst in ((0, sc16, dc), (3, se16, lambda a, b: r(place("de", L), a, b))):
            for ch in range(3):
                cur[0] = ("eg" if x0 else "cg") + str(ch)
                (df, ad), (cut, cuta) = dfad[x0 + ch], CUT[x0 + ch]
                for x, x1 in zip(cut, cut[1:]):
                    y = 1024 * ch + x
                    vt(r(df, x, x1), ind(recn, r(s16, y // 16, (y + x1 - x) // 16)), ("zrep", y, x1 - x), OP.subtract)
                for x, x1 in zip(cuta, cuta[1:]):
                    act(r(ad, x, x1), r(df, x, x1), AF.Abs)
                msum(dst(64 * ch, 64 * ch + 64), [(r(U, 15 - k, 143 - k), r(ad, k, 1024, 16)) for k in range(16)])
        cur[0] = "early"
        aff("p5", r(PD1, 4, 72, 6), phi, 5.0, -32.0)
        aff("w2", r(PD1, 5, 72, 6), u, 1.0, 32.0)
        s16c, cnh, nL32, nLh = new("H", L), new("H", 24), new("F", L), new("H", L)
        aff("s16c", s16c, sc16, 1.0, -SO)
        cur[0] = "E1"
        vt(cnh, cn, cnH, OP.add)
        xP, fp, Vh = place("cn", 2 * L), place("fp", L), new("H", L)
        mm(spread(xP, Sel, cnh))
        act(Vh, r(xP, 0, L), AF.Identity, scol, b11)
        msum(fp, [(I16, laneC), (I16, Vh), (LA, Vh)])
        G, Fe, Fo = new("B", L), new("B", L), new("B", L)
        act(G, fp, AF.Identity, gs, gb)
        act(Fe, fp, AF.Identity, r(fe, 0, 1), r(fe, 1, 2))
        act(Fo, fp, AF.Identity, r(fo, 0, 1), r(fo, 1, 2))
        for a in range(4):
            bank, ms, pp = ("e1", "e0")[a & 1], [], {"p0": 32 * a, "p1": 32 * a + 32}
            for x, F in ((0, Fe), (1, Fo)):
                ms.append((r((bank, L * x, L), 64, L), r(F, 0, 128, **pp), r(G, 64, L, **pp), True, True))
                ms.append((r((bank, L * x, L), 0, 64, p1=64), r(F, 0, 64, **pp), r(G, 0, 64, **pp), True, True))
                ms.append((r((bank, L * x, L), 0, 64, p0=64), r(F, 128, L, **pp), r(G, 128, L, **pp), True, True))
            mm(ms)
            for x in (0, 1):
                act(cube("pair", 0, 12, 32 * a + 16 * x, 32 * a + 16 * x + 16), (bank, L * x, L), AF.Relu, 512.0, -1535.0)
        cur[0] = "n"
        aff("nL32", nL32, r(xP, L, 2 * L), 1.0, SO)
        aff("nLh", nLh, r(xP, L, 2 * L))
        cur[0] = "slots"
        a5, q2, sg = new("H", L), new("H", L), new("B", L)
        for a, b in ((0, 128), (128, L)):
            act(r(q2, a, b), dc(a, b), AF.Relu, -64.0, h64)
            act(r(a5, a, b), dc(a, b), AF.Relu, -64.0, 32768.0)
            act(r(sg, a, b), dc(a, b), AF.Sign, 1.0, -512.0)
        cur[0] = "acc"
        sP, pas, q, yy, accS = place("sc", 24), new("B", 24), place("q", 96), new("F", 96), new("B", 96)
        for o, a, b, n in ((r(sP, 0, 16), 0, 128, 16), (r(sP, 16, 24), 64, L, 8)):
            msum(o, [(nOne, r(hdead, 0, n)), (r(q2, a, b), r(bo3, 0, n)), (r(a5, a, b), r(bo1, 0, n)), (r(sg, a, b), r(hdead, 0, n))])
        vt(pas, sP, half, OP.is_ge)
        ms = []
        for b in range(12):
            o = r(q, 8 * b, 8 * b + 8)
            ms.append((o, cube("pair", b, b + 1, 0, 128), r(pas, 8, 16) if b < 4 else r(pas, 0, 8), True, b < 8))
            if b >= 8:
                ms.append((o, cube("pair", b - 8, b - 7, 0, 128), r(pas, 16, 24), False, True))
        mm(ms)
        vt(yy, q, cmpc, EQ)
        vscan(accS, M8, yy, 0.0, OP.mult, OP.add)
        acc = r(accS, 7, 96, 8)
        cur[0] = "best"
        K1, K2, bq = place("K1", L), place("K2", L), place("best", 36)
        kt, ks, mx, rr, kh = new("F", 2 * L), new("F", 2 * L), new("F", 24), new("F", 24), new("H", 36)
        mm([(K1, nI, cK, True, False), (K1, cI, one, False, False), (K2, nI, cK, True, False)])
        mm([(K1, I16, q2, False, False), (K1, sI, s16c, False, True)])
        mm([(K2, kI, sg, False, False), (K2, nI, a5, False, False), (K2, sI, s16c, False, True)])
        vtr(r(kt, 0, L), K1)
        vtr(r(kt, L, 2 * L), K2)
        vscan(ks, RS, kt, 0.0, OP.add, OP.max)
        vt(mx, r(ks, 15, 2 * L, 16), hcol(0, 24), OP.max)
        vs(rr, mx, M4, -M4, OP.add, OP.add)
        vt(r(kh, 0, 24), mx, rr, OP.subtract)
        aff("kD", r(kh, 24, 36), r(mx, 0, 12), 1.0 / 64, 1536.53125)
        mm([(r(bq, ih, 36, 2), P[ih][x], r(kh, x, 36, 2), x == 0, x == 1) for ih in (0, 1) for x in (0, 1)])
        cur[0] = "near"
        ny16, has, pog, pos = new("U", 12), new("F", 12), new("F", L), new("F", L)
        aff("ny16", ny16, r(bq, 0, 12), 1.0, SO)
        vt(pog, ind(("po_t", DU, NR + L * (t + 1)), ny16), diagL, OP.mult)
        vscan(pos, M16, pog, 0.0, OP.mult, OP.add)
        aff("pos", r(PD1, 2, 72, 6), r(pos, 15, L, 16), 1.0, 4.0 * 77 * t - 32768.0 + 32.0 - 2048.0)
        aff("d5", r(PD1, 3, 72, 6), r(bq, 24, 36), -5.0 / 1024, h5)
        act(has, r(bq, 24, 36), AF.Sign, 1.0 / 1024, -1281.0)
        cur[0] = "newz"
        zP, rz, zm, zn = place("zP", L), new("B", L), new("B", L), new("B", L)
        aff("rz", rz, ind(("rec_t", DU, NR + L * (t + 1)), ny16))
        mm([(zP, I16, z, True, False)])
        mm([(zP, I16, rz, False, True)])
        aff("zm", zm, zP, 0.5, 159.75)
        aff("zn", zn, zm, 1.0, -160.0)
        send(zn, zin[t + 1], "rz%d" % (t + 1))
        cur[0] = "phase"
        px, phN, ph2, phL, lP = new("I", 72), new("I", 12), new("H", 12), new("F", L), place("lP", L)
        vt(r(PD0, 4, 72, 6), has, acc, OP.mult)
        vscan(px, PD0, PD1, 0.0, OP.mult, OP.add)
        vs(phN, r(px, 5, 72, 6), 4095, None, OP.bitwise_and)
        if not last:
            send(phN, ("pl%d" % (t + 1), 0, 12), "rp%d" % (t + 1))
        cur[0] = "phL"
        aff("ph2", ph2, phN, 1.0, -2048.0)
        mm(spread(lP, Sel, ph2))
        aff("phL", phL, lP, 1.0, 2048.0)
        if last:
            send(phL, ("pend", 0, L), "rp%d" % VIS)
        else:
            cur[0] = "cnt"
            aP, aS, aF, aY, aN, hx, hn = place("aP", 12), new("F", 12), new("F", 1), new("F", 1), new("F", 1), new("F", 27), new("F", 27)
            msum(aP, [(r(one, 0, 128), acc)])
            act(aS, aP, AF.Identity, 1.0, 0.0, aF)
            vs(aY, aF, -15.5, M32, OP.add, OP.add)
            vs(aN, aY, M32, aF, OP.subtract, OP.subtract)
            aff("hx", hx, coef, aN, 0.0)
            vt(hn, hx, cube("hb", t + 1, t + 2, 0, 27), OP.add)
        cur[0] = "ev"
        evh, thr, eP = r(ED1, 0, 96, 4), new("B", 2 * L), place("ev", 2 * L)
        aff("evh0", r(evh, 0, 12), e, 1.0, -SO)
        aff("evh1", r(evh, 12, 24), r(bq, 12, 24))
        mm(spread(eP, SelI, evh))
        act(thr, eP, AF.Abs)
        cur[0] = "lists"
        on, u24 = new("F", 72), new("U", 24)
        aff("acc2", r(LD0, 2, 98, 3), ind(accS, twice))
        vscan(on, r(LD0, 0, 72), LD1, 0.0, OP.mult, OP.add)
        aff("u24", u24, r(on, 2, 72, 3))
        cw, n16 = r(u24, 0, 12), r(u24, 12, 24)
        cur[0] = "slote"
        q2e, sge, ev16 = new("H", L), new("B", L), new("U", 96)
        act(q2e, place("de", L), AF.Relu, -64.0, h64)
        act(sge, place("de", L), AF.Sign, 1.0, -512.0)
        for a in (1, 0):
            cur[0] = "vic" if a else "win"
            o, sc = place(cur[0], L), new("F", L)
            mm([(o, nI, r(thr, L * a, L * a + L), True, False)] + spread(o, Sel, acc, False, a == 1))
            if a == 0:
                mm([(o, nBO, q2e, False, True)])
            vscan(sc, D2, o, 0.0, OP.mult, OP.max)
            vs(r(ED0, 48 * a + 2, 48 * a + 48, 4), r(sc, 15, L, 16), pw15, None, EQ)
            vscan(r(ev16, 48 * a, 48 * a + 48), r(ED0, 48 * a, 48 * a + 48), r(ED1, 48 * a, 48 * a + 48), 0.0, OP.mult, OP.add)
        cur[0] = "die"
        for b in range(12):
            vc(ind(recw, r(ev16, 50 + 4 * b, 51 + 4 * b)), c64)
        cur[0] = "born"
        vc(ind(recw, n16), zn)
        cur[0] = "bpo"
        vc(ind(pow_, n16), phL)
        cur[0] = "ent1"
        N1, ch1, mP, DP = new("F", L), new("F", L), place("m1", L), place("D1", L)
        msum(DP, [(I16, nLh), (nI, s16c)])
        msum(mP, [(TL, sg)])
        act(N1, mP, AF.Sign, -4.0, kb1)
        vt(ch1, N1, DP, OP.mult)
        vt(ind(celw, cw), nL32, ch1, OP.subtract)
        cur[0] = "ent2"
        N2, s16e, ch2, mP, DP = new("F", L), new("H", L), new("F", L), place("m2", L), place("D2", L)
        msum(mP, [(TH, sge)])
        act(N2, mP, AF.Sign, -4.0, kb2)
        aff("s16e", s16e, ind(celn, e16), 1.0, -SO)
        msum(DP, [(I16, nLh), (nI, s16e)])
        vt(ch2, N2, DP, OP.mult)
        for b in range(11, -1, -1):
            vt(ind(celw, r(ev16, 4 * b + 2, 4 * b + 3)), r(nL32, 16 * b, 16 * b + 16), r(ch2, 16 * b, 16 * b + 16), OP.subtract)
        if not last:
            hcol, z, phi = lambda a, b, hn=hn: r(hn, a, b), zin[t + 1], ("pl%d" % (t + 1), 0, 12)
    cur[0] = "out"
    dma(lambda g, T: g.sync.dma_start(out=T.ypat[:], in_=T.zend[:]), [("zend", 0, L, 1)], [("ypat", 0, 1, 1)], 48)
    dma(lambda g, T: g.sync.dma_start(out=T.yphi[:], in_=T.pend[::16, :]), [("pend", 0, L, 1)], [("yphi", 0, 1, 1)], 10)
    dma(lambda g, T: g.sync.dma_start(out=T.ypo[:], in_=T.po_t[::16, DU:DU + NR]), [("po_t", DU, DU + NR, 1)], [("ypo", 0, 1, 1)], 96)
    dma(lambda g, T: g.sync.dma_start(out=T.yrec[:], in_=T.rec_t[:, DU:DU + NR]), [("rec_t", DU, DU + NR, 1)], [("yrec", 0, 1, 1)], 768)
    dma(lambda g, T: g.sync.dma_start(out=T.ycel[:], in_=T.cel_t[:, DU:CW]), [("cel_t", DU, CW, 1)], [("ycel", 0, 1, 1)], 1024)
    return ops


def meet(a, b, s, lo, hi, st):
    if a >= hi or lo >= b:
        return False
    if s == 1 and st == 1:
        return True
    if s < st:
        a, b, s, lo, hi, st = lo, hi, st, a, b, s
    return any(lo <= x < hi and (x - lo) % st == 0 for x in range(a, b, s))


def depend(ops):
    hist, deps = {}, []
    for o in ops:
        d = set()
        acc = [(s, False) for s in o["r"]] + [(s, True) for s in o["w"]]
        for (buf, lo, hi, st), wr in acc:
            for (k, a, b, s, w) in hist.get(buf, []):
                if (w or wr) and meet(a, b, s, lo, hi, st):
                    d.add(k)
        for (buf, lo, hi, st), wr in acc:
            hh = hist.setdefault(buf, [])
            if wr:
                hist[buf] = hh = [x for x in hh if not (lo <= x[1] and x[2] <= hi + st - 1 and (st == 1 or (x[3] % st == 0 and (x[1] - lo) % st == 0)))]
            hh.append((o["i"], lo, hi, st, wr))
        d.discard(o["i"])
        deps.append(d)
    return deps


def sweep(ops, deps, succ, banks):
    n, qs = len(ops), [o["q"] for o in ops]
    key = [0.0] * n
    for i in range(n - 1, -1, -1):
        t = ops[i]["tag"]
        if t == "load":
            key[i] = 100.0 - i
        elif t[:-1] in DUE[qs[i]]:
            key[i] = -DUE[qs[i]][t[:-1]] - 20.0 * int(t[-1]) - 1e-4 * i
        else:
            key[i] = ops[i]["cost"] + max([CROSS + key[j] for j in succ[i]] or [-60.0])
    left = [len(d) for d in deps]
    cand = {q: [i for i in range(n) if not left[i] and qs[i] == q] for q in DUE}
    rt, free, order, end, used = [0.0] * n, {}, [], [0.0] * n, {b: {} for b in BANKS}
    while len(order) < n:
        best = []
        for q, li in cand.items():
            if li:
                at = {i: max([free.get(q, 0.0), rt[i]] + [end[k] + CROSS for b in banks[i] for o, k in used[b].items() if o != q]) for i in li}
                s0 = min(at.values()) + WIN
                b = max((i for i in li if at[i] <= s0), key=lambda i: (key[i], -i))
                if ops[b]["cost"] > 0.4:
                    b = max((i for i in li if at[i] <= s0 + HOLD), key=lambda i: (key[i], -i))
                best.append((at[b], b, q))
        s, i, q = min(best)
        cand[q].remove(i)
        end[i] = s + ops[i]["cost"]
        if q != "net":
            free[q] = end[i] - (LAT if q == "s" else 0.0)
        order.append(i)
        for b in banks[i]:
            used[b][q] = i
        for j in succ[i]:
            rt[j] = max(rt[j], end[i] + ((0.0 if q == "p" else SAME) if q == qs[j] else (CROSS if q != "net" else 0.3)))
            left[j] -= 1
            if not left[j]:
                cand[qs[j]].append(j)
    return order


def dice(seed):
    sd = [seed]

    def rnd():
        sd[0] = sd[0] * 16807 % 2147483647
        return sd[0] / 2147483647.0
    return rnd


def move(order, pa, pb, a, b, ahead, deps, succ):
    seg, take = order[pa:pb + 1], {b if ahead else a}
    for x in reversed(seg) if ahead else seg:
        if not take.isdisjoint(succ[x] if ahead else deps[x]):
            take.add(x)
    if a in take and b in take:
        return None
    return order[:pa] + [x for x in seg if (x in take) == ahead] + [x for x in seg if (x in take) != ahead] + order[pb + 1:]


def improve(ops, deps, succ, banks, order, steps, heat, mean, nm, seed, pull=0):
    n, models, rnd, nm = len(ops), [MODELS[x] for x in nm], dice(seed), len(nm)
    qs = [["v", "a", "p", "g", "s", "net"].index(o["q"]) for o in ops]
    bk = [[3 * BANKS.index(b) for b in x] for x in banks]
    cost = [[o["cost"] * m[1] * (m[8] if o["q"] == "p" else (1.0, 1.0, m[2], m[3])[o["kind"]]) if o["kind"] else LAT + (o["cost"] - LAT) * m[6] if o["q"] == "s" else
             o["cost"] * m[7] for o in ops] for m in models]
    pre = [[[(k, (0.0 if qs[k] == 2 else m[4]) if qs[k] == qs[i] else (0.3 if qs[k] == 5 else m[5])) for k in deps[i]] for i in range(n)] for m in models]
    wt = [PULL[pull][0] if o["tag"][:-1] in PULL[pull][1] else 1.0 for o in ops]
    wt = [mean * x / sum(wt) for x in wt]
    name, vis, twin, seen = [], [], {}, {}
    for o in ops:
        k = (o["tag"], o["q"])
        seen[k] = seen.get(k, 0) + 1
        name.append((o["tag"][:-1], o["q"], seen[k]))
        vis.append(int(o["tag"][-1]) if o["tag"][-1] in "012" else 9 + 9 * len(name))
        twin[(name[-1], vis[-1])] = o["i"]

    def play(order, m, old, p0):
        cs, cross, pr = cost[m], models[m][5], pre[m]
        end, why = list(old[0]), list(old[1])
        last, used = [-1] * 6, [-1] * (3 * len(BANKS))
        for i in order[:p0]:
            last[qs[i]] = i
            for b in bk[i]:
                used[b + qs[i]] = i
        free = [0.0 if k < 0 else end[k] - (LAT if q == 4 else 0.0) for q, k in enumerate(last)]
        free[5], last[5] = 0.0, -1
        for i in order[p0:]:
            q = qs[i]
            s, y = free[q], last[q]
            for k, l in pr[i]:
                x = end[k] + l
                if x > s:
                    s, y = x, k
            for b in bk[i]:
                for o in (0, 1, 2):
                    k = used[b + o]
                    if o != q and k >= 0 and end[k] + cross > s:
                        s, y = end[k] + cross, k
                used[b + q] = i
            e = end[i] = s + cs[i]
            why[i] = y
            if q < 5:
                free[q], last[q] = (e if q < 4 else e - LAT), i
        return end, why

    def value(order, old, p0):
        runs = [play(order, m, old[m], p0) for m in range(nm)]
        return sum(m[0] * (max(e) + sum(map(lambda a, b: a * b, e, wt))) for m, (e, y) in zip(models, runs)), runs
    now, runs = value(order, [([0.0] * n, [-1] * n)] * nm, 0)
    best = (sum(m[0] * max(e) for m, (e, y) in zip(models, runs)), order, runs)
    for it in range(steps):
        end, why = runs[int(rnd() * nm)]
        i = end.index(max(end)) if rnd() < 0.7 else int(rnd() * n)
        arcs = []
        while why[i] >= 0:
            if why[i] not in deps[i] and ops[i]["tag"] != "load":
                arcs.append((why[i], i))
            i = why[i]
        if not arcs:
            continue
        a, b = arcs[int(rnd() * len(arcs))]
        far, ahead, new, p0 = int(rnd() ** 2 * 14), rnd() < 0.5, order, n
        for a, b in [(a, b)] + ([(twin.get((name[a], vis[a] + d)), twin.get((name[b], vis[b] + d))) for d in (-2, -1, 1, 2)] if rnd() < 0.3 else []):
            if a is not None and b is not None and new.index(a) < new.index(b):
                pa, pb, f = new.index(a), new.index(b), far
                while f and (pa > 0 if ahead else pb < n - 1):
                    pa, pb = (pa - 1, pb) if ahead else (pa, pb + 1)
                    f -= qs[new[pa if ahead else pb]] == qs[a]
                x = move(new, pa, pb, a, b, ahead, deps, succ)
                if x:
                    new, p0 = x, min(p0, pa)
        if p0 == n:
            continue
        v, r = value(new, runs, p0)
        if v <= now + heat * (1.0 - it / steps) * rnd() ** 2:
            now, runs, order = v, r, new
            x = sum(m[0] * max(e) for m, (e, y) in zip(models, runs))
            if x < best[0]:
                best = (x, new, runs)
    return best[1], [max(e) for e, y in best[2]]


def swaps(ops, deps, succ, banks, order, steps, seed):
    n, rnd, cost = len(ops), dice(seed), [o["cost"] for o in ops]
    qs = [["v", "a", "p", "g", "s", "net"].index(o["q"]) for o in ops]
    res = [([qs[i]] if qs[i] < 5 else []) + [5 + BANKS.index(b) for b in banks[i]] for i in range(n)]
    lat = lambda k, i: (0.0 if qs[k] == 2 else SAME) if qs[k] == qs[i] else (0.3 if qs[k] == 5 else CROSS)
    gap = lambda r, k, i: (-LAT if r == 4 else 0.0) if r < 5 or qs[k] == qs[i] else CROSS
    pre, suc = [[(k, lat(k, i)) for k in deps[i]] for i in range(n)], [[(j, lat(i, j)) for j in succ[i]] for i in range(n)]

    def times(order):
        head, tail, last = [0.0] * n, [0.0] * n, {}
        rp, rn = [[] for i in range(n)], [[] for i in range(n)]
        for i in order:
            for r in res[i]:
                if r in last:
                    rp[i].append((r, last[r], gap(r, last[r], i)))
                    rn[last[r]].append((r, i, rp[i][-1][2]))
                last[r] = i
            head[i] = max([0.0] + [head[k] + cost[k] + l for k, l in pre[i]] + [head[k] + cost[k] + l for r, k, l in rp[i]])
        for i in reversed(order):
            tail[i] = cost[i] + max([0.0] + [tail[j] + l for j, l in suc[i]] + [tail[j] + l for r, j, l in rn[i]])
        return head, tail, rp, rn

    def guess(seq, r, before, after):
        h, t, inside, top = {}, {}, set(seq), 0.0
        for k, i in zip(before + seq[:-1] if before else [None] + seq[:-1], seq):
            h[i] = max([0.0 if k is None else h.get(k, head[k]) + cost[k] + gap(r, k, i)] + [h.get(p, head[p]) + cost[p] + l for p, l in pre[i]] +
                       [head[p] + cost[p] + l for q, p, l in rp[i] if q != r and p not in inside])
        for i, k in reversed(list(zip(seq, seq[1:] + (after or [None])))):
            t[i] = cost[i] + max([0.0 if k is None else t.get(k, tail[k]) + gap(r, i, k)] + [t.get(j, tail[j]) + l for j, l in suc[i]] +
                                 [tail[j] + l for q, j, l in rn[i] if q != r and j not in inside])
            top = max(top, h[i] + t[i])
        return top
    head, tail, rp, rn = times(order)
    best, forbid, since = (max(tail), order), {}, 0
    for it in range(steps):
        i, runs, cand, rated = tail.index(max(tail)), [], [], []
        while True:
            nx = [(r, j) for r, j, l in rn[i] if j not in succ[i] and abs(tail[i] - cost[i] - l - tail[j]) < 1e-9] + \
                 [(-1, j) for j, l in suc[i] if abs(tail[i] - cost[i] - l - tail[j]) < 1e-9]
            if not nx:
                break
            r, j = nx[int(rnd() * len(nx))]
            if r >= 0 and runs and runs[-1][0] == r and runs[-1][1][-1] == i:
                runs[-1][1].append(j)
            elif r >= 0:
                runs.append((r, [i, j]))
            i = j
        for r, run in runs:
            for x in range(len(run) - 1 if ops[run[-1]]["tag"] != "load" else 0):
                for y in sorted(set((x + 1, min(len(run) - 1, x + 1 + int(rnd() * 16)), len(run) - 1 if len(run) - x <= 17 else x + 1))):
                    cand += [(r, run[x:y + 1], True)] + ([(r, run[x:y + 1], False)] if y > x + 1 else [])
        for r, part, ahead in cand if len(cand) <= 30 else [cand[int(rnd() * len(cand))] for x in range(30)]:
            a, b = part[0], part[-1]
            if (deps[b] if ahead else succ[a]).isdisjoint(part):
                v = guess([b] + part[:-1] if ahead else part[1:] + [a], r, [k for q, k, l in rp[a] if q == r], [j for q, j, l in rn[b] if q == r])
                if forbid.get((b, a), -1) < it or v < best[0] - 1e-9:
                    rated.append((v + 1e-3 * rnd(), a, b, ahead, part))
        for v, a, b, ahead, part in sorted(rated):
            new = move(order, order.index(a), order.index(b), a, b, ahead, deps, succ)
            if new:
                for x in part[:-1] if ahead else part[1:]:
                    forbid[(x, b) if ahead else (a, x)] = it + 12 + int(rnd() * 12)
                order = new
                break
        head, tail, rp, rn = times(order)
        since += 1
        if max(tail) < best[0] - 1e-9:
            best, since = (max(tail), order), 0
        elif since > 1500:
            order, since, forbid = best[1], 0, {}
            head, tail, rp, rn = times(order)
    return best[1]


QSEM = {"v": "sv", "a": "sa", "p": "sp"}


def plan(ne):
    if "plan" not in CACHE:
        ops = build(ne)
        deps = depend(ops)
        succ = [set() for o in ops]
        for i, d in enumerate(deps):
            for k in d:
                succ[k].add(i)
        banks = [sorted(set(s[0] for s in o["r"] + o["w"] if s[0] in BANKS)) for o in ops]
        order, span = sweep(ops, deps, succ, banks), None
        for k, (steps, heat, mean, nm, pull, more) in enumerate(ROUNDS):
            order, span = improve(ops, deps, succ, banks, order, steps, heat, mean, nm, SEED + 2 * k, pull)
            order = swaps(ops, deps, succ, banks, order, more, SEED + 2 * k + 1)
        used = {b: {} for b in BANKS}
        for i in order:
            for b in banks[i]:
                deps[i] = deps[i] | {k for o, k in used[b].items() if o != ops[i]["q"]}
                used[b][ops[i]["q"]] = i
        CACHE["plan"] = (ops, deps, order, span)
    return CACHE["plan"]


def rank_program(g, core, T, topo):
    rank = T.rank_of(core)
    if rank is None:
        return
    me, dst = T.cores[rank], T.cores[(rank + STEP) % len(T.cores)]
    ops, deps, order, span = plan(len(topo.engines(me, dst)))
    eng = {"v": g.vector, "a": g.scalar, "p": g.tensor, "g": g, "s": g.sync}
    at, count, seen = {}, {}, {}
    for i in order:
        o = ops[i]
        q = o["q"]
        sem = o["sem"] or QSEM.get(q, "sg")
        count[sem] = count.get(sem, 0) + o["val"]
        at[i] = (sem, count[sem])
        if q == "net":
            continue
        need = {}
        for k in deps[i]:
            s, v = at[k]
            if s == "ls" or (q == "p" and ops[k]["q"] == "p"):
                continue
            need[s] = max(need.get(s, 0), v)
        for s in sorted(need):
            if seen.get((q, s), 0) < need[s]:
                eng[q].wait_ge(T.sem[s], need[s])
                seen[(q, s)] = need[s]
        if o["sem"] == "ls":
            o["fn"](g, T, me, dst, topo)
        else:
            o["fn"](g, T).then_inc(T.sem[sem], 1 if o["sem"] is None else 16)
    for s in sorted(count):
        g.sync.wait_ge(T.sem[s], count[s])
